import numpy as np, ml_dtypes
CORES = [66,74,82,90,194,202,210,218]
N = 8
import mx_ref
BF = ml_dtypes.bfloat16
def gcols(t, e):
    v = np.concatenate([t.reshape(8, 16, -1, 4), np.zeros((8, 16, 1, 4), BF)], axis=2)
    return np.ascontiguousarray(np.stack([v[g][:, e[g]] for g in range(8)])).reshape(128, -1)
def tile(rs):
    return np.stack(rs, axis=2).reshape(128, -1).astype(BF)
def pick(q, e):
    c = np.concatenate([q[0].reshape(128, -1, 4), np.zeros((128, 1, 4), np.uint8)], axis=1); s = np.concatenate([q[1], np.ones((16, 1), np.uint8)], axis=1)
    return (np.ascontiguousarray(c[:, e].reshape(128, -1)), np.ascontiguousarray(s[:, e]))
def join(*qs):
    return (np.concatenate([q[0] for q in qs], axis=1), np.concatenate([q[1] for q in qs], axis=1))
def put(q, e, v):
    c, s = q[0].reshape(128, -1, 4).copy(), q[1].copy(); c[:, e] = v[0].reshape(128, -1, 4); s[:, e] = v[1]
    return (c.reshape(128, -1), s)
def pk(c, s):
    return (np.ascontiguousarray(c), mx_ref.live(s))
def emit(q):
    return q[0], q[1]
def packed(v, rng):
    q = [mx_ref.quantize(np.ascontiguousarray(v[r])) for r in range(N)]
    return np.stack([a for a, b in q]), np.stack([mx_ref.plane(b, rng) for a, b in q])
def values_of_codes():
    e, c = np.zeros((128, 128, 4), np.float32), np.zeros((128, 2, 4), np.uint8)
    e[np.arange(128), np.arange(128), 0] = 1
    c[:127, :, 0] = np.arange(256).reshape(2, 128).T[:127]
    return mx_ref.matmul(mx_ref.quantize(e.reshape(128, 512).astype(BF)), (c.reshape(128, 8), np.full((16, 2), 127, np.uint8))).T.reshape(-1).astype(np.float64)
CODE_VALUE, SCALE_VALUE = values_of_codes(), 2.0 ** (np.arange(256) - 127.0)
def decode(q):
    return (CODE_VALUE[q[0]].reshape(16, 8, -1, 4) * SCALE_VALUE[q[1]][:, None, :, None] + 0.0).reshape(128, -1).astype(np.float32)
def f(rng, *shape):
    return mx_ref.flush((rng.standard_normal(shape, dtype=np.float32) * np.exp2(rng.integers(-2, 3, shape[:-1] + (1,)))).astype(BF))
def wide(rng, *shape, cols=0):
    v = rng.standard_normal(shape, dtype=np.float32) * np.exp2(rng.integers(-12, 13, shape)).astype(np.float32)
    if cols: v *= np.repeat(np.exp2(rng.integers(-cols, cols + 1, shape[:-2] + (1, shape[-1] // 4))) * (rng.random(shape[:-2] + (1, shape[-1] // 4)) > 0.0625), 4, axis=-1).astype(np.float32)
    return mx_ref.flush(v.astype(BF))
C, STEP = 224, [4, 1, 2]
def numbers_of(rng):
    return {"x": np.array(f(rng, N, 128, 4 * C)), "u": np.array(f(rng, N, 128, 512)), "v": np.array(f(rng, N, 128, 512))}
def layers(rng):
    return np.array(f(rng, N, 128, 2048)).reshape(N, 8, 16, 4, 8, 16, 4)
def weights(rng, w):
    c, p = packed(np.ascontiguousarray(w).reshape(N, 128, 2048), rng)
    return {"wc": c, "ws": p}
def both(x, u):
    return {"x": x.astype(np.float32).reshape(N, 128, 4 * C).astype(BF), "u": u.astype(np.float32).reshape(N, 128, 512).astype(BF)}
def setup_inputs(rng):
    return {**numbers_of(rng), **weights(rng, layers(rng))}
def setup_inputs_ties(rng):
    d = numbers_of(rng)
    e = rng.permutation(N)
    x = rng.integers(-1, 2, (N, 128, C, 4)) * (rng.random((N, 128, C, 4)) < 0.09375)
    u = rng.integers(-1, 2, (N, 128, 128, 4)) * (rng.random((N, 128, 128, 4)) < 0.09375)
    x[e[0]] = x[e[0]][:, :1].copy()
    x[e[1]] = 0
    u[e[2]] = u[e[2]][:, :1].copy()
    w = np.zeros((N, 128, 512, 4), np.float32)
    for r in range(N):
        a, c = rng.permutation(512)[:128], rng.permutation(512)[:128]
        w[r, a // 4, c, a % 4] = 64
    return {**both(x, u), "v": d["v"], **weights(rng, w.astype(BF))}
def setup_inputs_near(rng):
    d = numbers_of(rng)
    h, o = rng.permutation(8), rng.permutation(N) % 4
    x = d["x"].astype(np.float32).reshape(N, 8, 16, C, 4)
    u = d["u"].astype(np.float32).reshape(N, 8, 16, 128, 4)
    x[:, :, 8:] = 0
    u[:, :, :8] = 0
    x[:, h[:2], :8] = 0
    p = np.exp2(np.arange(4) - 23.0)
    for r in range(N):
        k = 1.0 if o[r] < 2 else 2.0 ** -29
        if o[r] == 3:
            x[r, h[0], 0, :, 0] = rng.choice([1.0, 1.125], C) * 2.0 ** -30
            u[r, h[0], 0, :, 0] = rng.choice([1.125, 1.25], 128) * 2.0 ** -30
        else:
            x[r, h[0], 0, :, 0] = -1.0 if o[r] == 1 else 1.0
            u[r, h[0], 0, :, 0] = k
            x[r, h[1], 0] = ((rng.integers(0, 16, (C, 1)) >> np.arange(4)) & 1) * p
            u[r, h[1], 0] = k
            x[r, h[1], 1] = p
            u[r, h[1], 1] = ((rng.integers(0, 16, (128, 1)) >> np.arange(4)) & 1) * k
            x[r, h[1], 2, :, 0] = 2.0 ** -10
            u[r, h[1], 2, :, 0] = k
        x[r, h[0], 0, rng.integers(C), 0] = 2.0 ** 29
    w = layers(rng)
    w[:, h[:2], :8] = 0
    for g in h[:2]: w[:, :, :, :, g, :8] = 0
    return {**both(x, u), "v": d["v"], **weights(rng, w)}
def setup_inputs_huge(rng):
    d = numbers_of(rng)
    e = rng.permutation(N)
    x = 0.7 + 0.3 * rng.random((N, 8, 16, C, 4))
    u = 0.7 + 0.3 * rng.random((N, 8, 16, 128, 4))
    for i in range(N):
        r = e[i]
        if i == 0:
            x[r] = -0.94 - 0.06 * rng.random((8, 16, C, 4))
            x[r][:, :, rng.permutation(C)[:4]] *= -1.0
            u[r] = 0.94 + 0.06 * rng.random((8, 16, 128, 4))
        elif i % 2 == 1: u[r] *= -1.0
        else:
            x[r] *= rng.choice([-1.0, 1.0], (1, 1, C, 1))
            u[r] *= rng.choice([-1.0, 1.0], (1, 1, 128, 1))
    w = np.zeros((N, 128, 4, 128, 4), np.float32)
    i = np.arange(128)
    for b in range(4): w[:, i, b, i, b] = -1
    return {**both(x * 2.0 ** 30, u * 2.0 ** 30), "v": d["v"], **weights(rng, w.astype(BF))}
def setup_inputs_odd(rng):
    d = numbers_of(rng)
    x = d["x"].astype(np.float32).reshape(N, 8, 16, C, 4)
    u = d["u"].astype(np.float32).reshape(N, 8, 16, 128, 4)
    for a, n in ((x, C), (u, 128)):
        a[:, :, :8] = (2 * rng.integers(0, 8, (N, 8, 8, n, 4)) + 1) * rng.choice([-1.0, 1.0], (N, 8, 8, n, 4)) * 2.0 ** -16
        a[:, :, 0, :, 0] = rng.choice([1.625, 1.75, 1.875, 1.96875], (N, 8, n))
        a[:, :, 8] = 0
        a[:, :, 8, :, 0] = 1
    w = layers(rng)
    w[:, :, :, :, :, :9] = 0
    for g in range(8): w[:, g, 8, 0, g, 0, 0] = 3
    return {**both(x, u), "v": d["v"], **weights(rng, w)}
def setup_inputs_spread(rng):
    d = setup_inputs(rng)
    d["x"] = wide(rng, N, 128, 4 * C, cols=6)
    return d
def check_inputs(d):
    b = []
    for k in ("x", "u", "v"):
        a = np.abs(d[k].astype(np.float32))
        if not (np.isfinite(a).all() and ((a == 0) | (a >= 2.0 ** -30) & (a <= 2.0 ** 30)).all()): b.append("a value of " + k)
    none, least, most = [emit(mx_ref.quantize(np.full((128, 16), k, np.float32).astype(BF)))[1][0, 0] for k in (0.0, 2.0 ** -30, 2.0 ** 30)]
    for r in range(N):
        if ((d["wc"][r] == 0x7F) | (d["wc"][r] == 0xFF)).any(): b.append("wc: a code that is no number")
        s = mx_ref.live(d["ws"][r])
        if ((s != none) & ((s < least) | (s > most))).any(): b.append("ws: a scale out of range")
    return b
def reference(x, u, v, wc, ws):
    lay = [pk(wc[r], ws[r]) for r in range(N)]
    now = [mx_ref.quantize(x[r]) for r in range(N)]
    stat = [mx_ref.quantize(u[r]) for r in range(N)]
    down, along = np.zeros((N, 8, C), np.int64), np.zeros((N, 8, 128), np.int64)
    for h in STEP:
        sent = []
        for r in range(N):
            own = decode(now[r])
            s = mx_ref.matmul(stat[r], now[r]) + np.float32(0.0)
            down[r] = np.argmax(s.reshape(8, 16, C), axis=1) + 16 * np.arange(8)[:, None]
            along[r] = np.argsort(-s, axis=1, kind="stable")[:, :8].T
            a = gcols(decode(stat[r]).astype(BF), down[r]).astype(np.float32)
            z = mx_ref.quantize(((own + a) * np.float32(0.5)).astype(BF))
            now[r] = mx_ref.quantize(tile([mx_ref.matmul(pick(lay[r], np.arange(128 * b, 128 * b + 128)), z) * np.float32(0.03125) + own[:, b::4] for b in range(4)]))
            sent.append(mx_ref.quantize(gcols(decode(now[r]).astype(BF), along[r])))
        stat = [sent[(r - h) % N] for r in range(N)]
    y, op = np.zeros((N, 128, C), np.float32), np.zeros((N, 8, C + 128), np.float32)
    oc, osc = np.zeros((N, 128, 4 * C), np.uint8), np.zeros((N, 16, C), np.uint8)
    uc, usc = np.zeros((N, 128, 512), np.uint8), np.zeros((N, 16, 128), np.uint8)
    for r in range(N):
        y[r] = mx_ref.matmul(mx_ref.quantize(v[r]), now[r])
        op[r, :, :C] = down[r]
        op[r, :, C:] = along[r]
        oc[r], osc[r] = emit(now[r])
        uc[r], usc[r] = emit(stat[r])
    return {"y": y, "op": op, "oc": oc, "osc": osc, "uc": uc, "usc": usc}

@@ -1,0 +1,398 @@
+from concourse.mybir import dt, AluOpType, ActivationFunctionType
+
+STEP = [4, 1, 2]
+C = 224
+BIG = 1.0e29
+PS = 232
+F8 = "float8_e4m3fn_x4"
+ALU = AluOpType
+ACT = ActivationFunctionType
+SEQ = "s0 s1 p0 s2 s3 n1 n2 n3 f1 s4 f2 n4 s5 f3 s6 D f4 n6 n5 X s7 E q f5 n7 e O c1 p1 Z0 c3 c4 c5 w3 c2 f6 f7 c6 c7 p5 w6 p4 w2 w7 Z2 Z1 P2 P6 Z3 N Q R0 r1 R3 r2"
+NS = [k for k in range(8) if "n%d" % k in SEQ.split()]
+
+SCRATCH = {
+    "xin": ("sbuf", [128, 4 * C], "bfloat16"), "uin": ("sbuf", [128, 512], "bfloat16"), "vin": ("sbuf", [128, 512], "bfloat16"),
+    "wq": ("sbuf", [128, 512], F8), "wsc": ("sbuf", [128, 512], "uint8"),
+    "qu": ("sbuf", [128, 128], F8), "squ": ("sbuf", [128, 128], "uint8"),
+    "qvv": ("sbuf", [128, 128], F8), "sqvv": ("sbuf", [128, 128], "uint8"),
+    "c32": ("sbuf", [128, 516], "bfloat16"), "dd": ("sbuf", [128, 516], "bfloat16"),
+    "dde": ("sbuf", [128, 516], "bfloat16"), "ddo": ("sbuf", [128, 516], "bfloat16"),
+    "cf": ("sbuf", [128, 512], F8), "scf": ("sbuf", [128, 512], "uint8"),
+    "ce": ("sbuf", [128, 512], F8), "sce": ("sbuf", [128, 512], "uint8"),
+    "cd": ("sbuf", [128, 512], F8), "scd": ("sbuf", [128, 512], "uint8"),
+    "zt": ("sbuf", [128, 4 * C], "bfloat16"), "xt": ("sbuf", [128, 4 * C], "bfloat16"), "vt": ("sbuf", [128, 512], "bfloat16"),
+    "bigc": ("sbuf", [128, C], "float32"), "rst": ("sbuf", [128, 128], "float32"),
+    "mones": ("sbuf", [128, 256], "bfloat16"), "ones": ("sbuf", [128, C], "bfloat16"), "zeros": ("sbuf", [128, C], "bfloat16"),
+    "mone7": ("sbuf", [128, 8], "float32"),
+    "pa": ("sbuf", [128, 288], "float32"), "nr": ("sbuf", [128, 256], "bfloat16"), "ag": ("sbuf", [128, 256], "bfloat16"),
+    "kt": ("sbuf", [128, 256], "bfloat16"), "ot": ("sbuf", [128, 32], "bfloat16"), "ott": ("sbuf", [128, 32], "bfloat16"),
+    "lst": ("sbuf", [128, 32], "uint16"),
+    "pb": ("sbuf", [128, 8 * PS], "float32"), "eq": ("sbuf", [128, 8], "float32"), "ne": ("sbuf", [128, 8], "float32"),
+    "sg": ("sbuf", [128, 8 * C], "bfloat16"), "fb": ("sbuf", [128, 8 * C], "bfloat16"),
+    "cb": ("sbuf", [128, 8 * C], "bfloat16"), "junk": ("sbuf", [128, 8 * C], "bfloat16"),
+    "nb": ("sbuf", [128, 32], "float32"), "nt": ("sbuf", [128, 32], "float32"),
+    "ot2": ("sbuf", [128, 32], "float32"), "ott2": ("sbuf", [128, 32], "float32"), "lst2": ("sbuf", [128, 16], "uint16"),
+    "ip": ("sbuf", [128, 2], "int32"), "t1": ("sbuf", [128, 2], "int32"), "t2": ("sbuf", [128, 2], "int32"), "t3": ("sbuf", [128, 2], "int32"),
+    "col": ("sbuf", [128, 8], "float32"),
+    "cz": ("sbuf", [128, 96], "float32"), "czt": ("sbuf", [128, 96], "float32"), "off": ("sbuf", [128, 8], "uint16"),
+    "kf": ("sbuf", [128, 64], "float32"), "kft": ("sbuf", [128, 64], "float32"), "kfo": ("sbuf", [128, 64], "float32"),
+    "yb": ("sbuf", [128, C], "float32"),
+    "ps": ("psum", [128, 4096], "float32"),
+}
+for _r in range(4):
+    SCRATCH["qx%d" % _r] = ("sbuf", [128, C], F8)
+    SCRATCH["sx%d" % _r] = ("sbuf", [128, C], "uint8")
+for _r in range(3):
+    for _q, _s in (("ue", "se"), ("uo", "so"), ("qz", "sz")):
+        SCRATCH["%s%d" % (_q, _r)] = ("sbuf", [128, C], F8)
+        SCRATCH["%s%d" % (_s, _r)] = ("sbuf", [128, C], "uint8")
+    SCRATCH["pk%d" % _r] = ("sbuf", [128, 256], F8)
+    SCRATCH["sk%d" % _r] = ("sbuf", [128, 256], "uint8")
+    SCRATCH["qv%d" % _r] = ("sbuf", [128, 128], F8)
+    SCRATCH["sv%d" % _r] = ("sbuf", [128, 128], "uint8")
+    SCRATCH["land%d" % (_r + 1)] = ("sbuf", [128, 128], F8)
+    SCRATCH["lsc%d" % (_r + 1)] = ("sbuf", [128, 128], "uint8")
+SEMAPHORES = ["vs", "ts", "sa", "gc0", "dk", "dn", "ldx", "ldu", "ldv", "ldw", "ldp", "loc", "arr1", "arr2", "arr3", "st"]
+
+
+def rank_program(g, core, T, topo):
+    rank = T.rank_of(core)
+    if rank is None:
+        return
+    queue = {"v": g.vector, "t": g.tensor, "a": g.scalar, "s": g.sync, "g": g}
+    csem = {"v": "vs", "t": "ts", "a": "sa", "g": "gc0"}
+    known = {q: {} for q in queue}
+    count = {s: 0 for s in SEMAPHORES}
+    clocks = {s: {} for s in SEMAPHORES}
+    regs = {}
+
+    def merge(a, b):
+        for s, n in b.items():
+            if a.get(s, 0) < n:
+                a[s] = n
+
+    def deps(q, reads, writes):
+        out = []
+        for w, items in ((False, reads), (True, writes)):
+            for name, lo, hi in items:
+                bank = name.startswith("bank")
+                for (l, h, ww, qq, tok) in regs.get(name, []):
+                    if l >= hi or h <= lo:
+                        continue
+                    if bank:
+                        if qq == q and (q == "t" or not (w or ww)):
+                            continue
+                    elif not (w or ww):
+                        continue
+                    out.append(tok)
+        return out
+
+    def need(q, toks):
+        best = {}
+        for tk in toks:
+            s, n, c = tk
+            if known[q].get(s, 0) < n and (s not in best or best[s][1] < n):
+                best[s] = tk
+        for s in list(best):
+            if any(o != s and best[o][2].get(s, 0) >= best[s][1] for o in best):
+                del best[s]
+        for s, tk in best.items():
+            queue[q].wait_ge(T.sem[s], tk[1])
+            merge(known[q], tk[2])
+
+    def note(q, tok, reads, writes):
+        for name, lo, hi in writes:
+            old = regs.get(name, [])
+            regs[name] = [e for e in old if not (lo <= e[0] and e[1] <= hi)] + [(lo, hi, True, q, tok)]
+        for name, lo, hi in reads:
+            regs.setdefault(name, []).append((lo, hi, False, q, tok))
+
+    def token(q, s, n):
+        count[s] += n
+        c = dict(known[q])
+        merge(c, clocks[s])
+        c[s] = count[s]
+        clocks[s] = c
+        return (s, count[s], c)
+
+    def run(q, reads, writes, fn):
+        need(q, deps(q, reads, writes))
+        fn().then_inc(T.sem[csem[q]], 1)
+        tok = token(q, csem[q], 1)
+        note(q, tok, reads, writes)
+        return tok
+
+    def dmas(s, jobs):
+        ds = [deps(q, r, w) for q, r, w, o, i in jobs]
+        toks = []
+        for (q, r, w, o, i), d in zip(jobs, ds):
+            need(q, d)
+            queue[q].dma_start(o, i).then_inc(T.sem[s], 16)
+            toks.append(token(q, s, 16))
+        for q, r, w, o, i in jobs:
+            note(q, toks[-1], r, w)
+        return toks[-1]
+
+    def R(name, lo=0, hi=None):
+        return (name, lo, 1 << 20 if hi is None else hi)
+
+    def bank(j, n):
+        return T.ps[:, 512 * j:512 * j + n]
+
+    def mm(j, n, a, sa, alo, b, sb, blo, start, stop):
+        run("t", [R(a, alo, alo + 128), R(sa, alo, alo + 128), R(b, blo, blo + n), R(sb, blo, blo + n)], [R("bank%d" % j)],
+            lambda: g.tensor.matmul_mx(bank(j, n), T[a][:, alo:alo + 128], T[sa][:, alo:alo + 128], T[b][:, blo:blo + n], T[sb][:, blo:blo + n], start, stop))
+
+    def vec(reads, writes, fn):
+        return run("v", reads, writes, fn)
+
+    def act(reads, writes, fn):
+        return run("a", reads, writes, fn)
+
+    def fill(name, view, c, lo=0, hi=None):
+        vec([], [R(name, lo, hi)], lambda: g.vector.memset(view, c))
+
+    def iota(name, view, pat, base, lo=0, hi=None):
+        run("g", [], [R(name, lo, hi)], lambda: g.iota(view, pat, base, 0, allow_small_or_imprecise_dtypes=True))
+
+    def quant(q, s, lo, n, tile, tlo, names):
+        vec(names, [R(q, lo, lo + n), R(s, lo, lo + n)], lambda: g.vector.quantize_mx(T[q][:, lo:lo + n], T[s][:, lo:lo + n], T[tile][:, tlo:tlo + 4 * n]))
+
+    def column(j, nm, sc, b):
+        vec([R(nm)], [R("col", j, j + 1)], lambda: g.vector.tensor_scalar(T.col[:, j:j + 1], T[nm][:, 0:1], sc, b, ALU.mult, ALU.add))
+
+    def bits(nm, m):
+        vec([R("ip")], [R(nm)], lambda: g.vector.tensor_scalar(T[nm][:, 0:1], T.ip[:, 0:1], m, None, ALU.bitwise_and))
+
+    xtok = dmas("ldx", [("s", [], [R("xin")], T.xin[:], T.x[:])])
+    dmas("ldu", [("a", [], [R("uin")], T.uin[:], T.u[:])])
+
+    fill("c32", T.c32[:], 32.0)
+    run("g", [], [R("ip")], lambda: g.iota(T.ip[:, 0:1], [[0, 1]], 0, 1))
+    run("g", [R("c32")], [R("dd")], lambda: g.affine_select(T.dd[:], T.c32[:], [[1, 516]], ALU.is_equal, 0.0, -3, -4))
+    for blk, base, pat in ((0, 0, [[20, 2], [4, 4], [1, 2]]), (1, 2, [[20, 2], [4, 4], [1, 2]]), (2, 0, [[2, 2], [4, 4], [1, 2]])):
+        for h in range(2):
+            lo = 32 * blk + 16 * h
+            iota("cz", T.cz[:, lo:lo + 16], pat, base, lo, lo + 16)
+    iota("mones", T.mones[:], [[0, 256]], -1)
+    iota("mone7", T.mone7[:], [[0, 8]], -1)
+    iota("ones", T.ones[:], [[0, C]], 1)
+    iota("zeros", T.zeros[:], [[0, C]], 0)
+    iota("nb", T.nb[:], [[0, 32]], 0)
+    iota("ot2", T.ot2[:], [[0, 32]], 0)
+    iota("kf", T.kf[:], [[0, 64]], 0)
+    fill("rst", T.rst[:], BIG)
+    bits("t2", 16)
+    bits("t1", 96)
+    bits("t3", 31)
+    column(3, "t2", -0.0625, 1.0)
+    column(2, "t2", 0.0625, 0.0)
+    column(0, "t1", 1.0, 16.0)
+    column(1, "t1", 1.0, 32.0)
+    column(4, "t3", 16.0, 16.0)
+    act([R("dd"), R("col", 3, 4)], [R("dde")], lambda: g.scalar.activation(T.dde[:], T.dd[:], ACT.Copy, scale=T.col[:, 3:4]))
+    act([R("dd"), R("col", 2, 3)], [R("ddo")], lambda: g.scalar.activation(T.ddo[:], T.dd[:], ACT.Copy, scale=T.col[:, 2:3]))
+    fill("rst", T.rst[:, 0:128:16], -BIG)
+    fill("pa", T.pa[:, 0:288:144], -BIG, 0, 1)
+    fill("pb", T.pb[:, 0:8 * PS:PS], -BIG)
+    fill("bigc", T.bigc[:], BIG)
+    for b in range(4):
+        quant("cf", "scf", 128 * b, 128, "dd", 3 - b, [R("dd")])
+    for b in range(4):
+        quant("ce", "sce", 128 * b, 128, "dde", 3 - b, [R("dde")])
+    quant("qu", "squ", 0, 128, "uin", 0, [R("uin")])
+    for b in range(4):
+        quant("cd", "scd", 128 * b, 128, "ddo", 3 - b, [R("ddo")])
+    quant("qx0", "sx0", 0, C, "xin", 0, [R("xin")])
+    need("s", [xtok])
+    dmas("ldw", [("s", [], [R("wq")], T.wq[:].bitcast(dt.uint8), T.wc[:])])
+    dmas("ldp", [("s", [], [R("wsc")], T.wsc[:], T.ws[:])])
+    dmas("ldv", [("s", [], [R("vin")], T.vin[:], T.v[:])])
+
+    SB, SB2, YB = 6, 7, 7
+    RB = [4, 5, 0, 1]
+    VB = [2, 3, 4, 5]
+    ncol = [16 * (k % 2) + k // 2 for k in range(8)]
+    for r in range(3):
+        last = r == 2
+        X, SX, X1, SX1 = "qx%d" % r, "sx%d" % r, "qx%d" % (r + 1), "sx%d" % (r + 1)
+        U, SU = ("qu", "squ") if r == 0 else ("land%d" % r, "lsc%d" % r)
+        ue, se, uo, so, qz, sz, pk, sk, qv, sv = [n + str(r) for n in ("ue", "se", "uo", "so", "qz", "sz", "pk", "sk", "qv", "sv")]
+
+        def tee(b, j):
+            mm(j, C, "cf", "scf", 128 * b, X, SX, 0, True, False)
+
+        if r:
+            for b in range(4):
+                tee(b, b)
+        for h in range(2):
+            mm(4 + h, 128, X, SX, 96 * h, U, SU, 0, True, True)
+        mm(SB, C, U, SU, 0, X, SX, 0, True, True)
+        mm(SB2, C, U, SU, 0, X, SX, 0, True, True)
+        if not r:
+            for b in range(4):
+                tee(b, b)
+        for h in range(2):
+            p0 = 144 * h
+            vec([R("bank%d" % (4 + h)), R("rst")], [R("pa", p0 + 1, p0 + 129)],
+                lambda: g.vector.tensor_tensor_scan(T.pa[:, p0 + 1:p0 + 129], T.rst[:], bank(4 + h, 128), -BIG, ALU.min, ALU.max))
+        for h in range(2):
+            p0 = 144 * h
+            vec([R("bank%d" % (4 + h)), R("pa", p0, p0 + 128)], [R("nr", 128 * h, 128 * h + 128)],
+                lambda: g.vector.tensor_tensor(T.nr[:, 128 * h:128 * h + 128], bank(4 + h, 128), T.pa[:, p0:p0 + 128], ALU.is_le))
+        for b in range(2):
+            tee(b, RB[b])
+        vec([R("nr"), R("mones")], [R("ag")], lambda: g.vector.tensor_tensor_scan(T.ag[:], T.nr[:], T.mones[:], 0.0, ALU.mult, ALU.add))
+        if not r:
+            vec([R("cz")], [R("czt")], lambda: g.vector.transpose(T.czt[:], T.cz[:]))
+        vec([R("ag")], [R("kt")], lambda: g.vector.transpose(T.kt[:], T.ag[:]))
+        dmas("dk", [("s" if h == 0 else "a", [R("kt")], [R("ot", 0, 16)], T.ot[32 * a + 16 * h:32 * a + 16 * h + 16, 0:16],
+                     T.kt[15:128:16, 128 * h + 32 * a:128 * h + 32 * a + 32]) for a in range(4) for h in range(2)])
+        if not r:
+            vec([R("czt")], [R("off")], lambda: g.vector.tensor_scalar(T.off[:, 0:6:2], T.czt[:, 0:96:32], 31.0, None, ALU.min))
+
+        def scan(k):
+            o = PS * k
+            d1 = [R("bigc")] if k == 0 else [R("pb", o - PS, o - PS + 224)]
+            vec([R("bank%d" % SB)] + d1, [R("pb", o + 1, o + 225)],
+                lambda: g.vector.tensor_tensor_scan(T.pb[:, o + 1:o + 225], bank(SB, C), T.bigc[:] if k == 0 else T.pb[:, o - PS:o - PS + 224], -BIG, ALU.max, ALU.min))
+
+        def sign(k):
+            o = PS * k + 224
+            act([R("bank%d" % SB2), R("pb", o, o + 1)], [R("sg", C * k, C * k + C)],
+                lambda: g.scalar.activation(T.sg[:, C * k:C * k + C], bank(SB2, C), ACT.Sign, bias=T.pb[:, o:o + 1], scale=-1.0))
+
+        def flags(k):
+            o = PS * k + 224
+            if k in NS:
+                vec([R("sg", C * k, C * k + C)], [R("fb", C * k, C * k + C)],
+                    lambda: g.vector.tensor_scalar(T.fb[:, C * k:C * k + C], T.sg[:, C * k:C * k + C], 0.0, None, ALU.is_equal))
+            else:
+                vec([R("bank%d" % SB), R("pb", o, o + 1)], [R("fb", C * k, C * k + C)],
+                    lambda: g.vector.tensor_scalar(T.fb[:, C * k:C * k + C], bank(SB, C), T.pb[:, o:o + 1], None, ALU.is_equal))
+
+        def same(k):
+            vec([R("pb")], [R("eq")], lambda: g.vector.tensor_tensor(T.eq[:, 1:8], T.pb[:, PS + 224:8 * PS:PS], T.pb[:, 224:7 * PS:PS], ALU.is_equal))
+
+        def less(k):
+            vec([R("eq"), R("mone7")], [R("ne")], lambda: g.vector.tensor_tensor_scan(T.ne[:, 1:8], T.mone7[:, 0:7], T.eq[:, 1:8], 0.0, ALU.add, ALU.mult))
+
+        def counts(k):
+            vec([R("fb", C * k, C * k + C), R("ne"), R("ones")], [R("cb", C * k, C * k + C)],
+                lambda: g.vector.tensor_tensor_scan(T.cb[:, C * k:C * k + C], T.fb[:, C * k:C * k + C], T.ones[:], T.ne[:, k:k + 1], ALU.add, ALU.min))
+
+        def places(k):
+            if k == 0:
+                act([R("pb", 0, 225)], [R("nb", ncol[0], ncol[0] + 1), R("junk", 0, C)],
+                    lambda: g.scalar.activation(T.junk[:, 0:C], T.pb[:, 1:225], ACT.Sign, bias=T.pb[:, 224:225], scale=-1.0, accum_out=T.nb[:, ncol[0]:ncol[0] + 1]))
+            else:
+                act([R("cb", C * k, C * k + C)], [R("nb", ncol[k], ncol[k] + 1), R("junk", C * k, C * k + C)],
+                    lambda: g.scalar.activation(T.junk[:, C * k:C * k + C], T.cb[:, C * k:C * k + C], ACT.Sign, bias=1.0, scale=-1.0, accum_out=T.nb[:, ncol[k]:ncol[k] + 1]))
+
+        def rest(k):
+            vec([R("cb", C * k, C * k + C), R("zeros")], [R("junk", C * k, C * k + C)],
+                lambda: g.vector.tensor_tensor_scan(T.junk[:, C * k:C * k + C], T.cb[:, C * k:C * k + C], T.zeros[:], 0.0, ALU.add, ALU.max))
+
+        def pair(k):
+            vec([R("junk", C * k, C * k + 2 * C)], [R("nb", ncol[k], ncol[k] + 1), R("nb", ncol[k + 1], ncol[k + 1] + 1)],
+                lambda: g.vector.tensor_scalar(T.nb[:, ncol[k]:ncol[k + 1] + 1:16], T.junk[:, C * k + C - 1:C * k + 2 * C:C], -1.0, float(C), ALU.mult, ALU.add))
+
+        def halves(k):
+            vec([R("ot", 0, 16)], [R("ot", 16, 32)], lambda: g.vector.tensor_copy(T.ot[:, 16:32], T.ot[:, 0:16]))
+
+        def turn(k):
+            vec([R("ot")], [R("ott")], lambda: g.vector.transpose(T.ott[:], T.ot[:]))
+
+        def picks(e):
+            q, s = ((ue, se), (uo, so))[e]
+            vec([R("ott"), R("off"), R("col")], [R("lst", 16 * e, 16 * e + 16)],
+                lambda: g.vector.tensor_scalar(T.lst[:, 16 * e:16 * e + 16], T.ott[:, 0:32].indirect(T.off[:, 2 * e:2 * e + 1]), -16.0, T.col[:, e:e + 1], ALU.max, ALU.add))
+            vec([R(U), R("lst", 16 * e, 16 * e + 16)], [R(q)],
+                lambda: g.vector.tensor_copy(T[q][:].bitcast(dt.uint32), T[U][:].bitcast(dt.uint32).indirect(T.lst[:, 16 * e:16 * e + 14])))
+            act([R(SU), R("lst", 16 * e, 16 * e + 16)], [R(s)],
+                lambda: g.scalar.activation(T[s][:], T[SU][:].indirect(T.lst[:, 16 * e:16 * e + 14]), ACT.Copy))
+            for b in range(4):
+                mm(b, C, ("ce", "cd")[e], ("sce", "scd")[e], 128 * b, q, s, 0, False, e == 1)
+
+        def zed(b):
+            act([R("bank%d" % b)], [R("zt%d" % b)], lambda: g.scalar.activation(T.zt[:, b:4 * C:4], bank(b, C), ACT.Copy, scale=2.0 ** -6))
+
+        def zedv(b):
+            vec([R("bank%d" % b)], [R("zt%d" % b)], lambda: g.vector.tensor_scalar(T.zt[:, b:4 * C:4], bank(b, C), 2.0 ** -6, None, ALU.mult))
+
+        def send_lists(k):
+            vec([R("nb")], [R("nt")], lambda: g.vector.transpose(T.nt[:], T.nb[:]))
+            dmas("dn", [("sa"[h], [R("nt")], [R("ot2", 16 * h, 16 * h + 16)], T.ot2[32 * a:32 * a + 16, 16 * h:16 * h + 16], T.nt[a:128:16, 0:32])
+                        for a in range(4) for h in range(2)])
+
+        def state(k):
+            for b in (2, 3):
+                tee(b, RB[b])
+            quant(qz, sz, 0, C, "zt", 0, [R("zt%d" % b) for b in range(4)])
+            for b in range(4):
+                mm(RB[b], C, "wq", "wsc", 128 * b, qz, sz, 0, False, True)
+
+        def newx(b):
+            act([R("bank%d" % RB[b])], [R("xt%d" % b)], lambda: g.scalar.activation(T.xt[:, b:4 * C:4], bank(RB[b], C), ACT.Copy, scale=2.0 ** -5))
+
+        def newxv(b):
+            vec([R("bank%d" % RB[b])], [R("xt%d" % b)], lambda: g.vector.tensor_scalar(T.xt[:, b:4 * C:4], bank(RB[b], C), 2.0 ** -5, None, ALU.mult))
+
+        steps = {"s": scan, "n": sign, "f": flags, "q": same, "e": less, "c": counts, "p": places, "w": rest, "P": pair,
+                 "D": halves, "X": turn, "E": lambda k: picks(0), "O": lambda k: picks(1), "Z": zed, "z": zedv,
+                 "N": send_lists, "Q": state, "R": newx, "r": newxv}
+        for word in SEQ.split():
+            steps[word[0]](int(word[1:] or "0"))
+        quant(X1, SX1, 0, C, "xt", 0, [R("xt%d" % b) for b in range(4)])
+        vec([R("ot2")], [R("ott2")], lambda: g.vector.transpose(T.ott2[:], T.ot2[:]))
+        vec([R("ott2"), R("off")], [R("lst2")], lambda: g.vector.tensor_copy(T.lst2[:], T.ott2[:, 0:32].indirect(T.off[:, 4:5])))
+        for e in range(2):
+            lo = 128 * e
+            vec([R(X1), R("lst2")], [R(pk, lo, lo + 128)],
+                lambda: g.vector.tensor_copy(T[pk][:, lo:lo + 128].bitcast(dt.uint32), T[X1][:].bitcast(dt.uint32).indirect(T.lst2[:, 8 * e:8 * e + 8])))
+            act([R(SX1), R("lst2")], [R(sk, lo, lo + 128)],
+                lambda: g.scalar.activation(T[sk][:, lo:lo + 128], T[SX1][:].indirect(T.lst2[:, 8 * e:8 * e + 8]), ACT.Copy))
+            for b in range(4):
+                mm(VB[b], 128, ("ce", "cd")[e], ("sce", "scd")[e], 128 * b, pk, sk, lo, e == 0, e == 1)
+        for b in range(4):
+            if b % 2 == 0:
+                act([R("bank%d" % VB[b])], [R("vt%d" % b)], lambda: g.scalar.activation(T.vt[:, b:512:4], bank(VB[b], 128), ACT.Copy, scale=2.0 ** -5))
+            else:
+                vec([R("bank%d" % VB[b])], [R("vt%d" % b)], lambda: g.vector.tensor_scalar(T.vt[:, b:512:4], bank(VB[b], 128), 2.0 ** -5, None, ALU.mult))
+        quant(qv, sv, 0, 128, "vt", 0, [R("vt%d" % b) for b in range(4)])
+        dst = T.cores[(rank + STEP[r]) % 8]
+        src = T.cores[(rank - STEP[r]) % 8]
+        rid, pid = topo.addr(dst, core)
+        need("g", deps("g", [R(qv), R(sv)], []))
+        arr = "arr%d" % (r + 1)
+        ld, ls = T["land%d" % (r + 1)], T["lsc%d" % (r + 1)]
+        g.remote_dma(ld[:].bitcast(dt.uint8), T[qv][:].bitcast(dt.uint8), T.sem[arr], T.sem["loc"], pid, rid, topo.mask(core, dst))
+        g.remote_dma(ls[:], T[sv][:], T.sem[arr], T.sem["loc"], pid, rid, topo.mask(core, dst))
+        count["loc"] += 2 * len(topo.engines(core, dst))
+        count[arr] = 2 * len(topo.engines(src, core))
+        note("g", (arr, count[arr], {arr: count[arr]}), [], [R("land%d" % (r + 1)), R("lsc%d" % (r + 1))])
+        if r == 0:
+            quant("qvv", "sqvv", 0, 128, "vin", 0, [R("vin")])
+    for h in range(2):
+        vec([R("ag")], [R("kf", 32 * h, 32 * h + 8)], lambda: g.vector.tensor_copy(T.kf[:, 32 * h:32 * h + 8], T.ag[:, 128 * h + 15:128 * h + 128:16]))
+    vec([R("kf")], [R("kft")], lambda: g.vector.transpose(T.kft[:], T.kf[:]))
+    vec([R("kft"), R("col")], [R("kfo")], lambda: g.vector.tensor_scalar(T.kfo[:], T.kft[:], -16.0, T.col[:, 4:5], ALU.max, ALU.add))
+    mm(YB, C, "qvv", "sqvv", 0, "qx3", "sx3", 0, True, True)
+    act([R("bank%d" % YB)], [R("yb")], lambda: g.scalar.activation(T.yb[:], bank(YB, C), ACT.Copy))
+    jobs = [("s", [R("qx3")], [], T.oc[:], T.qx3[:].bitcast(dt.uint8))]
+    jobs += [("s", [R("sx3")], [], T.osc[4 * k:4 * k + 4, :], T.sx3[32 * k:32 * k + 4, :]) for k in range(4)]
+    for A in range(4):
+        for e in range(2):
+            jobs.append(("s", [R("nt")], [], T.op[e:8:2, 224 + 32 * A:256 + 32 * A], T.nt[32 * A + 16 * e:32 * A + 16 * e + 4, 0:32]))
+    jobs.append(("s", [R("yb")], [], T.y[:], T.yb[:]))
+    for A in range(4):
+        for h in range(2):
+            if h == 0 or A:
+                jobs.append(("s", [R("kfo")], [], T.op[0:8, 96 * h + 32 * A:96 * h + 32 * A + 32], T.kfo[32 * A:32 * A + 8, 32 * h:32 * h + 32]))
+    dmas("st", jobs)
+    jobs = [("s", [R("land3")], [], T.uc[:], T.land3[:].bitcast(dt.uint8))]
+    jobs += [("as"[k % 2], [R("lsc3")], [], T.usc[4 * k:4 * k + 4, :], T.lsc3[32 * k:32 * k + 4, :]) for k in range(4)]
+    dmas("st", jobs)
+    g.wait_ge(T.sem["loc"], count["loc"])
+    for s in ("vs", "ts", "sa", "gc0", "dk", "dn", "ldx", "ldu", "ldv", "ldw", "ldp", "st"):
+        g.sync.wait_ge(T.sem[s], count[s])

@@ -3,39 +3,40 @@ from concourse.mybir import dt, AluOpType, ActivationFunctionType
 STEP = [4, 1, 2]
 C = 224
 BIG = 1.0e29
+KEY = 64.0
+ROUND = 12582912.0
 PS = 232
 F8 = "float8_e4m3fn_x4"
 ALU = AluOpType
 ACT = ActivationFunctionType
-SEQ = "s0 s1 p0 s2 s3 n1 n2 n3 f1 s4 f2 n4 s5 f3 s6 D f4 n6 n5 X s7 E q f5 n7 e O c1 p1 Z0 c3 c4 c5 w3 c2 f6 f7 c6 c7 p5 w6 p4 w2 w7 Z2 Z1 P2 P6 Z3 N Q R0 r1 R3 r2"
-NS = [k for k in range(8) if "n%d" % k in SEQ.split()]
+SEQ = "B0 c s0 U1 a U0 B1 s1 b s2 g n1 s3 t D s4 X s5 L n3 s6 e0 E0 M2 M3 n5 s7 n7 E1 M0 M1 e1 j K1 Z1 K0 u0 u1 u2 K2 u3 Z0 K3 U2 Z2 Z3 u4 u5 U3 u6 Q W3 u7 f W1 W2 W0 h r3 I0 i2 I1 i5 i3 R1 i4 N d x R2 R0 Y l P0 p0 G0 G2 G1 p1 P1 H0 H1 v1 C0 H2 C2 G3 H3 v3 V"
+SEQ0 = "k0 k3 k1 k4 k8 k2 k44 k9 k5 k25 k24 k10 k6 k7 k21 k11 k33 k12 k37 k35 k34 k17 k26 k29 k23 k13 k42 k16 k43 B0 k38 k39 k36 k14 k15 c B1 k20 s0 k18 a k28 k22 s1 T0 k45 k30 b k27 k31 k19 s2 k32 k46 g s3 k47 t T1 k48 n1 k49 D s4 X n3 s5 n5 L e0 k40 s6 T3 T2 E0 M3 M1 s7 E1 k41 e1 n7 M2 K2 j K3 Z3 K1 Z1 u0 u1 u2 U3 u3 u4 k50 u5 U2 k51 M0 K0 Z2 k52 Z0 u6 u7 Q f h I1 U0 i0 k53 i2 I5 U1 W1 R1 i4 i3 W2 N d W3 r3 R2 x l W0 R0 Y p0 P0 G3 P1 G0 p1 G2 H2 C2 H0 v0 G1 H1 H3 C1 v3 V"
 
 SCRATCH = {
     "xin": ("sbuf", [128, 4 * C], "bfloat16"), "uin": ("sbuf", [128, 512], "bfloat16"), "vin": ("sbuf", [128, 512], "bfloat16"),
     "wq": ("sbuf", [128, 512], F8), "wsc": ("sbuf", [128, 512], "uint8"),
     "qu": ("sbuf", [128, 128], F8), "squ": ("sbuf", [128, 128], "uint8"),
     "qvv": ("sbuf", [128, 128], F8), "sqvv": ("sbuf", [128, 128], "uint8"),
-    "c32": ("sbuf", [128, 516], "bfloat16"), "dd": ("sbuf", [128, 516], "bfloat16"),
+    "c32": ("sbuf", [128, 256], "bfloat16"), "dd": ("sbuf", [128, 516], "bfloat16"),
     "dde": ("sbuf", [128, 516], "bfloat16"), "ddo": ("sbuf", [128, 516], "bfloat16"),
     "cf": ("sbuf", [128, 512], F8), "scf": ("sbuf", [128, 512], "uint8"),
     "ce": ("sbuf", [128, 512], F8), "sce": ("sbuf", [128, 512], "uint8"),
     "cd": ("sbuf", [128, 512], F8), "scd": ("sbuf", [128, 512], "uint8"),
     "zt": ("sbuf", [128, 4 * C], "bfloat16"), "xt": ("sbuf", [128, 4 * C], "bfloat16"), "vt": ("sbuf", [128, 512], "bfloat16"),
-    "bigc": ("sbuf", [128, C], "float32"), "rst": ("sbuf", [128, 128], "float32"),
-    "mones": ("sbuf", [128, 256], "bfloat16"), "ones": ("sbuf", [128, C], "bfloat16"), "zeros": ("sbuf", [128, C], "bfloat16"),
-    "mone7": ("sbuf", [128, 8], "float32"),
-    "pa": ("sbuf", [128, 288], "float32"), "nr": ("sbuf", [128, 256], "bfloat16"), "ag": ("sbuf", [128, 256], "bfloat16"),
-    "kt": ("sbuf", [128, 256], "bfloat16"), "ot": ("sbuf", [128, 32], "bfloat16"), "ott": ("sbuf", [128, 32], "bfloat16"),
+    "bigc": ("sbuf", [128, C], "float32"), "rst": ("sbuf", [128, C], "float32"), "down": ("sbuf", [128, C], "bfloat16"),
+    "st": ("sbuf", [128, C], "float32"), "pa": ("sbuf", [128, PS], "float32"), "nr": ("sbuf", [128, C], "bfloat16"), "ag": ("sbuf", [128, 512], "bfloat16"),
+    "kt": ("sbuf", [128, 32], "bfloat16"), "kd": ("sbuf", [128, 64], "bfloat16"), "ktt": ("sbuf", [128, 64], "bfloat16"),
     "lst": ("sbuf", [128, 32], "uint16"),
-    "pb": ("sbuf", [128, 8 * PS], "float32"), "eq": ("sbuf", [128, 8], "float32"), "ne": ("sbuf", [128, 8], "float32"),
-    "sg": ("sbuf", [128, 8 * C], "bfloat16"), "fb": ("sbuf", [128, 8 * C], "bfloat16"),
-    "cb": ("sbuf", [128, 8 * C], "bfloat16"), "junk": ("sbuf", [128, 8 * C], "bfloat16"),
-    "nb": ("sbuf", [128, 32], "float32"), "nt": ("sbuf", [128, 32], "float32"),
-    "ot2": ("sbuf", [128, 32], "float32"), "ott2": ("sbuf", [128, 32], "float32"), "lst2": ("sbuf", [128, 16], "uint16"),
-    "ip": ("sbuf", [128, 2], "int32"), "t1": ("sbuf", [128, 2], "int32"), "t2": ("sbuf", [128, 2], "int32"), "t3": ("sbuf", [128, 2], "int32"),
+    "pb": ("sbuf", [128, 8 * PS], "float32"),
+    "sg": ("sbuf", [128, 5 * C], "bfloat16"), "keep": ("sbuf", [128, 5 * C], "bfloat16"), "key": ("sbuf", [128, 5 * C], "float16"),
+    "cols": ("sbuf", [128, C], "bfloat16"), "low": ("sbuf", [128, C], "bfloat16"), "qb": ("sbuf", [128, 8 * PS], "float16"),
+    "lev": ("sbuf", [128, 8], "bfloat16"),
+    "nb": ("sbuf", [128, 32], "bfloat16"), "nt": ("sbuf", [128, 32], "bfloat16"), "nfo": ("sbuf", [128, 32], "float32"),
+    "nd": ("sbuf", [128, 64], "bfloat16"), "ntt": ("sbuf", [128, 64], "bfloat16"), "lst2": ("sbuf", [128, 16], "uint16"),
+    "ip": ("sbuf", [128, 2], "int32"), "t2": ("sbuf", [128, 2], "int32"), "i1": ("sbuf", [128, 2], "int32"), "i2": ("sbuf", [128, 2], "int32"),
     "col": ("sbuf", [128, 8], "float32"),
-    "cz": ("sbuf", [128, 96], "float32"), "czt": ("sbuf", [128, 96], "float32"), "off": ("sbuf", [128, 8], "uint16"),
-    "kf": ("sbuf", [128, 64], "float32"), "kft": ("sbuf", [128, 64], "float32"), "kfo": ("sbuf", [128, 64], "float32"),
+    "cz": ("sbuf", [128, 288], "bfloat16"), "czt": ("sbuf", [128, 288], "bfloat16"), "off": ("sbuf", [128, 8], "uint16"),
+    "kfo": ("sbuf", [128, 32], "float32"),
     "yb": ("sbuf", [128, C], "float32"),
     "ps": ("psum", [128, 4096], "float32"),
 }
@@ -52,7 +53,8 @@ for _r in range(3):
     SCRATCH["sv%d" % _r] = ("sbuf", [128, 128], "uint8")
     SCRATCH["land%d" % (_r + 1)] = ("sbuf", [128, 128], F8)
     SCRATCH["lsc%d" % (_r + 1)] = ("sbuf", [128, 128], "uint8")
-SEMAPHORES = ["vs", "ts", "sa", "gc0", "dk", "dn", "ldx", "ldu", "ldv", "ldw", "ldp", "loc", "arr1", "arr2", "arr3", "st"]
+SEMAPHORES = ["vs", "ts", "sa", "gc0", "ldx", "ldu", "ldv", "ldw", "ldp", "loc", "st",
+              "arr1", "arr2", "arr3", "ars1", "ars2", "ars3"]
 
 
 def rank_program(g, core, T, topo):
@@ -149,250 +151,261 @@ def rank_program(g, core, T, topo):
     def act(reads, writes, fn):
         return run("a", reads, writes, fn)
 
-    def fill(name, view, c, lo=0, hi=None):
-        vec([], [R(name, lo, hi)], lambda: g.vector.memset(view, c))
+    def fill(names, view, c):
+        vec([], names, lambda: g.vector.memset(view, c))
 
-    def iota(name, view, pat, base, lo=0, hi=None):
-        run("g", [], [R(name, lo, hi)], lambda: g.iota(view, pat, base, 0, allow_small_or_imprecise_dtypes=True))
+    def afill(names, view, n, c):
+        act([R("c32")], names, lambda: g.scalar.activation(view, T.c32[:, 0:n], ACT.Identity, bias=c, scale=0.0))
+
+    def iota(names, view, pat, base, step=0):
+        run("g", [], names, lambda: g.iota(view, pat, base, step, allow_small_or_imprecise_dtypes=True))
 
     def quant(q, s, lo, n, tile, tlo, names):
         vec(names, [R(q, lo, lo + n), R(s, lo, lo + n)], lambda: g.vector.quantize_mx(T[q][:, lo:lo + n], T[s][:, lo:lo + n], T[tile][:, tlo:tlo + 4 * n]))
 
-    def column(j, nm, sc, b):
-        vec([R(nm)], [R("col", j, j + 1)], lambda: g.vector.tensor_scalar(T.col[:, j:j + 1], T[nm][:, 0:1], sc, b, ALU.mult, ALU.add))
+    def half(nm, j):
+        vec([R("dd"), R("col", j, j + 1)], [R(nm)], lambda: g.vector.tensor_scalar(T[nm][:, 3:515:4], T.dd[:, 3:515:4], T.col[:, j:j + 1], None, ALU.mult))
 
-    def bits(nm, m):
-        vec([R("ip")], [R(nm)], lambda: g.vector.tensor_scalar(T[nm][:, 0:1], T.ip[:, 0:1], m, None, ALU.bitwise_and))
+    def column(j, sc, b):
+        vec([R("t2")], [R("col", j, j + 1)], lambda: g.vector.tensor_scalar(T.col[:, j:j + 1], T.t2[:, 0:1], sc, b, ALU.mult, ALU.add))
 
-    xtok = dmas("ldx", [("s", [], [R("xin")], T.xin[:], T.x[:])])
-    dmas("ldu", [("a", [], [R("uin")], T.uin[:], T.u[:])])
+    def later_loads():
+        need("s", deps("s", [R("xin")], []))
+        dmas("ldw", [("s", [], [R("wq")], T.wq[:].bitcast(dt.uint8), T.wc[:])])
+        dmas("ldp", [("s", [], [R("wsc")], T.wsc[:], T.ws[:])])
+        dmas("ldv", [("s", [], [R("vin")], T.vin[:], T.v[:])])
 
-    fill("c32", T.c32[:], 32.0)
-    run("g", [], [R("ip")], lambda: g.iota(T.ip[:, 0:1], [[0, 1]], 0, 1))
-    run("g", [R("c32")], [R("dd")], lambda: g.affine_select(T.dd[:], T.c32[:], [[1, 516]], ALU.is_equal, 0.0, -3, -4))
-    for blk, base, pat in ((0, 0, [[20, 2], [4, 4], [1, 2]]), (1, 2, [[20, 2], [4, 4], [1, 2]]), (2, 0, [[2, 2], [4, 4], [1, 2]])):
-        for h in range(2):
-            lo = 32 * blk + 16 * h
-            iota("cz", T.cz[:, lo:lo + 16], pat, base, lo, lo + 16)
-    iota("mones", T.mones[:], [[0, 256]], -1)
-    iota("mone7", T.mone7[:], [[0, 8]], -1)
-    iota("ones", T.ones[:], [[0, C]], 1)
-    iota("zeros", T.zeros[:], [[0, C]], 0)
-    iota("nb", T.nb[:], [[0, 32]], 0)
-    iota("ot2", T.ot2[:], [[0, 32]], 0)
-    iota("kf", T.kf[:], [[0, 64]], 0)
-    fill("rst", T.rst[:], BIG)
-    bits("t2", 16)
-    bits("t1", 96)
-    bits("t3", 31)
-    column(3, "t2", -0.0625, 1.0)
-    column(2, "t2", 0.0625, 0.0)
-    column(0, "t1", 1.0, 16.0)
-    column(1, "t1", 1.0, 32.0)
-    column(4, "t3", 16.0, 16.0)
-    act([R("dd"), R("col", 3, 4)], [R("dde")], lambda: g.scalar.activation(T.dde[:], T.dd[:], ACT.Copy, scale=T.col[:, 3:4]))
-    act([R("dd"), R("col", 2, 3)], [R("ddo")], lambda: g.scalar.activation(T.ddo[:], T.dd[:], ACT.Copy, scale=T.col[:, 2:3]))
-    fill("rst", T.rst[:, 0:128:16], -BIG)
-    fill("pa", T.pa[:, 0:288:144], -BIG, 0, 1)
-    fill("pb", T.pb[:, 0:8 * PS:PS], -BIG)
-    fill("bigc", T.bigc[:], BIG)
-    for b in range(4):
-        quant("cf", "scf", 128 * b, 128, "dd", 3 - b, [R("dd")])
-    for b in range(4):
-        quant("ce", "sce", 128 * b, 128, "dde", 3 - b, [R("dde")])
-    quant("qu", "squ", 0, 128, "uin", 0, [R("uin")])
-    for b in range(4):
-        quant("cd", "scd", 128 * b, 128, "ddo", 3 - b, [R("ddo")])
-    quant("qx0", "sx0", 0, C, "xin", 0, [R("xin")])
-    need("s", [xtok])
-    dmas("ldw", [("s", [], [R("wq")], T.wq[:].bitcast(dt.uint8), T.wc[:])])
-    dmas("ldp", [("s", [], [R("wsc")], T.wsc[:], T.ws[:])])
-    dmas("ldv", [("s", [], [R("vin")], T.vin[:], T.v[:])])
+    def row(lo, hi, pat, base, step=0):
+        iota([R("cz", lo, hi)], T.cz[:, lo:hi], pat, base, step)
 
-    SB, SB2, YB = 6, 7, 7
-    RB = [4, 5, 0, 1]
-    VB = [2, 3, 4, 5]
-    ncol = [16 * (k % 2) + k // 2 for k in range(8)]
+    first = [
+        lambda: dmas("ldx", [("s", [], [R("xin")], T.xin[:], T.x[:])]),
+        lambda: dmas("ldu", [("a", [], [R("uin")], T.uin[:], T.u[:])]),
+        lambda: fill([R("c32")], T.c32[:], 32.0),
+        lambda: fill([R("dd")], T.dd[:], 0.0),
+        lambda: run("g", [], [R("ip")], lambda: g.iota(T.ip[:, 0:1], [[0, 1]], 0, 1)),
+        lambda: run("g", [R("c32")], [R("dd")], lambda: g.affine_select(T.dd[:, 3:515:4], T.c32[:, 0:128], [[1, 128]], ALU.is_equal, 0.0, 0, -1)),
+        lambda: fill([R("dde")], T.dde[:], 0.0),
+        lambda: fill([R("ddo")], T.ddo[:], 0.0),
+        lambda: vec([R("ip")], [R("t2")], lambda: g.vector.tensor_scalar(T.t2[:, 0:1], T.ip[:, 0:1], 16, None, ALU.bitwise_and)),
+        lambda: column(0, -0.0625, 1.0),
+        lambda: column(1, 0.0625, 0.0),
+        lambda: half("dde", 0),
+        lambda: half("ddo", 1),
+        lambda: afill([R("rst")], T.rst[:], C, BIG),
+        lambda: afill([R("pa", 0, 1)], T.pa[:, 0:1], 1, -BIG),
+        lambda: afill([R("rst")], T.rst[:, 0:C:16], C // 16, -BIG),
+        lambda: afill([R("bigc")], T.bigc[:], C, BIG),
+        lambda: afill([R("pb", PS * k, PS * k + 1) for k in range(8)], T.pb[:, 0:8 * PS:PS], 8, -BIG),
+        lambda: afill([R("low")], T.low[:], C, -KEY),
+        lambda: iota([R("down")], T.down[:], [[0, C // 16], [-1, 16]], 16),
+        lambda: iota([R("ag", C, 512)], T.ag[:, C:512], [[0, 512 - C]], 1),
+        lambda: row(0, 32, [[0, 2], [2, 8], [32, 2]], 0), lambda: row(32, 64, [[0, 2], [2, 8], [32, 2]], 1),
+        lambda: row(64, 192, [[16, 2], [0, 4], [1, 16]], 0),
+        lambda: row(192, 224, [[0, 16], [16, 2]], 16, 1), lambda: row(224, 256, [[0, 4], [32, 4], [0, 2]], 128, -1),
+        lambda: (row(256, 272, [[16, 2], [0, 4], [128, 2]], 0, 1), row(272, 288, [[16, 2], [0, 4], [128, 2]], 0, 1)),
+        lambda: iota([R("cols")], T.cols[:], [[1, C]], -112),
+        lambda: afill([R("keep0")], T.keep[:, 0:5 * C:5], C, 0.0), lambda: afill([R("keep1")], T.keep[:, 1:5 * C:5], C, 1.0),
+        lambda: afill([R("keep2")], T.keep[:, 2:5 * C:5], C, 1.0), lambda: afill([R("keep3")], T.keep[:, 3:5 * C:5], C, 1.0),
+        lambda: act([R("cols")], [R("sg0")], lambda: g.scalar.activation(T.sg[:, 0:5 * C:5], T.cols[:], ACT.Copy, scale=2.0 ** -8)),
+        lambda: vec([R("c32")], [R("qb", PS * k, PS * k + 1) for k in range(8)],
+                    lambda: g.vector.tensor_scalar(T.qb[:, 0:8 * PS:PS], T.c32[:, 0:8], KEY / 32.0, None, ALU.mult)),
+        lambda: quant("ce", "sce", 0, 128, "dde", 3, [R("dde")]), lambda: quant("ce", "sce", 128, 128, "dde", 2, [R("dde")]),
+        lambda: quant("ce", "sce", 256, 128, "dde", 1, [R("dde")]), lambda: quant("ce", "sce", 384, 128, "dde", 0, [R("dde")]),
+        lambda: quant("cd", "scd", 0, 128, "ddo", 3, [R("ddo")]), lambda: quant("cd", "scd", 128, 128, "ddo", 2, [R("ddo")]),
+        lambda: quant("cd", "scd", 256, 128, "ddo", 1, [R("ddo")]), lambda: quant("cd", "scd", 384, 128, "ddo", 0, [R("ddo")]),
+        lambda: quant("qu", "squ", 0, 128, "uin", 0, [R("uin")]),
+        lambda: quant("qx0", "sx0", 0, C, "xin", 0, [R("xin")]),
+        later_loads,
+        lambda: vec([R("cz")], [R("czt")], lambda: g.vector.transpose(T.czt[:], T.cz[:])),
+        lambda: vec([R("czt")], [R("off", 0, 6)], lambda: g.vector.tensor_copy(T.off[:, 0:6], T.czt[:, 0:192:32])),
+        lambda: afill([R("keep4")], T.keep[:, 4:5 * C:5], C, 1.0),
+        lambda: quant("cf", "scf", 384, 128, "dd", 0, [R("dd")]),
+        lambda: act([R("czt")], [R("col", 2, 3)], lambda: g.scalar.activation(T.col[:, 2:3], T.czt[:, 192:193], ACT.Copy)),
+        lambda: vec([R("czt")], [R("i1")], lambda: g.vector.tensor_copy(T.i1[:, 0:1], T.czt[:, 224:225])),
+        lambda: act([R("czt")], [R("col", 3, 4)], lambda: g.scalar.activation(T.col[:, 3:4], T.czt[:, 256:257], ACT.Copy, scale=0.25)),
+        lambda: vec([R("i1")], [R("i2")], lambda: g.vector.tensor_scalar(T.i2[:, 0:1], T.i1[:, 0:1], 127, None, ALU.bitwise_and)),
+        lambda: vec([R("i2"), R("col", 3, 4)], [R("off", 6, 7)], lambda: g.vector.tensor_scalar(T.off[:, 6:7], T.i2[:, 0:1], 2.0 ** -5, T.col[:, 3:4], ALU.mult, ALU.add)),
+    ]
+
+    SB = [6, 7]
+    RB = [4, 5, 7, 6]
+    YB = 4
     for r in range(3):
-        last = r == 2
         X, SX, X1, SX1 = "qx%d" % r, "sx%d" % r, "qx%d" % (r + 1), "sx%d" % (r + 1)
         U, SU = ("qu", "squ") if r == 0 else ("land%d" % r, "lsc%d" % r)
         ue, se, uo, so, qz, sz, pk, sk, qv, sv = [n + str(r) for n in ("ue", "se", "uo", "so", "qz", "sz", "pk", "sk", "qv", "sv")]
 
         def tee(b, j):
-            mm(j, C, "cf", "scf", 128 * b, X, SX, 0, True, False)
+            if r or b == 3:
+                mm(j, C, "cf", "scf", 128 * b, X, SX, 0, True, False)
+            else:
+                mm(j, C, "ce", "sce", 128 * b, X, SX, 0, True, False)
+                mm(j, C, "cd", "scd", 128 * b, X, SX, 0, False, False)
 
-        if r:
-            for b in range(4):
-                tee(b, b)
-        for h in range(2):
-            mm(4 + h, 128, X, SX, 96 * h, U, SU, 0, True, True)
-        mm(SB, C, U, SU, 0, X, SX, 0, True, True)
-        mm(SB2, C, U, SU, 0, X, SX, 0, True, True)
-        if not r:
-            for b in range(4):
-                tee(b, b)
-        for h in range(2):
-            p0 = 144 * h
-            vec([R("bank%d" % (4 + h)), R("rst")], [R("pa", p0 + 1, p0 + 129)],
-                lambda: g.vector.tensor_tensor_scan(T.pa[:, p0 + 1:p0 + 129], T.rst[:], bank(4 + h, 128), -BIG, ALU.min, ALU.max))
-        for h in range(2):
-            p0 = 144 * h
-            vec([R("bank%d" % (4 + h)), R("pa", p0, p0 + 128)], [R("nr", 128 * h, 128 * h + 128)],
-                lambda: g.vector.tensor_tensor(T.nr[:, 128 * h:128 * h + 128], bank(4 + h, 128), T.pa[:, p0:p0 + 128], ALU.is_le))
-        for b in range(2):
-            tee(b, RB[b])
-        vec([R("nr"), R("mones")], [R("ag")], lambda: g.vector.tensor_tensor_scan(T.ag[:], T.nr[:], T.mones[:], 0.0, ALU.mult, ALU.add))
-        if not r:
-            vec([R("cz")], [R("czt")], lambda: g.vector.transpose(T.czt[:], T.cz[:]))
-        vec([R("ag")], [R("kt")], lambda: g.vector.transpose(T.kt[:], T.ag[:]))
-        dmas("dk", [("s" if h == 0 else "a", [R("kt")], [R("ot", 0, 16)], T.ot[32 * a + 16 * h:32 * a + 16 * h + 16, 0:16],
-                     T.kt[15:128:16, 128 * h + 32 * a:128 * h + 32 * a + 32]) for a in range(4) for h in range(2)])
-        if not r:
-            vec([R("czt")], [R("off")], lambda: g.vector.tensor_scalar(T.off[:, 0:6:2], T.czt[:, 0:96:32], 31.0, None, ALU.min))
+        def turn_scores(k):
+            vec([R("bank%d" % SB[0])], [R("st")], lambda: g.vector.transpose(T.st[:], bank(SB[0], C)))
+
+        def highest(k):
+            vec([R("st"), R("rst")], [R("pa", 1, C + 1)], lambda: g.vector.tensor_tensor_scan(T.pa[:, 1:C + 1], T.rst[:], T.st[:], -BIG, ALU.min, ALU.max))
+
+        def records(k):
+            vec([R("st"), R("pa", 0, C)], [R("nr")], lambda: g.vector.tensor_tensor(T.nr[:], T.st[:], T.pa[:, 0:C], ALU.is_le))
+
+        def rows(k):
+            vec([R("nr"), R("down")], [R("ag", 0, C)], lambda: g.vector.tensor_tensor_scan(T.ag[:, 0:C], T.nr[:], T.down[:], 0.0, ALU.mult, ALU.max))
+
+        def ends(k):
+            vec([R("ag")], [R("kt")], lambda: g.vector.transpose(T.kt[:], T.ag[:, 15:512:16]))
+
+        def twice(k):
+            vec([R("kt"), R("off", 0, 6), R("col", 2, 3)], [R("kd")],
+                lambda: g.vector.tensor_scalar(T.kd[:], T.kt[:, 0:32].indirect(T.off[:, 2:6]), -1.0, T.col[:, 2:3], ALU.mult, ALU.add))
+
+        def turn(o, nm):
+            vec([R(nm)], [R(o)], lambda: g.vector.transpose(T[o][:], T[nm][:]))
+
+        def lists_down(k):
+            vec([R("ktt"), R("off", 0, 6)], [R("lst")], lambda: g.vector.tensor_copy(T.lst[:], T.ktt[:, 0:64].indirect(T.off[:, 0:2])))
+
+        def pick_u(e):
+            q = (ue, uo)[e]
+            vec([R(U), R("lst")], [R(q)],
+                lambda: g.vector.tensor_copy(T[q][:].bitcast(dt.uint32), T[U][:].bitcast(dt.uint32).indirect(T.lst[:, 16 * e:16 * e + 14])))
+
+        def pick_us(e):
+            s = (se, so)[e]
+            act([R(SU), R("lst")], [R(s)], lambda: g.scalar.activation(T[s][:], T[SU][:].indirect(T.lst[:, 16 * e:16 * e + 14]), ACT.Copy))
 
         def scan(k):
-            o = PS * k
-            d1 = [R("bigc")] if k == 0 else [R("pb", o - PS, o - PS + 224)]
-            vec([R("bank%d" % SB)] + d1, [R("pb", o + 1, o + 225)],
-                lambda: g.vector.tensor_tensor_scan(T.pb[:, o + 1:o + 225], bank(SB, C), T.bigc[:] if k == 0 else T.pb[:, o - PS:o - PS + 224], -BIG, ALU.max, ALU.min))
+            lo, hi = ((0, C), (0, C // 2), (C // 2, C))[k // 10]
+            k %= 10
+            o = PS * k + lo
+            n = hi - lo
+            d1 = [R("bigc")] if k == 0 else [R("pb", o - PS, o - PS + n)]
+            vec([R("bank%d" % SB[0])] + d1 + ([R("pb", o, o + 1)] if lo else []), [R("pb", o + 1, o + n + 1)],
+                lambda: g.vector.tensor_tensor_scan(T.pb[:, o + 1:o + n + 1], T.ps[:, 512 * SB[0] + lo:512 * SB[0] + hi], T.bigc[:, 0:n] if k == 0 else T.pb[:, o - PS:o - PS + n],
+                                                    T.pb[:, o:o + 1] if lo else -BIG, ALU.max, ALU.min))
 
         def sign(k):
-            o = PS * k + 224
-            act([R("bank%d" % SB2), R("pb", o, o + 1)], [R("sg", C * k, C * k + C)],
-                lambda: g.scalar.activation(T.sg[:, C * k:C * k + C], bank(SB2, C), ACT.Sign, bias=T.pb[:, o:o + 1], scale=-1.0))
+            o = PS * k + C
+            j = k // 2 + 1
+            act([R("bank%d" % SB[1]), R("pb", o, o + 1)], [R("sg%d" % j)],
+                lambda: g.scalar.activation(T.sg[:, j:5 * C:5], bank(SB[1], C), ACT.Sign, bias=T.pb[:, o:o + 1], scale=-1.0))
 
-        def flags(k):
-            o = PS * k + 224
-            if k in NS:
-                vec([R("sg", C * k, C * k + C)], [R("fb", C * k, C * k + C)],
-                    lambda: g.vector.tensor_scalar(T.fb[:, C * k:C * k + C], T.sg[:, C * k:C * k + C], 0.0, None, ALU.is_equal))
+        def keys(k):
+            vec([R("keep%d" % j) for j in range(5)] + [R("sg%d" % j) for j in range(5)], [R("key")],
+                lambda: g.vector.tensor_tensor_scan(T.key[:], T.keep[:], T.sg[:], 0.0, ALU.mult, ALU.add))
+
+        def least(k):
+            o = PS * k
+            b = o - PS
+            vec([R("key"), R("low") if k == 0 else R("qb", b, b + C)], [R("qb", o + 1, o + C + 1)],
+                lambda: g.vector.tensor_tensor_scan(T.qb[:, o + 1:o + C + 1], T.key[:, 4:5 * C:5], T.low[:] if k == 0 else T.qb[:, b:b + C], KEY, ALU.min, ALU.max))
+
+        def levels(k):
+            vec([R("qb")], [R("lev")], lambda: g.vector.tensor_scalar(T.lev[:], T.qb[:, C:8 * PS:PS], ROUND, -ROUND, ALU.add, ALU.add))
+
+        def fractions(k):
+            vec([R("qb"), R("lev")], [R("nba")], lambda: g.vector.tensor_tensor(T.nb[:, 0:32:4], T.qb[:, C:8 * PS:PS], T.lev[:], ALU.subtract))
+
+        def spread(q, k):
+            if k < 2:
+                o, i = T.nb[64 * k:64 * k + 64, 2:32:4], T.nb[64 - 64 * k:128 - 64 * k, 0:32:4]
+                rd, wr = [R("nba")], [R("nbb%d" % k)]
             else:
-                vec([R("bank%d" % SB), R("pb", o, o + 1)], [R("fb", C * k, C * k + C)],
-                    lambda: g.vector.tensor_scalar(T.fb[:, C * k:C * k + C], bank(SB, C), T.pb[:, o:o + 1], None, ALU.is_equal))
-
-        def same(k):
-            vec([R("pb")], [R("eq")], lambda: g.vector.tensor_tensor(T.eq[:, 1:8], T.pb[:, PS + 224:8 * PS:PS], T.pb[:, 224:7 * PS:PS], ALU.is_equal))
-
-        def less(k):
-            vec([R("eq"), R("mone7")], [R("ne")], lambda: g.vector.tensor_tensor_scan(T.ne[:, 1:8], T.mone7[:, 0:7], T.eq[:, 1:8], 0.0, ALU.add, ALU.mult))
-
-        def counts(k):
-            vec([R("fb", C * k, C * k + C), R("ne"), R("ones")], [R("cb", C * k, C * k + C)],
-                lambda: g.vector.tensor_tensor_scan(T.cb[:, C * k:C * k + C], T.fb[:, C * k:C * k + C], T.ones[:], T.ne[:, k:k + 1], ALU.add, ALU.min))
-
-        def places(k):
-            if k == 0:
-                act([R("pb", 0, 225)], [R("nb", ncol[0], ncol[0] + 1), R("junk", 0, C)],
-                    lambda: g.scalar.activation(T.junk[:, 0:C], T.pb[:, 1:225], ACT.Sign, bias=T.pb[:, 224:225], scale=-1.0, accum_out=T.nb[:, ncol[0]:ncol[0] + 1]))
+                a, b = k - 2, (k - 1) % 4
+                o, i = T.nb[32 * a:32 * a + 32, 1:32:2], T.nb[32 * b:32 * b + 32, 0:32:2]
+                rd, wr = [R("nba"), R("nbb%d" % (b // 2))], [R("nbc%d" % a)]
+            if q == "a":
+                act(rd, wr, lambda: g.scalar.activation(o, i, ACT.Copy))
             else:
-                act([R("cb", C * k, C * k + C)], [R("nb", ncol[k], ncol[k] + 1), R("junk", C * k, C * k + C)],
-                    lambda: g.scalar.activation(T.junk[:, C * k:C * k + C], T.cb[:, C * k:C * k + C], ACT.Sign, bias=1.0, scale=-1.0, accum_out=T.nb[:, ncol[k]:ncol[k] + 1]))
+                vec(rd, wr, lambda: g.vector.tensor_copy(o, i))
 
-        def rest(k):
-            vec([R("cb", C * k, C * k + C), R("zeros")], [R("junk", C * k, C * k + C)],
-                lambda: g.vector.tensor_tensor_scan(T.junk[:, C * k:C * k + C], T.cb[:, C * k:C * k + C], T.zeros[:], 0.0, ALU.add, ALU.max))
+        def turn_along(k):
+            vec([R("nba"), R("nbb0"), R("nbb1")] + [R("nbc%d" % a) for a in range(4)], [R("nt")], lambda: g.vector.transpose(T.nt[:], T.nb[:]))
 
-        def pair(k):
-            vec([R("junk", C * k, C * k + 2 * C)], [R("nb", ncol[k], ncol[k] + 1), R("nb", ncol[k + 1], ncol[k + 1] + 1)],
-                lambda: g.vector.tensor_scalar(T.nb[:, ncol[k]:ncol[k + 1] + 1:16], T.junk[:, C * k + C - 1:C * k + 2 * C:C], -1.0, float(C), ALU.mult, ALU.add))
+        def both(k):
+            vec([R("nt"), R("off", 0, 6)], [R("nd")], lambda: g.vector.tensor_copy(T.nd[:], T.nt[:, 0:32].indirect(T.off[:, 2:6])))
 
-        def halves(k):
-            vec([R("ot", 0, 16)], [R("ot", 16, 32)], lambda: g.vector.tensor_copy(T.ot[:, 16:32], T.ot[:, 0:16]))
+        def lists_along(k):
+            vec([R("ntt"), R("off", 6, 7)], [R("lst2")],
+                lambda: g.vector.tensor_scalar(T.lst2[:], T.ntt[:, 0:64].indirect(T.off[:, 6:7]), 256.0, 112.0, ALU.mult, ALU.add))
 
-        def turn(k):
-            vec([R("ot")], [R("ott")], lambda: g.vector.transpose(T.ott[:], T.ot[:]))
-
-        def picks(e):
-            q, s = ((ue, se), (uo, so))[e]
-            vec([R("ott"), R("off"), R("col")], [R("lst", 16 * e, 16 * e + 16)],
-                lambda: g.vector.tensor_scalar(T.lst[:, 16 * e:16 * e + 16], T.ott[:, 0:32].indirect(T.off[:, 2 * e:2 * e + 1]), -16.0, T.col[:, e:e + 1], ALU.max, ALU.add))
-            vec([R(U), R("lst", 16 * e, 16 * e + 16)], [R(q)],
-                lambda: g.vector.tensor_copy(T[q][:].bitcast(dt.uint32), T[U][:].bitcast(dt.uint32).indirect(T.lst[:, 16 * e:16 * e + 14])))
-            act([R(SU), R("lst", 16 * e, 16 * e + 16)], [R(s)],
-                lambda: g.scalar.activation(T[s][:], T[SU][:].indirect(T.lst[:, 16 * e:16 * e + 14]), ACT.Copy))
-            for b in range(4):
-                mm(b, C, ("ce", "cd")[e], ("sce", "scd")[e], 128 * b, q, s, 0, False, e == 1)
-
-        def zed(b):
-            act([R("bank%d" % b)], [R("zt%d" % b)], lambda: g.scalar.activation(T.zt[:, b:4 * C:4], bank(b, C), ACT.Copy, scale=2.0 ** -6))
-
-        def zedv(b):
-            vec([R("bank%d" % b)], [R("zt%d" % b)], lambda: g.vector.tensor_scalar(T.zt[:, b:4 * C:4], bank(b, C), 2.0 ** -6, None, ALU.mult))
-
-        def send_lists(k):
-            vec([R("nb")], [R("nt")], lambda: g.vector.transpose(T.nt[:], T.nb[:]))
-            dmas("dn", [("sa"[h], [R("nt")], [R("ot2", 16 * h, 16 * h + 16)], T.ot2[32 * a:32 * a + 16, 16 * h:16 * h + 16], T.nt[a:128:16, 0:32])
-                        for a in range(4) for h in range(2)])
-
-        def state(k):
-            for b in (2, 3):
-                tee(b, RB[b])
-            quant(qz, sz, 0, C, "zt", 0, [R("zt%d" % b) for b in range(4)])
-            for b in range(4):
-                mm(RB[b], C, "wq", "wsc", 128 * b, qz, sz, 0, False, True)
-
-        def newx(b):
-            act([R("bank%d" % RB[b])], [R("xt%d" % b)], lambda: g.scalar.activation(T.xt[:, b:4 * C:4], bank(RB[b], C), ACT.Copy, scale=2.0 ** -5))
-
-        def newxv(b):
-            vec([R("bank%d" % RB[b])], [R("xt%d" % b)], lambda: g.vector.tensor_scalar(T.xt[:, b:4 * C:4], bank(RB[b], C), 2.0 ** -5, None, ALU.mult))
-
-        steps = {"s": scan, "n": sign, "f": flags, "q": same, "e": less, "c": counts, "p": places, "w": rest, "P": pair,
-                 "D": halves, "X": turn, "E": lambda k: picks(0), "O": lambda k: picks(1), "Z": zed, "z": zedv,
-                 "N": send_lists, "Q": state, "R": newx, "r": newxv}
-        for word in SEQ.split():
-            steps[word[0]](int(word[1:] or "0"))
-        quant(X1, SX1, 0, C, "xt", 0, [R("xt%d" % b) for b in range(4)])
-        vec([R("ot2")], [R("ott2")], lambda: g.vector.transpose(T.ott2[:], T.ot2[:]))
-        vec([R("ott2"), R("off")], [R("lst2")], lambda: g.vector.tensor_copy(T.lst2[:], T.ott2[:, 0:32].indirect(T.off[:, 4:5])))
-        for e in range(2):
+        def pick_x(e):
             lo = 128 * e
             vec([R(X1), R("lst2")], [R(pk, lo, lo + 128)],
                 lambda: g.vector.tensor_copy(T[pk][:, lo:lo + 128].bitcast(dt.uint32), T[X1][:].bitcast(dt.uint32).indirect(T.lst2[:, 8 * e:8 * e + 8])))
+
+        def pick_xs(e):
+            lo = 128 * e
             act([R(SX1), R("lst2")], [R(sk, lo, lo + 128)],
                 lambda: g.scalar.activation(T[sk][:, lo:lo + 128], T[SX1][:].indirect(T.lst2[:, 8 * e:8 * e + 8]), ACT.Copy))
-            for b in range(4):
-                mm(VB[b], 128, ("ce", "cd")[e], ("sce", "scd")[e], 128 * b, pk, sk, lo, e == 0, e == 1)
-        for b in range(4):
-            if b % 2 == 0:
-                act([R("bank%d" % VB[b])], [R("vt%d" % b)], lambda: g.scalar.activation(T.vt[:, b:512:4], bank(VB[b], 128), ACT.Copy, scale=2.0 ** -5))
+
+        def cast(q, tile, b, j, n, scale):
+            if q == "a":
+                act([R("bank%d" % j)], [R(tile + str(b))], lambda: g.scalar.activation(T[tile][:, b:4 * n:4], bank(j, n), ACT.Copy, scale=scale))
             else:
-                vec([R("bank%d" % VB[b])], [R("vt%d" % b)], lambda: g.vector.tensor_scalar(T.vt[:, b:512:4], bank(VB[b], 128), 2.0 ** -5, None, ALU.mult))
-        quant(qv, sv, 0, 128, "vt", 0, [R("vt%d" % b) for b in range(4)])
-        dst = T.cores[(rank + STEP[r]) % 8]
-        src = T.cores[(rank - STEP[r]) % 8]
-        rid, pid = topo.addr(dst, core)
-        need("g", deps("g", [R(qv), R(sv)], []))
-        arr = "arr%d" % (r + 1)
-        ld, ls = T["land%d" % (r + 1)], T["lsc%d" % (r + 1)]
-        g.remote_dma(ld[:].bitcast(dt.uint8), T[qv][:].bitcast(dt.uint8), T.sem[arr], T.sem["loc"], pid, rid, topo.mask(core, dst))
-        g.remote_dma(ls[:], T[sv][:], T.sem[arr], T.sem["loc"], pid, rid, topo.mask(core, dst))
-        count["loc"] += 2 * len(topo.engines(core, dst))
-        count[arr] = 2 * len(topo.engines(src, core))
-        note("g", (arr, count[arr], {arr: count[arr]}), [], [R("land%d" % (r + 1)), R("lsc%d" % (r + 1))])
+                vec([R("bank%d" % j)], [R(tile + str(b))], lambda: g.vector.tensor_scalar(T[tile][:, b:4 * n:4], bank(j, n), scale, None, ALU.mult))
+
+        def hand_on(k):
+            quant(qv, sv, 0, 128, "vt", 0, [R("vt%d" % b) for b in range(4)])
+            dst = T.cores[(rank + STEP[r]) % 8]
+            src = T.cores[(rank - STEP[r]) % 8]
+            rid, pid = topo.addr(dst, core)
+            need("g", deps("g", [R(qv), R(sv)], []))
+            for nm, view, mine, sem in (("land", T["land%d" % (r + 1)][:].bitcast(dt.uint8), T[qv][:].bitcast(dt.uint8), "arr"), ("lsc", T["lsc%d" % (r + 1)][:], T[sv][:], "ars")):
+                arr = sem + str(r + 1)
+                g.remote_dma(view, mine, T.sem[arr], T.sem["loc"], pid, rid, topo.mask(core, dst))
+                count["loc"] += len(topo.engines(core, dst))
+                count[arr] = len(topo.engines(src, core))
+                note("g", (arr, count[arr], {arr: count[arr]}), [], [R(nm + str(r + 1))])
+
+        steps = {
+            "k": lambda k: first[k](),
+            "B": lambda j: mm(SB[j], C, U, SU, 0, X, SX, 0, True, True),
+            "T": lambda b: tee(b, b), "U": lambda b: tee(b, RB[b]),
+            "M": lambda b: mm(b, C, "ce", "sce", 128 * b, ue, se, 0, False, False),
+            "K": lambda b: mm(b, C, "cd", "scd", 128 * b, uo, so, 0, False, True),
+            "W": lambda b: mm(RB[b], C, "wq", "wsc", 128 * b, qz, sz, 0, False, True),
+            "G": lambda b: mm(b, 128, "ce", "sce", 128 * b, pk, sk, 0, True, False),
+            "H": lambda b: mm(b, 128, "cd", "scd", 128 * b, pk, sk, 128, False, True),
+            "c": turn_scores, "a": highest, "b": records, "g": rows, "t": ends, "D": twice, "X": lambda k: turn("ktt", "kd"),
+            "L": lists_down, "E": pick_u, "e": pick_us,
+            "s": scan, "n": sign, "j": keys, "u": least, "f": levels, "h": fractions,
+            "i": lambda k: spread("v", k), "I": lambda k: spread("a", k), "N": turn_along,
+            "d": both, "x": lambda k: turn("ntt", "nd"), "l": lists_along, "P": pick_x, "p": pick_xs,
+            "Z": lambda b: cast("a", "zt", b, b, C, 2.0 ** -6), "z": lambda b: cast("v", "zt", b, b, C, 2.0 ** -6),
+            "R": lambda b: cast("a", "xt", b, RB[b], C, 2.0 ** -5), "r": lambda b: cast("v", "xt", b, RB[b], C, 2.0 ** -5),
+            "C": lambda b: cast("a", "vt", b, b, 128, 2.0 ** -5), "v": lambda b: cast("v", "vt", b, b, 128, 2.0 ** -5),
+            "Q": lambda k: quant(qz, sz, 0, C, "zt", 0, [R("zt%d" % b) for b in range(4)]),
+            "Y": lambda k: quant(X1, SX1, 0, C, "xt", 0, [R("xt%d" % b) for b in range(4)]),
+            "V": hand_on,
+        }
+        if r:
+            for b in range(4):
+                tee(b, b)
+        for word in (SEQ if r else SEQ0).split():
+            steps[word[0]](int(word[1:] or "0"))
         if r == 0:
+            for b in range(3):
+                quant("cf", "scf", 128 * b, 128, "dd", 3 - b, [R("dd")])
             quant("qvv", "sqvv", 0, 128, "vin", 0, [R("vin")])
-    for h in range(2):
-        vec([R("ag")], [R("kf", 32 * h, 32 * h + 8)], lambda: g.vector.tensor_copy(T.kf[:, 32 * h:32 * h + 8], T.ag[:, 128 * h + 15:128 * h + 128:16]))
-    vec([R("kf")], [R("kft")], lambda: g.vector.transpose(T.kft[:], T.kf[:]))
-    vec([R("kft"), R("col")], [R("kfo")], lambda: g.vector.tensor_scalar(T.kfo[:], T.kft[:], -16.0, T.col[:, 4:5], ALU.max, ALU.add))
     mm(YB, C, "qvv", "sqvv", 0, "qx3", "sx3", 0, True, True)
     act([R("bank%d" % YB)], [R("yb")], lambda: g.scalar.activation(T.yb[:], bank(YB, C), ACT.Copy))
+    vec([R("nt")], [R("nfo")], lambda: g.vector.tensor_scalar(T.nfo[:], T.nt[:], 256.0, 112.0, ALU.mult, ALU.add))
+    vec([R("kt"), R("col", 2, 3)], [R("kfo")], lambda: g.vector.tensor_scalar(T.kfo[:], T.kt[:], -1.0, T.col[:, 2:3], ALU.mult, ALU.add))
     jobs = [("s", [R("qx3")], [], T.oc[:], T.qx3[:].bitcast(dt.uint8))]
     jobs += [("s", [R("sx3")], [], T.osc[4 * k:4 * k + 4, :], T.sx3[32 * k:32 * k + 4, :]) for k in range(4)]
-    for A in range(4):
-        for e in range(2):
-            jobs.append(("s", [R("nt")], [], T.op[e:8:2, 224 + 32 * A:256 + 32 * A], T.nt[32 * A + 16 * e:32 * A + 16 * e + 4, 0:32]))
-    jobs.append(("s", [R("yb")], [], T.y[:], T.yb[:]))
-    for A in range(4):
-        for h in range(2):
-            if h == 0 or A:
-                jobs.append(("s", [R("kfo")], [], T.op[0:8, 96 * h + 32 * A:96 * h + 32 * A + 32], T.kfo[32 * A:32 * A + 8, 32 * h:32 * h + 32]))
+    jobs.append(("a", [R("yb")], [], T.y[:], T.yb[:]))
+    jobs += [("a", [R("nfo")], [], T.op[0:8, C + 32 * a:C + 32 * a + 32], T.nfo[a:32:4, 0:32]) for a in range(4)]
+    for k in range(8):
+        p = 32 * (k // 2) + k % 2
+        jobs.append(("sa"[k // 6], [R("kfo")], [], T.op[k:k + 1, 0:C], T.kfo[p:p + 14:2, 0:32]))
     dmas("st", jobs)
     jobs = [("s", [R("land3")], [], T.uc[:], T.land3[:].bitcast(dt.uint8))]
     jobs += [("as"[k % 2], [R("lsc3")], [], T.usc[4 * k:4 * k + 4, :], T.lsc3[32 * k:32 * k + 4, :]) for k in range(4)]
     dmas("st", jobs)
     g.wait_ge(T.sem["loc"], count["loc"])
-    for s in ("vs", "ts", "sa", "gc0", "dk", "dn", "ldx", "ldu", "ldv", "ldw", "ldp", "st"):
+    for s in ("vs", "ts", "sa", "gc0", "ldx", "ldu", "ldv", "ldw", "ldp", "st"):
         g.sync.wait_ge(T.sem[s], count[s])

@@ -4,13 +4,12 @@ STEP = [4, 1, 2]
 C = 224
 BIG = 1.0e29
 KEY = 64.0
-ROUND = 12582912.0
 PS = 232
 F8 = "float8_e4m3fn_x4"
 ALU = AluOpType
 ACT = ActivationFunctionType
-SEQ = "B0 c s0 U1 a U0 B1 s1 b s2 g n1 s3 t D s4 X s5 L n3 s6 e0 E0 M2 M3 n5 s7 n7 E1 M0 M1 e1 j K1 Z1 K0 u0 u1 u2 K2 u3 Z0 K3 U2 Z2 Z3 u4 u5 U3 u6 Q W3 u7 f W1 W2 W0 h r3 I0 i2 I1 i5 i3 R1 i4 N d x R2 R0 Y l P0 p0 G0 G2 G1 p1 P1 H0 H1 v1 C0 H2 C2 G3 H3 v3 V"
-SEQ0 = "k0 k3 k1 k4 k8 k2 k44 k9 k5 k25 k24 k10 k6 k7 k21 k11 k33 k12 k37 k35 k34 k17 k26 k29 k23 k13 k42 k16 k43 B0 k38 k39 k36 k14 k15 c B1 k20 s0 k18 a k28 k22 s1 T0 k45 k30 b k27 k31 k19 s2 k32 k46 g s3 k47 t T1 k48 n1 k49 D s4 X n3 s5 n5 L e0 k40 s6 T3 T2 E0 M3 M1 s7 E1 k41 e1 n7 M2 K2 j K3 Z3 K1 Z1 u0 u1 u2 U3 u3 u4 k50 u5 U2 k51 M0 K0 Z2 k52 Z0 u6 u7 Q f h I1 U0 i0 k53 i2 I5 U1 W1 R1 i4 i3 W2 N d W3 r3 R2 x l W0 R0 Y p0 P0 G3 P1 G0 p1 G2 H2 C2 H0 v0 G1 H1 H3 C1 v3 V"
+SEQ = "T0 T1 T2 T3 U0 U1 B0 c s0 a s1 b s2 g t O B1 s3 n1 X s4 L s5 E0 n3 s6 s7 e0 n5 e1 M3 M2 E1 M0 M1 K3 n7 j Z3 u0 K0 u1 Z0 K2 z2 u2 K1 Z1 Q m0 m3 u3 u4 u5 m1 u6 m2 U2 U3 f u7 W3 R3 W0 R0 W1 r1 h2 h0 W2 R2 h1 I2 I3 Y A0 i1 i0 N o A2 w0 J2 A1 J1 x l F0 A3 w3 y2 y3 F1 V"
+SEQ0 = "k0 k1 k2 k3 k4 k5 k6 k13 k14 k33 k17 k8 k7 k9 k22 k18 k16 k30 k10 k55 k27 k11 k48 k12 k36 k26 k28 k35 k15 k32 k23 k19 k38 k42 k43 k44 B0 k34 k24 k39 k40 U0 c k47 s0 B1 a k31 T2 s1 T0 T3 k25 b s2 n1 U1 k29 k21 k20 k54 g k45 s3 t k49 k46 O T1 n3 s4 s5 X k51 s6 L n5 s7 U3 E0 e0 M1 E1 n7 j k37 M2 e1 u0 m1 k41 u1 m0 m2 k57 u2 M0 k50 K1 Z1 u3 K2 K0 Z0 z2 M3 K3 Z3 u4 Q U2 u5 W3 m3 k56 W0 R3 W2 W1 u6 f u7 k52 R0 h0 h2 R2 h1 r1 i0 I2 I1 I3 Y N d A2 J2 k53 A0 J0 A1 x A3 l w1 w3 F2 F0 y3 F1 V"
 
 SCRATCH = {
     "xin": ("sbuf", [128, 4 * C], "bfloat16"), "uin": ("sbuf", [128, 512], "bfloat16"), "vin": ("sbuf", [128, 512], "bfloat16"),
@@ -30,7 +29,7 @@ SCRATCH = {
     "pb": ("sbuf", [128, 8 * PS], "float32"),
     "sg": ("sbuf", [128, 5 * C], "bfloat16"), "keep": ("sbuf", [128, 5 * C], "bfloat16"), "key": ("sbuf", [128, 5 * C], "float16"),
     "cols": ("sbuf", [128, C], "bfloat16"), "low": ("sbuf", [128, C], "bfloat16"), "qb": ("sbuf", [128, 8 * PS], "float16"),
-    "lev": ("sbuf", [128, 8], "bfloat16"),
+    "lv": ("sbuf", [128, 40], "bfloat16"), "lev": ("sbuf", [128, 40], "bfloat16"), "dx": ("sbuf", [128, 4 * C], "bfloat16"),
     "nb": ("sbuf", [128, 32], "bfloat16"), "nt": ("sbuf", [128, 32], "bfloat16"), "nfo": ("sbuf", [128, 32], "float32"),
     "nd": ("sbuf", [128, 64], "bfloat16"), "ntt": ("sbuf", [128, 64], "bfloat16"), "lst2": ("sbuf", [128, 16], "uint16"),
     "ip": ("sbuf", [128, 2], "int32"), "t2": ("sbuf", [128, 2], "int32"), "i1": ("sbuf", [128, 2], "int32"), "i2": ("sbuf", [128, 2], "int32"),
@@ -47,8 +46,6 @@ for _r in range(3):
     for _q, _s in (("ue", "se"), ("uo", "so"), ("qz", "sz")):
         SCRATCH["%s%d" % (_q, _r)] = ("sbuf", [128, C], F8)
         SCRATCH["%s%d" % (_s, _r)] = ("sbuf", [128, C], "uint8")
-    SCRATCH["pk%d" % _r] = ("sbuf", [128, 256], F8)
-    SCRATCH["sk%d" % _r] = ("sbuf", [128, 256], "uint8")
     SCRATCH["qv%d" % _r] = ("sbuf", [128, 128], F8)
     SCRATCH["sv%d" % _r] = ("sbuf", [128, 128], "uint8")
     SCRATCH["land%d" % (_r + 1)] = ("sbuf", [128, 128], F8)
@@ -203,7 +200,7 @@ def rank_program(g, core, T, topo):
         lambda: row(0, 32, [[0, 2], [2, 8], [32, 2]], 0), lambda: row(32, 64, [[0, 2], [2, 8], [32, 2]], 1),
         lambda: row(64, 192, [[16, 2], [0, 4], [1, 16]], 0),
         lambda: row(192, 224, [[0, 16], [16, 2]], 16, 1), lambda: row(224, 256, [[0, 4], [32, 4], [0, 2]], 128, -1),
-        lambda: (row(256, 272, [[16, 2], [0, 4], [128, 2]], 0, 1), row(272, 288, [[16, 2], [0, 4], [128, 2]], 0, 1)),
+        lambda: row(256, 288, [[16, 2], [0, 8], [128, 2]], 0, 1),
         lambda: iota([R("cols")], T.cols[:], [[1, C]], -112),
         lambda: afill([R("keep0")], T.keep[:, 0:5 * C:5], C, 0.0), lambda: afill([R("keep1")], T.keep[:, 1:5 * C:5], C, 1.0),
         lambda: afill([R("keep2")], T.keep[:, 2:5 * C:5], C, 1.0), lambda: afill([R("keep3")], T.keep[:, 3:5 * C:5], C, 1.0),
@@ -226,6 +223,9 @@ def rank_program(g, core, T, topo):
         lambda: act([R("czt")], [R("col", 3, 4)], lambda: g.scalar.activation(T.col[:, 3:4], T.czt[:, 256:257], ACT.Copy, scale=0.25)),
         lambda: vec([R("i1")], [R("i2")], lambda: g.vector.tensor_scalar(T.i2[:, 0:1], T.i1[:, 0:1], 127, None, ALU.bitwise_and)),
         lambda: vec([R("i2"), R("col", 3, 4)], [R("off", 6, 7)], lambda: g.vector.tensor_scalar(T.off[:, 6:7], T.i2[:, 0:1], 2.0 ** -5, T.col[:, 3:4], ALU.mult, ALU.add)),
+        lambda: afill([R("lv4")], T.lv[:, 0:40:5], 8, 0.0),
+        lambda: quant("cf", "scf", 0, 128, "dd", 3, [R("dd")]), lambda: quant("cf", "scf", 128, 128, "dd", 2, [R("dd")]),
+        lambda: quant("cf", "scf", 256, 128, "dd", 1, [R("dd")]),
     ]
 
     SB = [6, 7]
@@ -234,7 +234,7 @@ def rank_program(g, core, T, topo):
     for r in range(3):
         X, SX, X1, SX1 = "qx%d" % r, "sx%d" % r, "qx%d" % (r + 1), "sx%d" % (r + 1)
         U, SU = ("qu", "squ") if r == 0 else ("land%d" % r, "lsc%d" % r)
-        ue, se, uo, so, qz, sz, pk, sk, qv, sv = [n + str(r) for n in ("ue", "se", "uo", "so", "qz", "sz", "pk", "sk", "qv", "sv")]
+        ue, se, uo, so, qz, sz, qv, sv = [n + str(r) for n in ("ue", "se", "uo", "so", "qz", "sz", "qv", "sv")]
 
         def tee(b, j):
             if r or b == 3:
@@ -258,9 +258,12 @@ def rank_program(g, core, T, topo):
         def ends(k):
             vec([R("ag")], [R("kt")], lambda: g.vector.transpose(T.kt[:], T.ag[:, 15:512:16]))
 
-        def twice(k):
-            vec([R("kt"), R("off", 0, 6), R("col", 2, 3)], [R("kd")],
-                lambda: g.vector.tensor_scalar(T.kd[:], T.kt[:, 0:32].indirect(T.off[:, 2:6]), -1.0, T.col[:, 2:3], ALU.mult, ALU.add))
+        def twice(q):
+            i, rd = T.kt[:, 0:32].indirect(T.off[:, 2:6]), [R("kt"), R("off", 0, 6), R("col", 2, 3)]
+            if q == "a":
+                act(rd, [R("kd")], lambda: g.scalar.activation(T.kd[:], i, ACT.Identity, bias=T.col[:, 2:3], scale=-1.0))
+            else:
+                vec(rd, [R("kd")], lambda: g.vector.tensor_scalar(T.kd[:], i, -1.0, T.col[:, 2:3], ALU.mult, ALU.add))
 
         def turn(o, nm):
             vec([R(nm)], [R(o)], lambda: g.vector.transpose(T[o][:], T[nm][:]))
@@ -303,20 +306,22 @@ def rank_program(g, core, T, topo):
             vec([R("key"), R("low") if k == 0 else R("qb", b, b + C)], [R("qb", o + 1, o + C + 1)],
                 lambda: g.vector.tensor_tensor_scan(T.qb[:, o + 1:o + C + 1], T.key[:, 4:5 * C:5], T.low[:] if k == 0 else T.qb[:, b:b + C], KEY, ALU.min, ALU.max))
 
+        def marks(j):
+            o = PS * (2 * j + 1) + C
+            act([R("pb")], [R("lv%d" % j)], lambda: g.scalar.activation(T.lv[:, j + 1:40:5], T.pb[:, C:8 * PS:PS], ACT.Sign, bias=T.pb[:, o:o + 1], scale=-1.0))
+
         def levels(k):
-            vec([R("qb")], [R("lev")], lambda: g.vector.tensor_scalar(T.lev[:], T.qb[:, C:8 * PS:PS], ROUND, -ROUND, ALU.add, ALU.add))
+            vec([R("lv%d" % j) for j in range(5)] + [R("keep%d" % j) for j in range(5)], [R("lev")],
+                lambda: g.vector.tensor_tensor_scan(T.lev[:], T.keep[:, 0:40], T.lv[:], 0.0, ALU.mult, ALU.add))
 
         def fractions(k):
-            vec([R("qb"), R("lev")], [R("nba")], lambda: g.vector.tensor_tensor(T.nb[:, 0:32:4], T.qb[:, C:8 * PS:PS], T.lev[:], ALU.subtract))
+            o, i, n, c, nm = ((0, 0, 128, 0, "nba"), (0, 64, 64, 2, "nbb0"), (64, 0, 64, 2, "nbb1"))[k]
+            vec([R("qb"), R("lev")], [R(nm)], lambda: g.vector.tensor_tensor(T.nb[o:o + n, c:32:4], T.qb[i:i + n, C:8 * PS:PS], T.lev[i:i + n, 4:40:5], ALU.subtract))
 
-        def spread(q, k):
-            if k < 2:
-                o, i = T.nb[64 * k:64 * k + 64, 2:32:4], T.nb[64 - 64 * k:128 - 64 * k, 0:32:4]
-                rd, wr = [R("nba")], [R("nbb%d" % k)]
-            else:
-                a, b = k - 2, (k - 1) % 4
-                o, i = T.nb[32 * a:32 * a + 32, 1:32:2], T.nb[32 * b:32 * b + 32, 0:32:2]
-                rd, wr = [R("nba"), R("nbb%d" % (b // 2))], [R("nbc%d" % a)]
+        def spread(q, a):
+            b = (a + 1) % 4
+            o, i = T.nb[32 * a:32 * a + 32, 1:32:2], T.nb[32 * b:32 * b + 32, 0:32:2]
+            rd, wr = [R("nba"), R("nbb%d" % (b // 2))], [R("nbc%d" % a)]
             if q == "a":
                 act(rd, wr, lambda: g.scalar.activation(o, i, ACT.Copy))
             else:
@@ -325,28 +330,30 @@ def rank_program(g, core, T, topo):
         def turn_along(k):
             vec([R("nba"), R("nbb0"), R("nbb1")] + [R("nbc%d" % a) for a in range(4)], [R("nt")], lambda: g.vector.transpose(T.nt[:], T.nb[:]))
 
-        def both(k):
-            vec([R("nt"), R("off", 0, 6)], [R("nd")], lambda: g.vector.tensor_copy(T.nd[:], T.nt[:, 0:32].indirect(T.off[:, 2:6])))
+        def both(q):
+            i = T.nt[:, 0:32].indirect(T.off[:, 2:6])
+            if q == "a":
+                act([R("nt"), R("off", 0, 6)], [R("nd")], lambda: g.scalar.activation(T.nd[:], i, ACT.Copy))
+            else:
+                vec([R("nt"), R("off", 0, 6)], [R("nd")], lambda: g.vector.tensor_copy(T.nd[:], i))
 
         def lists_along(k):
             vec([R("ntt"), R("off", 6, 7)], [R("lst2")],
                 lambda: g.vector.tensor_scalar(T.lst2[:], T.ntt[:, 0:64].indirect(T.off[:, 6:7]), 256.0, 112.0, ALU.mult, ALU.add))
 
-        def pick_x(e):
-            lo = 128 * e
-            vec([R(X1), R("lst2")], [R(pk, lo, lo + 128)],
-                lambda: g.vector.tensor_copy(T[pk][:, lo:lo + 128].bitcast(dt.uint32), T[X1][:].bitcast(dt.uint32).indirect(T.lst2[:, 8 * e:8 * e + 8])))
-
-        def pick_xs(e):
-            lo = 128 * e
-            act([R(SX1), R("lst2")], [R(sk, lo, lo + 128)],
-                lambda: g.scalar.activation(T[sk][:, lo:lo + 128], T[SX1][:].indirect(T.lst2[:, 8 * e:8 * e + 8]), ACT.Copy))
-
-        def cast(q, tile, b, j, n, scale):
+        def cast(q, tile, b, j, scale):
+            o = T.dx[:, C * b:C * b + C] if tile == "dx" else T[tile][:, b:4 * C:4]
             if q == "a":
-                act([R("bank%d" % j)], [R(tile + str(b))], lambda: g.scalar.activation(T[tile][:, b:4 * n:4], bank(j, n), ACT.Copy, scale=scale))
+                act([R("bank%d" % j)], [R(tile + str(b))], lambda: g.scalar.activation(o, bank(j, C), ACT.Copy, scale=scale))
             else:
-                vec([R("bank%d" % j)], [R(tile + str(b))], lambda: g.vector.tensor_scalar(T[tile][:, b:4 * n:4], bank(j, n), scale, None, ALU.mult))
+                vec([R("bank%d" % j)], [R(tile + str(b))], lambda: g.vector.tensor_scalar(o, bank(j, C), scale, None, ALU.mult))
+
+        def gather(q, b):
+            o, i = T.vt[:, b:512:4], T.dx[:, C * b:C * b + C].indirect(T.lst2[:, 0:8])
+            if q == "a":
+                act([R("dx%d" % b), R("lst2")], [R("vt%d" % b)], lambda: g.scalar.activation(o, i, ACT.Copy))
+            else:
+                vec([R("dx%d" % b), R("lst2")], [R("vt%d" % b)], lambda: g.vector.tensor_copy(o, i))
 
         def hand_on(k):
             quant(qv, sv, 0, 128, "vt", 0, [R("vt%d" % b) for b in range(4)])
@@ -368,28 +375,23 @@ def rank_program(g, core, T, topo):
             "M": lambda b: mm(b, C, "ce", "sce", 128 * b, ue, se, 0, False, False),
             "K": lambda b: mm(b, C, "cd", "scd", 128 * b, uo, so, 0, False, True),
             "W": lambda b: mm(RB[b], C, "wq", "wsc", 128 * b, qz, sz, 0, False, True),
-            "G": lambda b: mm(b, 128, "ce", "sce", 128 * b, pk, sk, 0, True, False),
-            "H": lambda b: mm(b, 128, "cd", "scd", 128 * b, pk, sk, 128, False, True),
-            "c": turn_scores, "a": highest, "b": records, "g": rows, "t": ends, "D": twice, "X": lambda k: turn("ktt", "kd"),
-            "L": lists_down, "E": pick_u, "e": pick_us,
-            "s": scan, "n": sign, "j": keys, "u": least, "f": levels, "h": fractions,
+            "A": lambda b: mm(b, C, "cf", "scf", 128 * b, X1, SX1, 0, True, True),
+            "c": turn_scores, "a": highest, "b": records, "g": rows, "t": ends, "X": lambda k: turn("ktt", "kd"),
+            "D": lambda k: twice("v"), "O": lambda k: twice("a"), "L": lists_down, "E": pick_u, "e": pick_us,
+            "s": scan, "n": sign, "j": keys, "u": least, "m": marks, "f": levels, "h": fractions,
             "i": lambda k: spread("v", k), "I": lambda k: spread("a", k), "N": turn_along,
-            "d": both, "x": lambda k: turn("ntt", "nd"), "l": lists_along, "P": pick_x, "p": pick_xs,
-            "Z": lambda b: cast("a", "zt", b, b, C, 2.0 ** -6), "z": lambda b: cast("v", "zt", b, b, C, 2.0 ** -6),
-            "R": lambda b: cast("a", "xt", b, RB[b], C, 2.0 ** -5), "r": lambda b: cast("v", "xt", b, RB[b], C, 2.0 ** -5),
-            "C": lambda b: cast("a", "vt", b, b, 128, 2.0 ** -5), "v": lambda b: cast("v", "vt", b, b, 128, 2.0 ** -5),
+            "d": lambda k: both("v"), "o": lambda k: both("a"), "x": lambda k: turn("ntt", "nd"), "l": lists_along,
+            "Z": lambda b: cast("a", "zt", b, b, 2.0 ** -6), "z": lambda b: cast("v", "zt", b, b, 2.0 ** -6),
+            "R": lambda b: cast("a", "xt", b, RB[b], 2.0 ** -5), "r": lambda b: cast("v", "xt", b, RB[b], 2.0 ** -5),
+            "J": lambda b: cast("a", "dx", b, b, 2.0 ** -5), "w": lambda b: cast("v", "dx", b, b, 2.0 ** -5),
+            "F": lambda b: gather("a", b), "y": lambda b: gather("v", b),
             "Q": lambda k: quant(qz, sz, 0, C, "zt", 0, [R("zt%d" % b) for b in range(4)]),
             "Y": lambda k: quant(X1, SX1, 0, C, "xt", 0, [R("xt%d" % b) for b in range(4)]),
             "V": hand_on,
         }
-        if r:
-            for b in range(4):
-                tee(b, b)
         for word in (SEQ if r else SEQ0).split():
             steps[word[0]](int(word[1:] or "0"))
         if r == 0:
-            for b in range(3):
-                quant("cf", "scf", 128 * b, 128, "dd", 3 - b, [R("dd")])
             quant("qvv", "sqvv", 0, 128, "vin", 0, [R("vin")])
     mm(YB, C, "qvv", "sqvv", 0, "qx3", "sx3", 0, True, True)
     act([R("bank%d" % YB)], [R("yb")], lambda: g.scalar.activation(T.yb[:], bank(YB, C), ACT.Copy))

@@ -2,14 +2,15 @@ from concourse.mybir import dt, AluOpType, ActivationFunctionType
 
 STEP = [4, 1, 2]
 C = 224
+H = C // 2
 BIG = 1.0e29
 KEY = 64.0
 PS = 232
 F8 = "float8_e4m3fn_x4"
 ALU = AluOpType
 ACT = ActivationFunctionType
-SEQ = "T0 T1 T2 T3 U0 U1 B0 c s0 a s1 b s2 g t O B1 s3 n1 X s4 L s5 E0 n3 s6 s7 e0 n5 e1 M3 M2 E1 M0 M1 K3 n7 j Z3 u0 K0 u1 Z0 K2 z2 u2 K1 Z1 Q m0 m3 u3 u4 u5 m1 u6 m2 U2 U3 f u7 W3 R3 W0 R0 W1 r1 h2 h0 W2 R2 h1 I2 I3 Y A0 i1 i0 N o A2 w0 J2 A1 J1 x l F0 A3 w3 y2 y3 F1 V"
-SEQ0 = "k0 k1 k2 k3 k4 k5 k6 k13 k14 k33 k17 k8 k7 k9 k22 k18 k16 k30 k10 k55 k27 k11 k48 k12 k36 k26 k28 k35 k15 k32 k23 k19 k38 k42 k43 k44 B0 k34 k24 k39 k40 U0 c k47 s0 B1 a k31 T2 s1 T0 T3 k25 b s2 n1 U1 k29 k21 k20 k54 g k45 s3 t k49 k46 O T1 n3 s4 s5 X k51 s6 L n5 s7 U3 E0 e0 M1 E1 n7 j k37 M2 e1 u0 m1 k41 u1 m0 m2 k57 u2 M0 k50 K1 Z1 u3 K2 K0 Z0 z2 M3 K3 Z3 u4 Q U2 u5 W3 m3 k56 W0 R3 W2 W1 u6 f u7 k52 R0 h0 h2 R2 h1 r1 i0 I2 I1 I3 Y N d A2 J2 k53 A0 J0 A1 x A3 l w1 w3 F2 F0 y3 F1 V"
+SEQ = "U0 U1 U2 U3 B0 s10 c s11 s20 G1 a s12 s21 b s13 s22 g s14 s23 H1 t1 t0 G0 H0 G2 G3 H3 s15 s24 X s16 s25 L s17 s26 H2 p2 s27 p1 p3 B1 n1 n3 n5 n7 p0 j1 j2 u10 m2 Q m0 m3 m1 u11 u20 u12 u21 u13 u22 W2 u14 u23 u15 u24 f u16 W0 u25 u17 u26 u27 R2 R0 W1 W3 R1 R3 Y A2 h0 h2 h1 i1 i3 I2 I0 N0 N1 x l J2 A1 A3 A0 w0 J1 J3 y2 F1 F3 y0 V"
+SEQ0 = "k0 k1 k2 k3 k5 k25 k21 k44 k17 k28 k13 k16 k33 k58 k48 k56 k23 k24 k55 k42 k43 k57 k30 k26 k19 k45 k46 k27 k54 B0 k31 P3 k47 s10 G1 G0 P1 c P2 B1 s11 s20 k49 k14 k15 a C3 s21 s12 b H1 k32 k29 C2 H0 C1 G3 P0 C0 s13 s22 U3 g G2 s14 s23 k20 t1 t0 H3 s15 n1 H2 n3 s24 X s16 s25 n5 L s17 s26 p1 s27 m2 n7 U0 m3 p3 p0 p2 U1 k18 j1 Q u10 U2 j2 u11 u20 W1 u12 k50 m1 m0 u21 f u13 k51 u22 u14 W3 W0 u23 u15 u24 u16 W2 u25 u17 u26 k52 u27 R3 R1 R2 R0 Y A2 h0 h2 h1 k53 I1 i2 A3 A0 I3 i0 N0 N1 x l A1 w1 J2 J3 J0 F3 y2 F0 y1 V"
 
 SCRATCH = {
     "xin": ("sbuf", [128, 4 * C], "bfloat16"), "uin": ("sbuf", [128, 512], "bfloat16"), "vin": ("sbuf", [128, 512], "bfloat16"),
@@ -17,25 +18,19 @@ SCRATCH = {
     "qu": ("sbuf", [128, 128], F8), "squ": ("sbuf", [128, 128], "uint8"),
     "qvv": ("sbuf", [128, 128], F8), "sqvv": ("sbuf", [128, 128], "uint8"),
     "c32": ("sbuf", [128, 256], "bfloat16"), "dd": ("sbuf", [128, 516], "bfloat16"),
-    "dde": ("sbuf", [128, 516], "bfloat16"), "ddo": ("sbuf", [128, 516], "bfloat16"),
     "cf": ("sbuf", [128, 512], F8), "scf": ("sbuf", [128, 512], "uint8"),
-    "ce": ("sbuf", [128, 512], F8), "sce": ("sbuf", [128, 512], "uint8"),
-    "cd": ("sbuf", [128, 512], F8), "scd": ("sbuf", [128, 512], "uint8"),
     "zt": ("sbuf", [128, 4 * C], "bfloat16"), "xt": ("sbuf", [128, 4 * C], "bfloat16"), "vt": ("sbuf", [128, 512], "bfloat16"),
+    "du": ("sbuf", [128, 512], "bfloat16"), "dx": ("sbuf", [128, 4 * C], "bfloat16"),
     "bigc": ("sbuf", [128, C], "float32"), "rst": ("sbuf", [128, C], "float32"), "down": ("sbuf", [128, C], "bfloat16"),
     "st": ("sbuf", [128, C], "float32"), "pa": ("sbuf", [128, PS], "float32"), "nr": ("sbuf", [128, C], "bfloat16"), "ag": ("sbuf", [128, 512], "bfloat16"),
-    "kt": ("sbuf", [128, 32], "bfloat16"), "kd": ("sbuf", [128, 64], "bfloat16"), "ktt": ("sbuf", [128, 64], "bfloat16"),
-    "lst": ("sbuf", [128, 32], "uint16"),
+    "kt": ("sbuf", [128, 64], "bfloat16"), "lst": ("sbuf", [128, 16], "uint16"), "kfo": ("sbuf", [128, 32], "float32"),
     "pb": ("sbuf", [128, 8 * PS], "float32"),
     "sg": ("sbuf", [128, 5 * C], "bfloat16"), "keep": ("sbuf", [128, 5 * C], "bfloat16"), "key": ("sbuf", [128, 5 * C], "float16"),
-    "cols": ("sbuf", [128, C], "bfloat16"), "low": ("sbuf", [128, C], "bfloat16"), "qb": ("sbuf", [128, 8 * PS], "float16"),
-    "lv": ("sbuf", [128, 40], "bfloat16"), "lev": ("sbuf", [128, 40], "bfloat16"), "dx": ("sbuf", [128, 4 * C], "bfloat16"),
-    "nb": ("sbuf", [128, 32], "bfloat16"), "nt": ("sbuf", [128, 32], "bfloat16"), "nfo": ("sbuf", [128, 32], "float32"),
-    "nd": ("sbuf", [128, 64], "bfloat16"), "ntt": ("sbuf", [128, 64], "bfloat16"), "lst2": ("sbuf", [128, 16], "uint16"),
-    "ip": ("sbuf", [128, 2], "int32"), "t2": ("sbuf", [128, 2], "int32"), "i1": ("sbuf", [128, 2], "int32"), "i2": ("sbuf", [128, 2], "int32"),
-    "col": ("sbuf", [128, 8], "float32"),
-    "cz": ("sbuf", [128, 288], "bfloat16"), "czt": ("sbuf", [128, 288], "bfloat16"), "off": ("sbuf", [128, 8], "uint16"),
-    "kfo": ("sbuf", [128, 32], "float32"),
+    "cols": ("sbuf", [128, C], "bfloat16"), "low": ("sbuf", [128, C], "bfloat16"), "qb": ("sbuf", [128, 9 * PS], "float16"),
+    "lv": ("sbuf", [128, 40], "bfloat16"), "lev": ("sbuf", [128, 40], "bfloat16"),
+    "nb": ("sbuf", [128, 64], "bfloat16"), "nt": ("sbuf", [128, 64], "bfloat16"), "lst2": ("sbuf", [128, 16], "uint16"), "nfo": ("sbuf", [128, 32], "float32"),
+    "i1": ("sbuf", [128, 2], "int32"), "i2": ("sbuf", [128, 2], "int32"), "col": ("sbuf", [128, 4], "float32"),
+    "cz": ("sbuf", [128, 160], "bfloat16"), "czt": ("sbuf", [128, 160], "bfloat16"), "off": ("sbuf", [128, 4], "uint16"),
     "yb": ("sbuf", [128, C], "float32"),
     "ps": ("psum", [128, 4096], "float32"),
 }
@@ -43,9 +38,8 @@ for _r in range(4):
     SCRATCH["qx%d" % _r] = ("sbuf", [128, C], F8)
     SCRATCH["sx%d" % _r] = ("sbuf", [128, C], "uint8")
 for _r in range(3):
-    for _q, _s in (("ue", "se"), ("uo", "so"), ("qz", "sz")):
-        SCRATCH["%s%d" % (_q, _r)] = ("sbuf", [128, C], F8)
-        SCRATCH["%s%d" % (_s, _r)] = ("sbuf", [128, C], "uint8")
+    SCRATCH["qz%d" % _r] = ("sbuf", [128, C], F8)
+    SCRATCH["sz%d" % _r] = ("sbuf", [128, C], "uint8")
     SCRATCH["qv%d" % _r] = ("sbuf", [128, 128], F8)
     SCRATCH["sv%d" % _r] = ("sbuf", [128, 128], "uint8")
     SCRATCH["land%d" % (_r + 1)] = ("sbuf", [128, 128], F8)
@@ -160,11 +154,11 @@ def rank_program(g, core, T, topo):
     def quant(q, s, lo, n, tile, tlo, names):
         vec(names, [R(q, lo, lo + n), R(s, lo, lo + n)], lambda: g.vector.quantize_mx(T[q][:, lo:lo + n], T[s][:, lo:lo + n], T[tile][:, tlo:tlo + 4 * n]))
 
-    def half(nm, j):
-        vec([R("dd"), R("col", j, j + 1)], [R(nm)], lambda: g.vector.tensor_scalar(T[nm][:, 3:515:4], T.dd[:, 3:515:4], T.col[:, j:j + 1], None, ALU.mult))
-
-    def column(j, sc, b):
-        vec([R("t2")], [R("col", j, j + 1)], lambda: g.vector.tensor_scalar(T.col[:, j:j + 1], T.t2[:, 0:1], sc, b, ALU.mult, ALU.add))
+    def scaled(q, reads, writes, o, i, scale):
+        if q == "a":
+            act(reads, writes, lambda: g.scalar.activation(o, i, ACT.Copy, scale=scale))
+        else:
+            vec(reads, writes, lambda: g.vector.tensor_scalar(o, i, scale, None, ALU.mult))
 
     def later_loads():
         need("s", deps("s", [R("xin")], []))
@@ -175,73 +169,62 @@ def rank_program(g, core, T, topo):
     def row(lo, hi, pat, base, step=0):
         iota([R("cz", lo, hi)], T.cz[:, lo:hi], pat, base, step)
 
-    first = [
-        lambda: dmas("ldx", [("s", [], [R("xin")], T.xin[:], T.x[:])]),
-        lambda: dmas("ldu", [("a", [], [R("uin")], T.uin[:], T.u[:])]),
-        lambda: fill([R("c32")], T.c32[:], 32.0),
-        lambda: fill([R("dd")], T.dd[:], 0.0),
-        lambda: run("g", [], [R("ip")], lambda: g.iota(T.ip[:, 0:1], [[0, 1]], 0, 1)),
-        lambda: run("g", [R("c32")], [R("dd")], lambda: g.affine_select(T.dd[:, 3:515:4], T.c32[:, 0:128], [[1, 128]], ALU.is_equal, 0.0, 0, -1)),
-        lambda: fill([R("dde")], T.dde[:], 0.0),
-        lambda: fill([R("ddo")], T.ddo[:], 0.0),
-        lambda: vec([R("ip")], [R("t2")], lambda: g.vector.tensor_scalar(T.t2[:, 0:1], T.ip[:, 0:1], 16, None, ALU.bitwise_and)),
-        lambda: column(0, -0.0625, 1.0),
-        lambda: column(1, 0.0625, 0.0),
-        lambda: half("dde", 0),
-        lambda: half("ddo", 1),
-        lambda: afill([R("rst")], T.rst[:], C, BIG),
-        lambda: afill([R("pa", 0, 1)], T.pa[:, 0:1], 1, -BIG),
-        lambda: afill([R("rst")], T.rst[:, 0:C:16], C // 16, -BIG),
-        lambda: afill([R("bigc")], T.bigc[:], C, BIG),
-        lambda: afill([R("pb", PS * k, PS * k + 1) for k in range(8)], T.pb[:, 0:8 * PS:PS], 8, -BIG),
-        lambda: afill([R("low")], T.low[:], C, -KEY),
-        lambda: iota([R("down")], T.down[:], [[0, C // 16], [-1, 16]], 16),
-        lambda: iota([R("ag", C, 512)], T.ag[:, C:512], [[0, 512 - C]], 1),
-        lambda: row(0, 32, [[0, 2], [2, 8], [32, 2]], 0), lambda: row(32, 64, [[0, 2], [2, 8], [32, 2]], 1),
-        lambda: row(64, 192, [[16, 2], [0, 4], [1, 16]], 0),
-        lambda: row(192, 224, [[0, 16], [16, 2]], 16, 1), lambda: row(224, 256, [[0, 4], [32, 4], [0, 2]], 128, -1),
-        lambda: row(256, 288, [[16, 2], [0, 8], [128, 2]], 0, 1),
-        lambda: iota([R("cols")], T.cols[:], [[1, C]], -112),
-        lambda: afill([R("keep0")], T.keep[:, 0:5 * C:5], C, 0.0), lambda: afill([R("keep1")], T.keep[:, 1:5 * C:5], C, 1.0),
-        lambda: afill([R("keep2")], T.keep[:, 2:5 * C:5], C, 1.0), lambda: afill([R("keep3")], T.keep[:, 3:5 * C:5], C, 1.0),
-        lambda: act([R("cols")], [R("sg0")], lambda: g.scalar.activation(T.sg[:, 0:5 * C:5], T.cols[:], ACT.Copy, scale=2.0 ** -8)),
-        lambda: vec([R("c32")], [R("qb", PS * k, PS * k + 1) for k in range(8)],
-                    lambda: g.vector.tensor_scalar(T.qb[:, 0:8 * PS:PS], T.c32[:, 0:8], KEY / 32.0, None, ALU.mult)),
-        lambda: quant("ce", "sce", 0, 128, "dde", 3, [R("dde")]), lambda: quant("ce", "sce", 128, 128, "dde", 2, [R("dde")]),
-        lambda: quant("ce", "sce", 256, 128, "dde", 1, [R("dde")]), lambda: quant("ce", "sce", 384, 128, "dde", 0, [R("dde")]),
-        lambda: quant("cd", "scd", 0, 128, "ddo", 3, [R("ddo")]), lambda: quant("cd", "scd", 128, 128, "ddo", 2, [R("ddo")]),
-        lambda: quant("cd", "scd", 256, 128, "ddo", 1, [R("ddo")]), lambda: quant("cd", "scd", 384, 128, "ddo", 0, [R("ddo")]),
-        lambda: quant("qu", "squ", 0, 128, "uin", 0, [R("uin")]),
-        lambda: quant("qx0", "sx0", 0, C, "xin", 0, [R("xin")]),
-        later_loads,
-        lambda: vec([R("cz")], [R("czt")], lambda: g.vector.transpose(T.czt[:], T.cz[:])),
-        lambda: vec([R("czt")], [R("off", 0, 6)], lambda: g.vector.tensor_copy(T.off[:, 0:6], T.czt[:, 0:192:32])),
-        lambda: afill([R("keep4")], T.keep[:, 4:5 * C:5], C, 1.0),
-        lambda: quant("cf", "scf", 384, 128, "dd", 0, [R("dd")]),
-        lambda: act([R("czt")], [R("col", 2, 3)], lambda: g.scalar.activation(T.col[:, 2:3], T.czt[:, 192:193], ACT.Copy)),
-        lambda: vec([R("czt")], [R("i1")], lambda: g.vector.tensor_copy(T.i1[:, 0:1], T.czt[:, 224:225])),
-        lambda: act([R("czt")], [R("col", 3, 4)], lambda: g.scalar.activation(T.col[:, 3:4], T.czt[:, 256:257], ACT.Copy, scale=0.25)),
-        lambda: vec([R("i1")], [R("i2")], lambda: g.vector.tensor_scalar(T.i2[:, 0:1], T.i1[:, 0:1], 127, None, ALU.bitwise_and)),
-        lambda: vec([R("i2"), R("col", 3, 4)], [R("off", 6, 7)], lambda: g.vector.tensor_scalar(T.off[:, 6:7], T.i2[:, 0:1], 2.0 ** -5, T.col[:, 3:4], ALU.mult, ALU.add)),
-        lambda: afill([R("lv4")], T.lv[:, 0:40:5], 8, 0.0),
-        lambda: quant("cf", "scf", 0, 128, "dd", 3, [R("dd")]), lambda: quant("cf", "scf", 128, 128, "dd", 2, [R("dd")]),
-        lambda: quant("cf", "scf", 256, 128, "dd", 1, [R("dd")]),
-    ]
+    def order():
+        for x in range(2):
+            for h in range(2):
+                lo = 16 * x + h
+                iota([R("cz%d" % lo)], T.cz[:, lo:lo + 15:2], [[32 if h == x else 2, 8]], 16 * x + 15 if h == x else C + x)
+
+    def keeps(j):
+        afill([R("keep%d" % j)], T.keep[:, j:5 * C:5], C, 1.0 if j else 0.0)
+
+    def unpacker(b):
+        quant("cf", "scf", 128 * b, 128, "dd", 3 - b, [R("dd")])
+
+    first = {
+        0: lambda: dmas("ldx", [("s", [], [R("xin")], T.xin[:], T.x[:])]),
+        1: lambda: dmas("ldu", [("a", [], [R("uin")], T.uin[:], T.u[:])]),
+        44: later_loads,
+        42: lambda: quant("qu", "squ", 0, 128, "uin", 0, [R("uin")]),
+        43: lambda: quant("qx0", "sx0", 0, C, "xin", 0, [R("xin")]),
+        2: lambda: fill([R("c32")], T.c32[:], 32.0),
+        3: lambda: fill([R("dd")], T.dd[:], 0.0),
+        5: lambda: run("g", [R("c32")], [R("dd")], lambda: g.affine_select(T.dd[:, 3:515:4], T.c32[:, 0:128], [[1, 128]], ALU.is_equal, 0.0, 0, -1)),
+        55: lambda: unpacker(0), 56: lambda: unpacker(1), 57: lambda: unpacker(2), 48: lambda: unpacker(3),
+        13: lambda: afill([R("rst")], T.rst[:], C, BIG),
+        15: lambda: afill([R("rst")], T.rst[:, 0:C:16], C // 16, -BIG),
+        14: lambda: afill([R("pa", 0, 1)], T.pa[:, 0:1], 1, -BIG),
+        19: lambda: iota([R("down")], T.down[:], [[0, C // 16], [-1, 16]], 16),
+        20: lambda: iota([R("ag", C, 512)], T.ag[:, C:512], [[0, 512 - C]], 1),
+        16: lambda: afill([R("bigc")], T.bigc[:], C, BIG),
+        17: lambda: afill([R("pb", PS * k, PS * k + 1) for k in range(8)], T.pb[:, 0:8 * PS:PS], 8, -BIG),
+        27: lambda: iota([R("cols")], T.cols[:], [[1, C]], -H),
+        32: lambda: scaled("a", [R("cols")], [R("sg0")], T.sg[:, 0:5 * C:5], T.cols[:], 2.0 ** -8),
+        28: lambda: keeps(0), 29: lambda: keeps(1), 30: lambda: keeps(2), 31: lambda: keeps(3), 47: lambda: keeps(4),
+        54: lambda: afill([R("lv4")], T.lv[:, 0:40:5], 8, 0.0),
+        18: lambda: afill([R("low")], T.low[:], C, -KEY),
+        33: lambda: scaled("v", [R("c32")], [R("qb", PS * k, PS * k + 1) for k in range(8)], T.qb[:, 0:8 * PS:PS], T.c32[:, 0:8], KEY / 32.0),
+        58: lambda: scaled("v", [R("c32")], [R("qb", H + 1, C + 2)], T.qb[:, H + 1:C + 2], T.c32[:, 0:H + 1], -KEY / 32.0),
+        21: order,
+        23: lambda: row(32, 64, [[16, 2], [0, 16]], 16, 1),
+        24: lambda: row(64, 96, [[0, 16], [16, 2]], 16, 1),
+        25: lambda: row(96, 128, [[0, 4], [32, 4], [0, 2]], 128, -1),
+        26: lambda: (row(128, 144, [[0, 8], [128, 2]], 0, 1), row(144, 160, [[0, 8], [-128, 2]], 144, 1)),
+        45: lambda: vec([R("cz"), R("cz0"), R("cz1"), R("cz16"), R("cz17")], [R("czt")], lambda: g.vector.transpose(T.czt[:], T.cz[:])),
+        46: lambda: vec([R("czt")], [R("off", 0, 1)], lambda: g.vector.tensor_copy(T.off[:, 0:1], T.czt[:, 0:1])),
+        49: lambda: scaled("a", [R("czt")], [R("col", 0, 2)], T.col[:, 0:2], T.czt[:, 32:96:32], 1.0),
+        50: lambda: vec([R("czt")], [R("i1")], lambda: g.vector.tensor_copy(T.i1[:, 0:1], T.czt[:, 96:97])),
+        51: lambda: scaled("a", [R("czt")], [R("col", 2, 3)], T.col[:, 2:3], T.czt[:, 128:129], 0.25),
+        52: lambda: vec([R("i1")], [R("i2")], lambda: g.vector.tensor_scalar(T.i2[:, 0:1], T.i1[:, 0:1], 127, None, ALU.bitwise_and)),
+        53: lambda: vec([R("i2"), R("col", 2, 3)], [R("off", 2, 3)], lambda: g.vector.tensor_scalar(T.off[:, 2:3], T.i2[:, 0:1], 2.0 ** -5, T.col[:, 2:3], ALU.mult, ALU.add)),
+    }
 
     SB = [6, 7]
-    RB = [4, 5, 7, 6]
-    YB = 4
+    AB = [4, 5, 7, 6]
     for r in range(3):
         X, SX, X1, SX1 = "qx%d" % r, "sx%d" % r, "qx%d" % (r + 1), "sx%d" % (r + 1)
         U, SU = ("qu", "squ") if r == 0 else ("land%d" % r, "lsc%d" % r)
-        ue, se, uo, so, qz, sz, qv, sv = [n + str(r) for n in ("ue", "se", "uo", "so", "qz", "sz", "qv", "sv")]
-
-        def tee(b, j):
-            if r or b == 3:
-                mm(j, C, "cf", "scf", 128 * b, X, SX, 0, True, False)
-            else:
-                mm(j, C, "ce", "sce", 128 * b, X, SX, 0, True, False)
-                mm(j, C, "cd", "scd", 128 * b, X, SX, 0, False, False)
+        qz, sz, qv, sv = [n + str(r) for n in ("qz", "sz", "qv", "sv")]
 
         def turn_scores(k):
             vec([R("bank%d" % SB[0])], [R("st")], lambda: g.vector.transpose(T.st[:], bank(SB[0], C)))
@@ -256,32 +239,21 @@ def rank_program(g, core, T, topo):
             vec([R("nr"), R("down")], [R("ag", 0, C)], lambda: g.vector.tensor_tensor_scan(T.ag[:, 0:C], T.nr[:], T.down[:], 0.0, ALU.mult, ALU.max))
 
         def ends(k):
-            vec([R("ag")], [R("kt")], lambda: g.vector.transpose(T.kt[:], T.ag[:, 15:512:16]))
+            vec([R("ag")], [R("kt", 32 * k, 32 * k + 32)], lambda: g.vector.transpose(T.kt[:, 32 * k:32 * k + 32], T.ag[:, 15:512:16]))
 
-        def twice(q):
-            i, rd = T.kt[:, 0:32].indirect(T.off[:, 2:6]), [R("kt"), R("off", 0, 6), R("col", 2, 3)]
-            if q == "a":
-                act(rd, [R("kd")], lambda: g.scalar.activation(T.kd[:], i, ACT.Identity, bias=T.col[:, 2:3], scale=-1.0))
-            else:
-                vec(rd, [R("kd")], lambda: g.vector.tensor_scalar(T.kd[:], i, -1.0, T.col[:, 2:3], ALU.mult, ALU.add))
-
-        def turn(o, nm):
-            vec([R(nm)], [R(o)], lambda: g.vector.transpose(T[o][:], T[nm][:]))
+        def exchange_down(k):
+            vec([R("kt")], [R("ag", C, 256)], lambda: g.vector.transpose(T.ag[:, C:256], T.kt[:, 16:48]))
 
         def lists_down(k):
-            vec([R("ktt"), R("off", 0, 6)], [R("lst")], lambda: g.vector.tensor_copy(T.lst[:], T.ktt[:, 0:64].indirect(T.off[:, 0:2])))
+            vec([R("ag", 0, 256), R("off", 0, 1), R("col", 0, 2)], [R("lst")],
+                lambda: g.vector.tensor_scalar(T.lst[:], T.ag[:, 0:256].indirect(T.off[:, 0:1]), -1.0, T.col[:, 0:1], ALU.mult, ALU.add))
 
-        def pick_u(e):
-            q = (ue, uo)[e]
-            vec([R(U), R("lst")], [R(q)],
-                lambda: g.vector.tensor_copy(T[q][:].bitcast(dt.uint32), T[U][:].bitcast(dt.uint32).indirect(T.lst[:, 16 * e:16 * e + 14])))
-
-        def pick_us(e):
-            s = (se, so)[e]
-            act([R(SU), R("lst")], [R(s)], lambda: g.scalar.activation(T[s][:], T[SU][:].indirect(T.lst[:, 16 * e:16 * e + 14]), ACT.Copy))
+        def zed(b):
+            vec([R("du%d" % b), R("dx%d" % b), R("lst")], [R("zt%d" % b)],
+                lambda: g.vector.tensor_tensor(T.zt[:, b:4 * C:4], T.du[:, 128 * b:128 * b + 128].indirect(T.lst[:, 0:14]), T.dx[:, C * b:C * b + C], ALU.add))
 
         def scan(k):
-            lo, hi = ((0, C), (0, C // 2), (C // 2, C))[k // 10]
+            lo, hi = ((0, C), (0, H), (H, C))[k // 10]
             k %= 10
             o = PS * k + lo
             n = hi - lo
@@ -297,14 +269,18 @@ def rank_program(g, core, T, topo):
                 lambda: g.scalar.activation(T.sg[:, j:5 * C:5], bank(SB[1], C), ACT.Sign, bias=T.pb[:, o:o + 1], scale=-1.0))
 
         def keys(k):
-            vec([R("keep%d" % j) for j in range(5)] + [R("sg%d" % j) for j in range(5)], [R("key")],
-                lambda: g.vector.tensor_tensor_scan(T.key[:], T.keep[:], T.sg[:], 0.0, ALU.mult, ALU.add))
+            lo = 5 * H * (k - 1)
+            vec([R("keep%d" % j) for j in range(5)] + [R("sg%d" % j) for j in range(5)], [R("key%d" % k)],
+                lambda: g.vector.tensor_tensor_scan(T.key[:, lo:lo + 5 * H], T.keep[:, lo:lo + 5 * H], T.sg[:, lo:lo + 5 * H], 0.0, ALU.mult, ALU.add))
 
         def least(k):
-            o = PS * k
-            b = o - PS
-            vec([R("key"), R("low") if k == 0 else R("qb", b, b + C)], [R("qb", o + 1, o + C + 1)],
-                lambda: g.vector.tensor_tensor_scan(T.qb[:, o + 1:o + C + 1], T.key[:, 4:5 * C:5], T.low[:] if k == 0 else T.qb[:, b:b + C], KEY, ALU.min, ALU.max))
+            o = PS * (k % 10)
+            if k < 20:
+                vec([R("key1"), R("low") if o == 0 else R("qb", o - PS, o - PS + H)], [R("qb", o + 1, o + H + 1)],
+                    lambda: g.vector.tensor_tensor_scan(T.qb[:, o + 1:o + H + 1], T.key[:, 4:5 * H:5], T.low[:, 0:H] if o == 0 else T.qb[:, o - PS:o - PS + H], KEY, ALU.min, ALU.max))
+            else:
+                vec([R("key1"), R("key2"), R("qb", o + H, o + C + 1)], [R("qb", o + PS + H + 1, o + PS + C + 2)],
+                    lambda: g.vector.tensor_tensor_scan(T.qb[:, o + PS + H + 1:o + PS + C + 2], T.key[:, 5 * H - 1:5 * C:5], T.qb[:, o + H:o + C + 1], -KEY, ALU.min, ALU.max))
 
         def marks(j):
             o = PS * (2 * j + 1) + C
@@ -316,44 +292,32 @@ def rank_program(g, core, T, topo):
 
         def fractions(k):
             o, i, n, c, nm = ((0, 0, 128, 0, "nba"), (0, 64, 64, 2, "nbb0"), (64, 0, 64, 2, "nbb1"))[k]
-            vec([R("qb"), R("lev")], [R(nm)], lambda: g.vector.tensor_tensor(T.nb[o:o + n, c:32:4], T.qb[i:i + n, C:8 * PS:PS], T.lev[i:i + n, 4:40:5], ALU.subtract))
+            vec([R("qb"), R("lev")], [R(nm)], lambda: g.vector.tensor_tensor(T.nb[o:o + n, c:32:4], T.qb[i:i + n, PS + C + 1:9 * PS:PS], T.lev[i:i + n, 4:40:5], ALU.subtract))
 
         def spread(q, a):
             b = (a + 1) % 4
-            o, i = T.nb[32 * a:32 * a + 32, 1:32:2], T.nb[32 * b:32 * b + 32, 0:32:2]
-            rd, wr = [R("nba"), R("nbb%d" % (b // 2))], [R("nbc%d" % a)]
-            if q == "a":
-                act(rd, wr, lambda: g.scalar.activation(o, i, ACT.Copy))
-            else:
-                vec(rd, wr, lambda: g.vector.tensor_copy(o, i))
+            scaled(q, [R("nba"), R("nbb%d" % (b // 2))], [R("nbc%d" % a)], T.nb[32 * a:32 * a + 32, 1:32:2], T.nb[32 * b:32 * b + 32, 0:32:2], 1.0)
+
+        spreads = [R("nba"), R("nbb0"), R("nbb1")] + [R("nbc%d" % a) for a in range(4)]
 
         def turn_along(k):
-            vec([R("nba"), R("nbb0"), R("nbb1")] + [R("nbc%d" % a) for a in range(4)], [R("nt")], lambda: g.vector.transpose(T.nt[:], T.nb[:]))
+            vec(spreads, [R("nt", 32 * k, 32 * k + 32)], lambda: g.vector.transpose(T.nt[:, 32 * k:32 * k + 32], T.nb[:, 0:32]))
 
-        def both(q):
-            i = T.nt[:, 0:32].indirect(T.off[:, 2:6])
-            if q == "a":
-                act([R("nt"), R("off", 0, 6)], [R("nd")], lambda: g.scalar.activation(T.nd[:], i, ACT.Copy))
-            else:
-                vec([R("nt"), R("off", 0, 6)], [R("nd")], lambda: g.vector.tensor_copy(T.nd[:], i))
+        def exchange_along(k):
+            vec([R("nt")], [R("nbd")], lambda: g.vector.transpose(T.nb[:, 32:64], T.nt[:, 16:48]))
 
         def lists_along(k):
-            vec([R("ntt"), R("off", 6, 7)], [R("lst2")],
-                lambda: g.vector.tensor_scalar(T.lst2[:], T.ntt[:, 0:64].indirect(T.off[:, 6:7]), 256.0, 112.0, ALU.mult, ALU.add))
+            vec(spreads + [R("nbd"), R("off", 2, 3)], [R("lst2")],
+                lambda: g.vector.tensor_scalar(T.lst2[:], T.nb[:, 0:64].indirect(T.off[:, 2:3]), 256.0, float(H), ALU.mult, ALU.add))
 
-        def cast(q, tile, b, j, scale):
-            o = T.dx[:, C * b:C * b + C] if tile == "dx" else T[tile][:, b:4 * C:4]
-            if q == "a":
-                act([R("bank%d" % j)], [R(tile + str(b))], lambda: g.scalar.activation(o, bank(j, C), ACT.Copy, scale=scale))
-            else:
-                vec([R("bank%d" % j)], [R(tile + str(b))], lambda: g.vector.tensor_scalar(o, bank(j, C), scale, None, ALU.mult))
+        def state(q, b):
+            scaled(q, [R("bank%d" % b)], [R("xt%d" % b)], T.xt[:, b:4 * C:4], bank(b, C), 2.0 ** -5)
+
+        def plane(q, nm, n, b, j):
+            scaled(q, [R("bank%d" % j)], [R(nm + str(b))], T[nm][:, n * b:n * b + n], bank(j, n), 2.0 ** -6)
 
         def gather(q, b):
-            o, i = T.vt[:, b:512:4], T.dx[:, C * b:C * b + C].indirect(T.lst2[:, 0:8])
-            if q == "a":
-                act([R("dx%d" % b), R("lst2")], [R("vt%d" % b)], lambda: g.scalar.activation(o, i, ACT.Copy))
-            else:
-                vec([R("dx%d" % b), R("lst2")], [R("vt%d" % b)], lambda: g.vector.tensor_copy(o, i))
+            scaled(q, [R("dx%d" % b), R("lst2")], [R("vt%d" % b)], T.vt[:, b:512:4], T.dx[:, C * b:C * b + C].indirect(T.lst2[:, 0:8]), 2.0)
 
         def hand_on(k):
             quant(qv, sv, 0, 128, "vt", 0, [R("vt%d" % b) for b in range(4)])
@@ -371,19 +335,18 @@ def rank_program(g, core, T, topo):
         steps = {
             "k": lambda k: first[k](),
             "B": lambda j: mm(SB[j], C, U, SU, 0, X, SX, 0, True, True),
-            "T": lambda b: tee(b, b), "U": lambda b: tee(b, RB[b]),
-            "M": lambda b: mm(b, C, "ce", "sce", 128 * b, ue, se, 0, False, False),
-            "K": lambda b: mm(b, C, "cd", "scd", 128 * b, uo, so, 0, False, True),
-            "W": lambda b: mm(RB[b], C, "wq", "wsc", 128 * b, qz, sz, 0, False, True),
-            "A": lambda b: mm(b, C, "cf", "scf", 128 * b, X1, SX1, 0, True, True),
-            "c": turn_scores, "a": highest, "b": records, "g": rows, "t": ends, "X": lambda k: turn("ktt", "kd"),
-            "D": lambda k: twice("v"), "O": lambda k: twice("a"), "L": lists_down, "E": pick_u, "e": pick_us,
+            "U": lambda b: mm(b, C, "cf", "scf", 128 * b, X, SX, 0, True, False),
+            "W": lambda b: mm(b, C, "wq", "wsc", 128 * b, qz, sz, 0, False, True),
+            "G": lambda b: mm(4 + b % 2, 128, "cf", "scf", 128 * b, U, SU, 0, True, True),
+            "H": lambda b: plane("a", "du", 128, b, 4 + b % 2), "q": lambda b: plane("v", "du", 128, b, 4 + b % 2),
+            "P": lambda b: mm(b, C, "cf", "scf", 128 * b, X, SX, 0, True, True),
+            "C": lambda b: plane("a", "dx", C, b, b), "v": lambda b: plane("v", "dx", C, b, b),
+            "A": lambda b: mm(AB[b], C, "cf", "scf", 128 * b, X1, SX1, 0, True, True),
+            "J": lambda b: plane("a", "dx", C, b, AB[b]), "w": lambda b: plane("v", "dx", C, b, AB[b]),
+            "c": turn_scores, "a": highest, "b": records, "g": rows, "t": ends, "X": exchange_down, "L": lists_down, "p": zed,
             "s": scan, "n": sign, "j": keys, "u": least, "m": marks, "f": levels, "h": fractions,
-            "i": lambda k: spread("v", k), "I": lambda k: spread("a", k), "N": turn_along,
-            "d": lambda k: both("v"), "o": lambda k: both("a"), "x": lambda k: turn("ntt", "nd"), "l": lists_along,
-            "Z": lambda b: cast("a", "zt", b, b, 2.0 ** -6), "z": lambda b: cast("v", "zt", b, b, 2.0 ** -6),
-            "R": lambda b: cast("a", "xt", b, RB[b], 2.0 ** -5), "r": lambda b: cast("v", "xt", b, RB[b], 2.0 ** -5),
-            "J": lambda b: cast("a", "dx", b, b, 2.0 ** -5), "w": lambda b: cast("v", "dx", b, b, 2.0 ** -5),
+            "i": lambda k: spread("v", k), "I": lambda k: spread("a", k), "N": turn_along, "x": exchange_along, "l": lists_along,
+            "R": lambda b: state("a", b), "r": lambda b: state("v", b),
             "F": lambda b: gather("a", b), "y": lambda b: gather("v", b),
             "Q": lambda k: quant(qz, sz, 0, C, "zt", 0, [R("zt%d" % b) for b in range(4)]),
             "Y": lambda k: quant(X1, SX1, 0, C, "xt", 0, [R("xt%d" % b) for b in range(4)]),
@@ -393,10 +356,10 @@ def rank_program(g, core, T, topo):
             steps[word[0]](int(word[1:] or "0"))
         if r == 0:
             quant("qvv", "sqvv", 0, 128, "vin", 0, [R("vin")])
-    mm(YB, C, "qvv", "sqvv", 0, "qx3", "sx3", 0, True, True)
-    act([R("bank%d" % YB)], [R("yb")], lambda: g.scalar.activation(T.yb[:], bank(YB, C), ACT.Copy))
-    vec([R("nt")], [R("nfo")], lambda: g.vector.tensor_scalar(T.nfo[:], T.nt[:], 256.0, 112.0, ALU.mult, ALU.add))
-    vec([R("kt"), R("col", 2, 3)], [R("kfo")], lambda: g.vector.tensor_scalar(T.kfo[:], T.kt[:], -1.0, T.col[:, 2:3], ALU.mult, ALU.add))
+    mm(0, C, "qvv", "sqvv", 0, "qx3", "sx3", 0, True, True)
+    act([R("bank0")], [R("yb")], lambda: g.scalar.activation(T.yb[:], bank(0, C), ACT.Copy))
+    vec([R("nt")], [R("nfo")], lambda: g.vector.tensor_scalar(T.nfo[:], T.nt[:, 0:32], 256.0, float(H), ALU.mult, ALU.add))
+    vec([R("kt"), R("col", 0, 2)], [R("kfo")], lambda: g.vector.tensor_scalar(T.kfo[:], T.kt[:, 0:32], -1.0, T.col[:, 1:2], ALU.mult, ALU.add))
     jobs = [("s", [R("qx3")], [], T.oc[:], T.qx3[:].bitcast(dt.uint8))]
     jobs += [("s", [R("sx3")], [], T.osc[4 * k:4 * k + 4, :], T.sx3[32 * k:32 * k + 4, :]) for k in range(4)]
     jobs.append(("a", [R("yb")], [], T.y[:], T.yb[:]))

@@ -9,8 +9,9 @@ PS = 232
 F8 = "float8_e4m3fn_x4"
 ALU = AluOpType
 ACT = ActivationFunctionType
-SEQ = "U0 U1 U2 U3 B0 s10 c s11 s20 G1 a s12 s21 b s13 s22 g s14 s23 H1 t1 t0 G0 H0 G2 G3 H3 s15 s24 X s16 s25 L s17 s26 H2 p2 s27 p1 p3 B1 n1 n3 n5 n7 p0 j1 j2 u10 m2 Q m0 m3 m1 u11 u20 u12 u21 u13 u22 W2 u14 u23 u15 u24 f u16 W0 u25 u17 u26 u27 R2 R0 W1 W3 R1 R3 Y A2 h0 h2 h1 i1 i3 I2 I0 N0 N1 x l J2 A1 A3 A0 w0 J1 J3 y2 F1 F3 y0 V"
-SEQ0 = "k0 k1 k2 k3 k5 k25 k21 k44 k17 k28 k13 k16 k33 k58 k48 k56 k23 k24 k55 k42 k43 k57 k30 k26 k19 k45 k46 k27 k54 B0 k31 P3 k47 s10 G1 G0 P1 c P2 B1 s11 s20 k49 k14 k15 a C3 s21 s12 b H1 k32 k29 C2 H0 C1 G3 P0 C0 s13 s22 U3 g G2 s14 s23 k20 t1 t0 H3 s15 n1 H2 n3 s24 X s16 s25 n5 L s17 s26 p1 s27 m2 n7 U0 m3 p3 p0 p2 U1 k18 j1 Q u10 U2 j2 u11 u20 W1 u12 k50 m1 m0 u21 f u13 k51 u22 u14 W3 W0 u23 u15 u24 u16 W2 u25 u17 u26 k52 u27 R3 R1 R2 R0 Y A2 h0 h2 h1 k53 I1 i2 A3 A0 I3 i0 N0 N1 x l A1 w1 J2 J3 J0 F3 y2 F0 y1 V"
+FAR = True
+SEQ = "P1 P2 P0 v1 C0 C2 A1 A0 A2 w0 J1 A3 w3 J2 F0 y1 F2 y3 V B0 U1 s10 c s11 s20 G1 a G0 H1 H0 G2 s12 s21 b s13 s22 G3 H3 g s14 s23 B1 t1 U2 n1 t0 s15 s24 X s16 s25 n3 L H2 n5 s17 s26 p0 K3 s27 n7 p2 U0 p1 T3 M3 j1 Q u10 j2 U3 W1 W2 m1 m3 u11 m2 m0 f u20 u12 r1 u21 R2 u13 W3 r3 u22 u14 h0 h2 u23 u15 W0 R0 Y S0 S1 u24 h5 u16 h6 u25 h7 u17 h4 u26 h8 h10 h1 u27 h11 h9 h3 h15 h14 h12 h13 N0 N1 x l S2"
+SEQ0 = "k0 k1 k2 k28 k24 k30 k3 k13 k16 k58 k15 k26 k5 k56 k55 k48 k21 k23 k20 k42 k43 k31 k18 G1 H1 k14 k17 k27 k57 k33 G0 k19 k25 k45 k49 k46 k44 B0 s10 c s20 s11 a G3 k29 H3 P2 P3 C3 s21 s12 b s13 k54 H0 B1 P1 k47 C1 s22 n1 G2 P0 U1 g s14 s23 H2 t0 t1 s15 s24 k32 C2 X s16 s25 n5 U3 L n3 s17 s26 p3 s27 p1 p2 C0 p0 U0 n7 m0 j1 m2 m1 Q u10 j2 U2 W2 u11 W1 m3 u12 f u20 R2 r1 u21 W3 W0 r0 u22 u13 R3 Y S0 S1 u14 u23 h2 h3 u15 u24 h0 u16 u25 h5 h4 h7 u17 u26 h11 h1 h9 u27 h10 h8 h6 h15 h14 h13 h12 N1 N0 x l S2 k59 k61"
 
 SCRATCH = {
     "xin": ("sbuf", [128, 4 * C], "bfloat16"), "uin": ("sbuf", [128, 512], "bfloat16"), "vin": ("sbuf", [128, 512], "bfloat16"),
@@ -19,8 +20,9 @@ SCRATCH = {
     "qvv": ("sbuf", [128, 128], F8), "sqvv": ("sbuf", [128, 128], "uint8"),
     "c32": ("sbuf", [128, 256], "bfloat16"), "dd": ("sbuf", [128, 516], "bfloat16"),
     "cf": ("sbuf", [128, 512], F8), "scf": ("sbuf", [128, 512], "uint8"),
+    "dh": ("sbuf", [128, 516], "bfloat16"), "ch": ("sbuf", [128, 256], F8), "sch": ("sbuf", [128, 256], "uint8"), "ga": ("sbuf", [128, 2 * C], "bfloat16"),
     "zt": ("sbuf", [128, 4 * C], "bfloat16"), "xt": ("sbuf", [128, 4 * C], "bfloat16"), "vt": ("sbuf", [128, 512], "bfloat16"),
-    "du": ("sbuf", [128, 512], "bfloat16"), "dx": ("sbuf", [128, 4 * C], "bfloat16"),
+    "du": ("sbuf", [128, 512], "bfloat16"), "dx": ("sbuf", [128, 4 * C], "bfloat16"), "dy": ("sbuf", [128, 4 * C], "bfloat16"),
     "bigc": ("sbuf", [128, C], "float32"), "rst": ("sbuf", [128, C], "float32"), "down": ("sbuf", [128, C], "bfloat16"),
     "st": ("sbuf", [128, C], "float32"), "pa": ("sbuf", [128, PS], "float32"), "nr": ("sbuf", [128, C], "bfloat16"), "ag": ("sbuf", [128, 512], "bfloat16"),
     "kt": ("sbuf", [128, 64], "bfloat16"), "lst": ("sbuf", [128, 16], "uint16"), "kfo": ("sbuf", [128, 32], "float32"),
@@ -28,9 +30,8 @@ SCRATCH = {
     "sg": ("sbuf", [128, 5 * C], "bfloat16"), "keep": ("sbuf", [128, 5 * C], "bfloat16"), "key": ("sbuf", [128, 5 * C], "float16"),
     "cols": ("sbuf", [128, C], "bfloat16"), "low": ("sbuf", [128, C], "bfloat16"), "qb": ("sbuf", [128, 9 * PS], "float16"),
     "lv": ("sbuf", [128, 40], "bfloat16"), "lev": ("sbuf", [128, 40], "bfloat16"),
-    "nb": ("sbuf", [128, 64], "bfloat16"), "nt": ("sbuf", [128, 64], "bfloat16"), "lst2": ("sbuf", [128, 16], "uint16"), "nfo": ("sbuf", [128, 32], "float32"),
-    "i1": ("sbuf", [128, 2], "int32"), "i2": ("sbuf", [128, 2], "int32"), "col": ("sbuf", [128, 4], "float32"),
-    "cz": ("sbuf", [128, 160], "bfloat16"), "czt": ("sbuf", [128, 160], "bfloat16"), "off": ("sbuf", [128, 4], "uint16"),
+    "nb": ("sbuf", [128, 64], "bfloat16"), "nt": ("sbuf", [128, 64], "bfloat16"), "nd": ("sbuf", [128, 8], "bfloat16"), "nfo": ("sbuf", [128, 32], "float32"),
+    "col": ("sbuf", [128, 2], "float32"), "cz": ("sbuf", [128, 128], "bfloat16"), "czt": ("sbuf", [128, 128], "bfloat16"), "off": ("sbuf", [128, 4], "uint16"),
     "yb": ("sbuf", [128, C], "float32"),
     "ps": ("psum", [128, 4096], "float32"),
 }
@@ -42,10 +43,12 @@ for _r in range(3):
     SCRATCH["sz%d" % _r] = ("sbuf", [128, C], "uint8")
     SCRATCH["qv%d" % _r] = ("sbuf", [128, 128], F8)
     SCRATCH["sv%d" % _r] = ("sbuf", [128, 128], "uint8")
-    SCRATCH["land%d" % (_r + 1)] = ("sbuf", [128, 128], F8)
-    SCRATCH["lsc%d" % (_r + 1)] = ("sbuf", [128, 128], "uint8")
+    SCRATCH["land%d" % (_r + 1)] = ("sbuf", [128, C if FAR else 128], F8)
+    SCRATCH["lsc%d" % (_r + 1)] = ("sbuf", [128, C if FAR else 128], "uint8")
+    SCRATCH["lin%d" % (_r + 1)] = ("sbuf", [128, 8], "uint16")
+    SCRATCH["lout%d" % _r] = ("sbuf", [128, 16], "uint16")
 SEMAPHORES = ["vs", "ts", "sa", "gc0", "ldx", "ldu", "ldv", "ldw", "ldp", "loc", "st",
-              "arr1", "arr2", "arr3", "ars1", "ars2", "ars3"]
+              "arr1", "arr2", "arr3", "ars1", "ars2", "ars3", "arl1", "arl2", "arl3"]
 
 
 def rank_program(g, core, T, topo):
@@ -191,6 +194,8 @@ def rank_program(g, core, T, topo):
         3: lambda: fill([R("dd")], T.dd[:], 0.0),
         5: lambda: run("g", [R("c32")], [R("dd")], lambda: g.affine_select(T.dd[:, 3:515:4], T.c32[:, 0:128], [[1, 128]], ALU.is_equal, 0.0, 0, -1)),
         55: lambda: unpacker(0), 56: lambda: unpacker(1), 57: lambda: unpacker(2), 48: lambda: unpacker(3),
+        59: lambda: scaled("a", [R("dd")], [R("dh")], T.dh[:], T.dd[:], 2.0 ** -6),
+        60: lambda: quant("ch", "sch", 0, 128, "dh", 1, [R("dh")]), 61: lambda: quant("ch", "sch", 128, 128, "dh", 0, [R("dh")]),
         13: lambda: afill([R("rst")], T.rst[:], C, BIG),
         15: lambda: afill([R("rst")], T.rst[:, 0:C:16], C // 16, -BIG),
         14: lambda: afill([R("pa", 0, 1)], T.pa[:, 0:1], 1, -BIG),
@@ -208,23 +213,40 @@ def rank_program(g, core, T, topo):
         21: order,
         23: lambda: row(32, 64, [[16, 2], [0, 16]], 16, 1),
         24: lambda: row(64, 96, [[0, 16], [16, 2]], 16, 1),
-        25: lambda: row(96, 128, [[0, 4], [32, 4], [0, 2]], 128, -1),
-        26: lambda: (row(128, 144, [[0, 8], [128, 2]], 0, 1), row(144, 160, [[0, 8], [-128, 2]], 144, 1)),
+        25: lambda: iota([R("nbz")], T.nb[:, 8:32], [[0, 24]], 0),
+        26: lambda: (row(96, 112, [[0, 2], [1, 4], [32, 2]], 0), row(112, 128, [[0, 2], [1, 4], [-32, 2]], 36)),
         45: lambda: vec([R("cz"), R("cz0"), R("cz1"), R("cz16"), R("cz17")], [R("czt")], lambda: g.vector.transpose(T.czt[:], T.cz[:])),
-        46: lambda: vec([R("czt")], [R("off", 0, 1)], lambda: g.vector.tensor_copy(T.off[:, 0:1], T.czt[:, 0:1])),
+        46: lambda: vec([R("czt")], [R("off")], lambda: g.vector.tensor_copy(T.off[:, 0:4:2], T.czt[:, 0:128:96])),
         49: lambda: scaled("a", [R("czt")], [R("col", 0, 2)], T.col[:, 0:2], T.czt[:, 32:96:32], 1.0),
-        50: lambda: vec([R("czt")], [R("i1")], lambda: g.vector.tensor_copy(T.i1[:, 0:1], T.czt[:, 96:97])),
-        51: lambda: scaled("a", [R("czt")], [R("col", 2, 3)], T.col[:, 2:3], T.czt[:, 128:129], 0.25),
-        52: lambda: vec([R("i1")], [R("i2")], lambda: g.vector.tensor_scalar(T.i2[:, 0:1], T.i1[:, 0:1], 127, None, ALU.bitwise_and)),
-        53: lambda: vec([R("i2"), R("col", 2, 3)], [R("off", 2, 3)], lambda: g.vector.tensor_scalar(T.off[:, 2:3], T.i2[:, 0:1], 2.0 ** -5, T.col[:, 2:3], ALU.mult, ALU.add)),
     }
+
+    def outputs():
+        mm(0, C, "qvv", "sqvv", 0, "qx3", "sx3", 0, True, True)
+        act([R("bank0")], [R("yb")], lambda: g.scalar.activation(T.yb[:], bank(0, C), ACT.Copy))
+        vec([R("nt")], [R("nfo")], lambda: g.vector.tensor_scalar(T.nfo[:], T.nt[:, 0:32], 256.0, float(H), ALU.mult, ALU.add))
+        vec([R("kt"), R("col", 0, 2)], [R("kfo")], lambda: g.vector.tensor_scalar(T.kfo[:], T.kt[:, 0:32], -1.0, T.col[:, 1:2], ALU.mult, ALU.add))
+        jobs = [("s", [R("qx3")], [], T.oc[:], T.qx3[:].bitcast(dt.uint8))]
+        jobs += [("s", [R("sx3")], [], T.osc[4 * k:4 * k + 4, :], T.sx3[32 * k:32 * k + 4, :]) for k in range(4)]
+        jobs.append(("s", [R("yb")], [], T.y[:], T.yb[:]))
+        jobs += [("s", [R("nfo")], [], T.op[2 * a:2 * a + 2, C:C + 128], T.nfo[32 * a:32 * a + 8, 0:32]) for a in range(4)]
+        for k in range(8):
+            p = 32 * (k // 2) + k % 2
+            jobs.append(("s" if FAR else "sa"[k % 2], [R("kfo")], [], T.op[k:k + 1, 0:C], T.kfo[p:p + 14:2, 0:32]))
+        dmas("st", jobs)
 
     SB = [6, 7]
     AB = [4, 5, 7, 6]
-    for r in range(3):
+    for r in range(4 if FAR else 3):
         X, SX, X1, SX1 = "qx%d" % r, "sx%d" % r, "qx%d" % (r + 1), "sx%d" % (r + 1)
-        U, SU = ("qu", "squ") if r == 0 else ("land%d" % r, "lsc%d" % r)
-        qz, sz, qv, sv = [n + str(r) for n in ("qz", "sz", "qv", "sv")]
+        qz, sz, LO = "qz%d" % r, "sz%d" % r, "lout%d" % r
+        if FAR:
+            qv, sv = "qv%d" % (r - 1), "sv%d" % (r - 1)
+            U, SU = ("qu", "squ") if r == 0 else (qv, sv)
+            LX, LS, LI, DY = "land%d" % r, "lsc%d" % r, "lin%d" % r, "dy"
+        else:
+            qv, sv = "qv%d" % r, "sv%d" % r
+            U, SU = ("qu", "squ") if r == 0 else ("land%d" % r, "lsc%d" % r)
+            LX, LS, LI, DY = X1, SX1, LO, "dx"
 
         def turn_scores(k):
             vec([R("bank%d" % SB[0])], [R("st")], lambda: g.vector.transpose(T.st[:], bank(SB[0], C)))
@@ -251,6 +273,14 @@ def rank_program(g, core, T, topo):
         def zed(b):
             vec([R("du%d" % b), R("dx%d" % b), R("lst")], [R("zt%d" % b)],
                 lambda: g.vector.tensor_tensor(T.zt[:, b:4 * C:4], T.du[:, 128 * b:128 * b + 128].indirect(T.lst[:, 0:14]), T.dx[:, C * b:C * b + C], ALU.add))
+
+        def picked(b):
+            o = C * (b - 2)
+            scaled("a", [R("du%d" % b), R("lst")], [R("ga", o, o + C)], T.ga[:, o:o + C], T.du[:, 128 * b:128 * b + 128].indirect(T.lst[:, 0:14]), 1.0)
+
+        def added(b):
+            o = C * (b - 2)
+            vec([R("ga", o, o + C), R("bank%d" % b)], [R("zt%d" % b)], lambda: g.vector.tensor_tensor(T.zt[:, b:4 * C:4], T.ga[:, o:o + C], bank(b, C), ALU.add))
 
         def scan(k):
             lo, hi = ((0, C), (0, H), (H, C))[k // 10]
@@ -291,14 +321,21 @@ def rank_program(g, core, T, topo):
                 lambda: g.vector.tensor_tensor_scan(T.lev[:], T.keep[:, 0:40], T.lv[:], 0.0, ALU.mult, ALU.add))
 
         def fractions(k):
-            o, i, n, c, nm = ((0, 0, 128, 0, "nba"), (0, 64, 64, 2, "nbb0"), (64, 0, 64, 2, "nbb1"))[k]
-            vec([R("qb"), R("lev")], [R(nm)], lambda: g.vector.tensor_tensor(T.nb[o:o + n, c:32:4], T.qb[i:i + n, PS + C + 1:9 * PS:PS], T.lev[i:i + n, 4:40:5], ALU.subtract))
+            a, q = k // 4, k % 4
+            o = PS * (2 * a + 1) + C + 1
+            vec([R("qb", o, o + 1), R("qb", o + PS, o + PS + 1), R("lev")], [R("nb%d" % k)],
+                lambda: g.vector.tensor_tensor(T.nb[32 * a:32 * a + 32, q:8:4], T.qb[32 * q:32 * q + 32, o:o + PS + 1:PS], T.lev[32 * q:32 * q + 32, 10 * a + 4:10 * a + 10:5], ALU.subtract))
 
-        def spread(q, a):
-            b = (a + 1) % 4
-            scaled(q, [R("nba"), R("nbb%d" % (b // 2))], [R("nbc%d" % a)], T.nb[32 * a:32 * a + 32, 1:32:2], T.nb[32 * b:32 * b + 32, 0:32:2], 1.0)
+        def early(a):
+            o = PS * (2 * a + 1) + C + 1
+            vec([R("qb", o, o + 1), R("qb", o + PS, o + PS + 1), R("lev")], [R("nd", 2 * a, 2 * a + 2)],
+                lambda: g.vector.tensor_tensor(T.nd[:, 2 * a:2 * a + 2], T.qb[:, o:o + PS + 1:PS], T.lev[:, 10 * a + 4:10 * a + 10:5], ALU.subtract))
 
-        spreads = [R("nba"), R("nbb0"), R("nbb1")] + [R("nbc%d" % a) for a in range(4)]
+        def spread(e, k):
+            a, q = k // 4, k % 4
+            scaled(e, [R("nd", 2 * a, 2 * a + 2)], [R("nb%d" % k)], T.nb[32 * a:32 * a + 32, q:8:4], T.nd[32 * q:32 * q + 32, 2 * a:2 * a + 2], 1.0)
+
+        spreads = [R("nb%d" % k) for k in range(16)] + [R("nbz")]
 
         def turn_along(k):
             vec(spreads, [R("nt", 32 * k, 32 * k + 32)], lambda: g.vector.transpose(T.nt[:, 32 * k:32 * k + 32], T.nb[:, 0:32]))
@@ -307,30 +344,38 @@ def rank_program(g, core, T, topo):
             vec([R("nt")], [R("nbd")], lambda: g.vector.transpose(T.nb[:, 32:64], T.nt[:, 16:48]))
 
         def lists_along(k):
-            vec(spreads + [R("nbd"), R("off", 2, 3)], [R("lst2")],
-                lambda: g.vector.tensor_scalar(T.lst2[:], T.nb[:, 0:64].indirect(T.off[:, 2:3]), 256.0, float(H), ALU.mult, ALU.add))
+            vec(spreads + [R("nbd"), R("off", 2, 3)], [R(LO)],
+                lambda: g.vector.tensor_scalar(T[LO][:], T.nb[:, 0:64].indirect(T.off[:, 2:3]), 256.0, float(H), ALU.mult, ALU.add))
 
         def state(q, b):
-            scaled(q, [R("bank%d" % b)], [R("xt%d" % b)], T.xt[:, b:4 * C:4], bank(b, C), 2.0 ** -5)
+            lo, hi = ((0, C), (0, H), (H, C))[b // 10]
+            b %= 10
+            scaled(q, [R("bank%d" % b)], [R("xt%d" % b, lo, hi)], T.xt[:, 4 * lo + b:4 * hi:4], T.ps[:, 512 * b + lo:512 * b + hi], 2.0 ** -5)
 
         def plane(q, nm, n, b, j):
             scaled(q, [R("bank%d" % j)], [R(nm + str(b))], T[nm][:, n * b:n * b + n], bank(j, n), 2.0 ** -6)
 
         def gather(q, b):
-            scaled(q, [R("dx%d" % b), R("lst2")], [R("vt%d" % b)], T.vt[:, b:512:4], T.dx[:, C * b:C * b + C].indirect(T.lst2[:, 0:8]), 2.0)
+            scaled(q, [R(DY + str(b)), R(LI)], [R("vt%d" % b)], T.vt[:, b:512:4], T[DY][:, C * b:C * b + C].indirect(T[LI][:, 0:8]), 2.0)
 
         def hand_on(k):
-            quant(qv, sv, 0, 128, "vt", 0, [R("vt%d" % b) for b in range(4)])
+            nm, mine, sem = (("land", X1 if FAR else qv, "arr"), ("lsc", SX1 if FAR else sv, "ars"), ("lin", LO, "arl"))[k]
             dst = T.cores[(rank + STEP[r]) % 8]
             src = T.cores[(rank - STEP[r]) % 8]
             rid, pid = topo.addr(dst, core)
-            need("g", deps("g", [R(qv), R(sv)], []))
-            for nm, view, mine, sem in (("land", T["land%d" % (r + 1)][:].bitcast(dt.uint8), T[qv][:].bitcast(dt.uint8), "arr"), ("lsc", T["lsc%d" % (r + 1)][:], T[sv][:], "ars")):
-                arr = sem + str(r + 1)
-                g.remote_dma(view, mine, T.sem[arr], T.sem["loc"], pid, rid, topo.mask(core, dst))
-                count["loc"] += len(topo.engines(core, dst))
-                count[arr] = len(topo.engines(src, core))
-                note("g", (arr, count[arr], {arr: count[arr]}), [], [R(nm + str(r + 1))])
+            need("g", deps("g", [R(mine)], []))
+            nm, arr = nm + str(r + 1), sem + str(r + 1)
+            o, i = T[nm][:], T[mine][:, 0:8] if k == 2 else T[mine][:]
+            g.remote_dma(o if k else o.bitcast(dt.uint8), i if k else i.bitcast(dt.uint8), T.sem[arr], T.sem["loc"], pid, rid, topo.mask(core, dst))
+            count["loc"] += len(topo.engines(core, dst))
+            count[arr] = len(topo.engines(src, core))
+            note("g", (arr, count[arr], {arr: count[arr]}), [], [R(nm)])
+
+        def stationary(k):
+            quant(qv, sv, 0, 128, "vt", 0, [R("vt%d" % b) for b in range(4)])
+            if not FAR:
+                hand_on(0)
+                hand_on(1)
 
         steps = {
             "k": lambda k: first[k](),
@@ -341,35 +386,27 @@ def rank_program(g, core, T, topo):
             "H": lambda b: plane("a", "du", 128, b, 4 + b % 2), "q": lambda b: plane("v", "du", 128, b, 4 + b % 2),
             "P": lambda b: mm(b, C, "cf", "scf", 128 * b, X, SX, 0, True, True),
             "C": lambda b: plane("a", "dx", C, b, b), "v": lambda b: plane("v", "dx", C, b, b),
-            "A": lambda b: mm(AB[b], C, "cf", "scf", 128 * b, X1, SX1, 0, True, True),
-            "J": lambda b: plane("a", "dx", C, b, AB[b]), "w": lambda b: plane("v", "dx", C, b, AB[b]),
+            "A": lambda b: mm(AB[b], C, "cf", "scf", 128 * b, LX, LS, 0, True, True),
+            "J": lambda b: plane("a", DY, C, b, AB[b]), "w": lambda b: plane("v", DY, C, b, AB[b]),
             "c": turn_scores, "a": highest, "b": records, "g": rows, "t": ends, "X": exchange_down, "L": lists_down, "p": zed,
+            "T": lambda b: mm(b, C, "ch", "sch", 128 * (b - 2), X, SX, 0, True, True), "K": picked, "M": added,
             "s": scan, "n": sign, "j": keys, "u": least, "m": marks, "f": levels, "h": fractions,
-            "i": lambda k: spread("v", k), "I": lambda k: spread("a", k), "N": turn_along, "x": exchange_along, "l": lists_along,
+            "e": early, "i": lambda k: spread("v", k), "I": lambda k: spread("a", k), "N": turn_along, "x": exchange_along, "l": lists_along,
             "R": lambda b: state("a", b), "r": lambda b: state("v", b),
             "F": lambda b: gather("a", b), "y": lambda b: gather("v", b),
             "Q": lambda k: quant(qz, sz, 0, C, "zt", 0, [R("zt%d" % b) for b in range(4)]),
             "Y": lambda k: quant(X1, SX1, 0, C, "xt", 0, [R("xt%d" % b) for b in range(4)]),
-            "V": hand_on,
+            "S": hand_on, "V": stationary,
         }
-        for word in (SEQ if r else SEQ0).split():
+        for word in [w for w in (SEQ if r else SEQ0).split() if r < 3 or w[0] in "AJwFyV"]:
             steps[word[0]](int(word[1:] or "0"))
         if r == 0:
             quant("qvv", "sqvv", 0, 128, "vin", 0, [R("vin")])
-    mm(0, C, "qvv", "sqvv", 0, "qx3", "sx3", 0, True, True)
-    act([R("bank0")], [R("yb")], lambda: g.scalar.activation(T.yb[:], bank(0, C), ACT.Copy))
-    vec([R("nt")], [R("nfo")], lambda: g.vector.tensor_scalar(T.nfo[:], T.nt[:, 0:32], 256.0, float(H), ALU.mult, ALU.add))
-    vec([R("kt"), R("col", 0, 2)], [R("kfo")], lambda: g.vector.tensor_scalar(T.kfo[:], T.kt[:, 0:32], -1.0, T.col[:, 1:2], ALU.mult, ALU.add))
-    jobs = [("s", [R("qx3")], [], T.oc[:], T.qx3[:].bitcast(dt.uint8))]
-    jobs += [("s", [R("sx3")], [], T.osc[4 * k:4 * k + 4, :], T.sx3[32 * k:32 * k + 4, :]) for k in range(4)]
-    jobs.append(("a", [R("yb")], [], T.y[:], T.yb[:]))
-    jobs += [("a", [R("nfo")], [], T.op[0:8, C + 32 * a:C + 32 * a + 32], T.nfo[a:32:4, 0:32]) for a in range(4)]
-    for k in range(8):
-        p = 32 * (k // 2) + k % 2
-        jobs.append(("sa"[k // 6], [R("kfo")], [], T.op[k:k + 1, 0:C], T.kfo[p:p + 14:2, 0:32]))
-    dmas("st", jobs)
-    jobs = [("s", [R("land3")], [], T.uc[:], T.land3[:].bitcast(dt.uint8))]
-    jobs += [("as"[k % 2], [R("lsc3")], [], T.usc[4 * k:4 * k + 4, :], T.lsc3[32 * k:32 * k + 4, :]) for k in range(4)]
+        if r == 2:
+            outputs()
+    UL, SL = ("qv2", "sv2") if FAR else ("land3", "lsc3")
+    jobs = [("a", [R(UL)], [], T.uc[:], T[UL][:].bitcast(dt.uint8))]
+    jobs += [("sa"[k // 3], [R(SL)], [], T.usc[4 * k:4 * k + 4, :], T[SL][32 * k:32 * k + 4, :]) for k in range(4)]
     dmas("st", jobs)
     g.wait_ge(T.sem["loc"], count["loc"])
     for s in ("vs", "ts", "sa", "gc0", "ldx", "ldu", "ldv", "ldw", "ldp", "st"):

from concourse.mybir import dt, AluOpType, ActivationFunctionType

STEP = [4, 1, 2]
C = 224
H = C // 2
BIG = 1.0e29
KEY = 64.0
PS = 232
F8 = "float8_e4m3fn_x4"
ALU = AluOpType
ACT = ActivationFunctionType
FAR = True
SEQ = "P1 P2 P0 v1 C0 C2 A1 A0 A2 w0 J1 A3 w3 J2 F0 y1 F2 y3 V B0 U1 s10 c s11 s20 G1 a G0 H1 H0 G2 s12 s21 b s13 s22 G3 H3 g s14 s23 B1 t1 U2 n1 t0 s15 s24 X s16 s25 n3 L H2 n5 s17 s26 p0 K3 s27 n7 p2 U0 p1 T3 M3 j1 Q u10 j2 U3 W1 W2 m1 m3 u11 m2 m0 f u20 u12 r1 u21 R2 u13 W3 r3 u22 u14 h0 h2 u23 u15 W0 R0 Y S0 S1 u24 h5 u16 h6 u25 h7 u17 h4 u26 h8 h10 h1 u27 h11 h9 h3 h15 h14 h12 h13 N0 N1 x l S2"
SEQ0 = "k0 k1 k2 k28 k24 k30 k3 k13 k16 k58 k15 k26 k5 k56 k55 k48 k21 k23 k20 k42 k43 k31 k18 G1 H1 k14 k17 k27 k57 k33 G0 k19 k25 k45 k49 k46 k44 B0 s10 c s20 s11 a G3 k29 H3 P2 P3 C3 s21 s12 b s13 k54 H0 B1 P1 k47 C1 s22 n1 G2 P0 U1 g s14 s23 H2 t0 t1 s15 s24 k32 C2 X s16 s25 n5 U3 L n3 s17 s26 p3 s27 p1 p2 C0 p0 U0 n7 m0 j1 m2 m1 Q u10 j2 U2 W2 u11 W1 m3 u12 f u20 R2 r1 u21 W3 W0 r0 u22 u13 R3 Y S0 S1 u14 u23 h2 h3 u15 u24 h0 u16 u25 h5 h4 h7 u17 u26 h11 h1 h9 u27 h10 h8 h6 h15 h14 h13 h12 N1 N0 x l S2 k59 k61"

SCRATCH = {
    "xin": ("sbuf", [128, 4 * C], "bfloat16"), "uin": ("sbuf", [128, 512], "bfloat16"), "vin": ("sbuf", [128, 512], "bfloat16"),
    "wq": ("sbuf", [128, 512], F8), "wsc": ("sbuf", [128, 512], "uint8"),
    "qu": ("sbuf", [128, 128], F8), "squ": ("sbuf", [128, 128], "uint8"),
    "qvv": ("sbuf", [128, 128], F8), "sqvv": ("sbuf", [128, 128], "uint8"),
    "c32": ("sbuf", [128, 256], "bfloat16"), "dd": ("sbuf", [128, 516], "bfloat16"),
    "cf": ("sbuf", [128, 512], F8), "scf": ("sbuf", [128, 512], "uint8"),
    "dh": ("sbuf", [128, 516], "bfloat16"), "ch": ("sbuf", [128, 256], F8), "sch": ("sbuf", [128, 256], "uint8"), "ga": ("sbuf", [128, 2 * C], "bfloat16"),
    "zt": ("sbuf", [128, 4 * C], "bfloat16"), "xt": ("sbuf", [128, 4 * C], "bfloat16"), "vt": ("sbuf", [128, 512], "bfloat16"),
    "du": ("sbuf", [128, 512], "bfloat16"), "dx": ("sbuf", [128, 4 * C], "bfloat16"), "dy": ("sbuf", [128, 4 * C], "bfloat16"),
    "bigc": ("sbuf", [128, C], "float32"), "rst": ("sbuf", [128, C], "float32"), "down": ("sbuf", [128, C], "bfloat16"),
    "st": ("sbuf", [128, C], "float32"), "pa": ("sbuf", [128, PS], "float32"), "nr": ("sbuf", [128, C], "bfloat16"), "ag": ("sbuf", [128, 512], "bfloat16"),
    "kt": ("sbuf", [128, 64], "bfloat16"), "lst": ("sbuf", [128, 16], "uint16"), "kfo": ("sbuf", [128, 32], "float32"),
    "pb": ("sbuf", [128, 8 * PS], "float32"),
    "sg": ("sbuf", [128, 5 * C], "bfloat16"), "keep": ("sbuf", [128, 5 * C], "bfloat16"), "key": ("sbuf", [128, 5 * C], "float16"),
    "cols": ("sbuf", [128, C], "bfloat16"), "low": ("sbuf", [128, C], "bfloat16"), "qb": ("sbuf", [128, 9 * PS], "float16"),
    "lv": ("sbuf", [128, 40], "bfloat16"), "lev": ("sbuf", [128, 40], "bfloat16"),
    "nb": ("sbuf", [128, 64], "bfloat16"), "nt": ("sbuf", [128, 64], "bfloat16"), "nd": ("sbuf", [128, 8], "bfloat16"), "nfo": ("sbuf", [128, 32], "float32"),
    "col": ("sbuf", [128, 2], "float32"), "cz": ("sbuf", [128, 128], "bfloat16"), "czt": ("sbuf", [128, 128], "bfloat16"), "off": ("sbuf", [128, 4], "uint16"),
    "yb": ("sbuf", [128, C], "float32"),
    "ps": ("psum", [128, 4096], "float32"),
}
for _r in range(4):
    SCRATCH["qx%d" % _r] = ("sbuf", [128, C], F8)
    SCRATCH["sx%d" % _r] = ("sbuf", [128, C], "uint8")
for _r in range(3):
    SCRATCH["qz%d" % _r] = ("sbuf", [128, C], F8)
    SCRATCH["sz%d" % _r] = ("sbuf", [128, C], "uint8")
    SCRATCH["qv%d" % _r] = ("sbuf", [128, 128], F8)
    SCRATCH["sv%d" % _r] = ("sbuf", [128, 128], "uint8")
    SCRATCH["land%d" % (_r + 1)] = ("sbuf", [128, C if FAR else 128], F8)
    SCRATCH["lsc%d" % (_r + 1)] = ("sbuf", [128, C if FAR else 128], "uint8")
    SCRATCH["lin%d" % (_r + 1)] = ("sbuf", [128, 8], "uint16")
    SCRATCH["lout%d" % _r] = ("sbuf", [128, 16], "uint16")
SEMAPHORES = ["vs", "ts", "sa", "gc0", "ldx", "ldu", "ldv", "ldw", "ldp", "loc", "st",
              "arr1", "arr2", "arr3", "ars1", "ars2", "ars3", "arl1", "arl2", "arl3"]


def rank_program(g, core, T, topo):
    rank = T.rank_of(core)
    if rank is None:
        return
    queue = {"v": g.vector, "t": g.tensor, "a": g.scalar, "s": g.sync, "g": g}
    csem = {"v": "vs", "t": "ts", "a": "sa", "g": "gc0"}
    known = {q: {} for q in queue}
    count = {s: 0 for s in SEMAPHORES}
    clocks = {s: {} for s in SEMAPHORES}
    regs = {}

    def merge(a, b):
        for s, n in b.items():
            if a.get(s, 0) < n:
                a[s] = n

    def deps(q, reads, writes):
        out = []
        for w, items in ((False, reads), (True, writes)):
            for name, lo, hi in items:
                bank = name.startswith("bank")
                for (l, h, ww, qq, tok) in regs.get(name, []):
                    if l >= hi or h <= lo:
                        continue
                    if bank:
                        if qq == q and (q == "t" or not (w or ww)):
                            continue
                    elif not (w or ww):
                        continue
                    out.append(tok)
        return out

    def need(q, toks):
        best = {}
        for tk in toks:
            s, n, c = tk
            if known[q].get(s, 0) < n and (s not in best or best[s][1] < n):
                best[s] = tk
        for s in list(best):
            if any(o != s and best[o][2].get(s, 0) >= best[s][1] for o in best):
                del best[s]
        for s, tk in best.items():
            queue[q].wait_ge(T.sem[s], tk[1])
            merge(known[q], tk[2])

    def note(q, tok, reads, writes):
        for name, lo, hi in writes:
            old = regs.get(name, [])
            regs[name] = [e for e in old if not (lo <= e[0] and e[1] <= hi)] + [(lo, hi, True, q, tok)]
        for name, lo, hi in reads:
            regs.setdefault(name, []).append((lo, hi, False, q, tok))

    def token(q, s, n):
        count[s] += n
        c = dict(known[q])
        merge(c, clocks[s])
        c[s] = count[s]
        clocks[s] = c
        return (s, count[s], c)

    def run(q, reads, writes, fn):
        need(q, deps(q, reads, writes))
        fn().then_inc(T.sem[csem[q]], 1)
        tok = token(q, csem[q], 1)
        note(q, tok, reads, writes)
        return tok

    def dmas(s, jobs):
        ds = [deps(q, r, w) for q, r, w, o, i in jobs]
        toks = []
        for (q, r, w, o, i), d in zip(jobs, ds):
            need(q, d)
            queue[q].dma_start(o, i).then_inc(T.sem[s], 16)
            toks.append(token(q, s, 16))
        for q, r, w, o, i in jobs:
            note(q, toks[-1], r, w)
        return toks[-1]

    def R(name, lo=0, hi=None):
        return (name, lo, 1 << 20 if hi is None else hi)

    def bank(j, n):
        return T.ps[:, 512 * j:512 * j + n]

    def mm(j, n, a, sa, alo, b, sb, blo, start, stop):
        run("t", [R(a, alo, alo + 128), R(sa, alo, alo + 128), R(b, blo, blo + n), R(sb, blo, blo + n)], [R("bank%d" % j)],
            lambda: g.tensor.matmul_mx(bank(j, n), T[a][:, alo:alo + 128], T[sa][:, alo:alo + 128], T[b][:, blo:blo + n], T[sb][:, blo:blo + n], start, stop))

    def vec(reads, writes, fn):
        return run("v", reads, writes, fn)

    def act(reads, writes, fn):
        return run("a", reads, writes, fn)

    def fill(names, view, c):
        vec([], names, lambda: g.vector.memset(view, c))

    def afill(names, view, n, c):
        act([R("c32")], names, lambda: g.scalar.activation(view, T.c32[:, 0:n], ACT.Identity, bias=c, scale=0.0))

    def iota(names, view, pat, base, step=0):
        run("g", [], names, lambda: g.iota(view, pat, base, step, allow_small_or_imprecise_dtypes=True))

    def quant(q, s, lo, n, tile, tlo, names):
        vec(names, [R(q, lo, lo + n), R(s, lo, lo + n)], lambda: g.vector.quantize_mx(T[q][:, lo:lo + n], T[s][:, lo:lo + n], T[tile][:, tlo:tlo + 4 * n]))

    def scaled(q, reads, writes, o, i, scale):
        if q == "a":
            act(reads, writes, lambda: g.scalar.activation(o, i, ACT.Copy, scale=scale))
        else:
            vec(reads, writes, lambda: g.vector.tensor_scalar(o, i, scale, None, ALU.mult))

    def later_loads():
        need("s", deps("s", [R("xin")], []))
        dmas("ldw", [("s", [], [R("wq")], T.wq[:].bitcast(dt.uint8), T.wc[:])])
        dmas("ldp", [("s", [], [R("wsc")], T.wsc[:], T.ws[:])])
        dmas("ldv", [("s", [], [R("vin")], T.vin[:], T.v[:])])

    def row(lo, hi, pat, base, step=0):
        iota([R("cz", lo, hi)], T.cz[:, lo:hi], pat, base, step)

    def order():
        for x in range(2):
            for h in range(2):
                lo = 16 * x + h
                iota([R("cz%d" % lo)], T.cz[:, lo:lo + 15:2], [[32 if h == x else 2, 8]], 16 * x + 15 if h == x else C + x)

    def keeps(j):
        afill([R("keep%d" % j)], T.keep[:, j:5 * C:5], C, 1.0 if j else 0.0)

    def unpacker(b):
        quant("cf", "scf", 128 * b, 128, "dd", 3 - b, [R("dd")])

    first = {
        0: lambda: dmas("ldx", [("s", [], [R("xin")], T.xin[:], T.x[:])]),
        1: lambda: dmas("ldu", [("a", [], [R("uin")], T.uin[:], T.u[:])]),
        44: later_loads,
        42: lambda: quant("qu", "squ", 0, 128, "uin", 0, [R("uin")]),
        43: lambda: quant("qx0", "sx0", 0, C, "xin", 0, [R("xin")]),
        2: lambda: fill([R("c32")], T.c32[:], 32.0),
        3: lambda: fill([R("dd")], T.dd[:], 0.0),
        5: lambda: run("g", [R("c32")], [R("dd")], lambda: g.affine_select(T.dd[:, 3:515:4], T.c32[:, 0:128], [[1, 128]], ALU.is_equal, 0.0, 0, -1)),
        55: lambda: unpacker(0), 56: lambda: unpacker(1), 57: lambda: unpacker(2), 48: lambda: unpacker(3),
        59: lambda: scaled("a", [R("dd")], [R("dh")], T.dh[:], T.dd[:], 2.0 ** -6),
        60: lambda: quant("ch", "sch", 0, 128, "dh", 1, [R("dh")]), 61: lambda: quant("ch", "sch", 128, 128, "dh", 0, [R("dh")]),
        13: lambda: afill([R("rst")], T.rst[:], C, BIG),
        15: lambda: afill([R("rst")], T.rst[:, 0:C:16], C // 16, -BIG),
        14: lambda: afill([R("pa", 0, 1)], T.pa[:, 0:1], 1, -BIG),
        19: lambda: iota([R("down")], T.down[:], [[0, C // 16], [-1, 16]], 16),
        20: lambda: iota([R("ag", C, 512)], T.ag[:, C:512], [[0, 512 - C]], 1),
        16: lambda: afill([R("bigc")], T.bigc[:], C, BIG),
        17: lambda: afill([R("pb", PS * k, PS * k + 1) for k in range(8)], T.pb[:, 0:8 * PS:PS], 8, -BIG),
        27: lambda: iota([R("cols")], T.cols[:], [[1, C]], -H),
        32: lambda: scaled("a", [R("cols")], [R("sg0")], T.sg[:, 0:5 * C:5], T.cols[:], 2.0 ** -8),
        28: lambda: keeps(0), 29: lambda: keeps(1), 30: lambda: keeps(2), 31: lambda: keeps(3), 47: lambda: keeps(4),
        54: lambda: afill([R("lv4")], T.lv[:, 0:40:5], 8, 0.0),
        18: lambda: afill([R("low")], T.low[:], C, -KEY),
        33: lambda: scaled("v", [R("c32")], [R("qb", PS * k, PS * k + 1) for k in range(8)], T.qb[:, 0:8 * PS:PS], T.c32[:, 0:8], KEY / 32.0),
        58: lambda: scaled("v", [R("c32")], [R("qb", H + 1, C + 2)], T.qb[:, H + 1:C + 2], T.c32[:, 0:H + 1], -KEY / 32.0),
        21: order,
        23: lambda: row(32, 64, [[16, 2], [0, 16]], 16, 1),
        24: lambda: row(64, 96, [[0, 16], [16, 2]], 16, 1),
        25: lambda: iota([R("nbz")], T.nb[:, 8:32], [[0, 24]], 0),
        26: lambda: (row(96, 112, [[0, 2], [1, 4], [32, 2]], 0), row(112, 128, [[0, 2], [1, 4], [-32, 2]], 36)),
        45: lambda: vec([R("cz"), R("cz0"), R("cz1"), R("cz16"), R("cz17")], [R("czt")], lambda: g.vector.transpose(T.czt[:], T.cz[:])),
        46: lambda: vec([R("czt")], [R("off")], lambda: g.vector.tensor_copy(T.off[:, 0:4:2], T.czt[:, 0:128:96])),
        49: lambda: scaled("a", [R("czt")], [R("col", 0, 2)], T.col[:, 0:2], T.czt[:, 32:96:32], 1.0),
    }

    def outputs():
        mm(0, C, "qvv", "sqvv", 0, "qx3", "sx3", 0, True, True)
        act([R("bank0")], [R("yb")], lambda: g.scalar.activation(T.yb[:], bank(0, C), ACT.Copy))
        vec([R("nt")], [R("nfo")], lambda: g.vector.tensor_scalar(T.nfo[:], T.nt[:, 0:32], 256.0, float(H), ALU.mult, ALU.add))
        vec([R("kt"), R("col", 0, 2)], [R("kfo")], lambda: g.vector.tensor_scalar(T.kfo[:], T.kt[:, 0:32], -1.0, T.col[:, 1:2], ALU.mult, ALU.add))
        jobs = [("s", [R("qx3")], [], T.oc[:], T.qx3[:].bitcast(dt.uint8))]
        jobs += [("s", [R("sx3")], [], T.osc[4 * k:4 * k + 4, :], T.sx3[32 * k:32 * k + 4, :]) for k in range(4)]
        jobs.append(("s", [R("yb")], [], T.y[:], T.yb[:]))
        jobs += [("s", [R("nfo")], [], T.op[2 * a:2 * a + 2, C:C + 128], T.nfo[32 * a:32 * a + 8, 0:32]) for a in range(4)]
        for k in range(8):
            p = 32 * (k // 2) + k % 2
            jobs.append(("s" if FAR else "sa"[k % 2], [R("kfo")], [], T.op[k:k + 1, 0:C], T.kfo[p:p + 14:2, 0:32]))
        dmas("st", jobs)

    SB = [6, 7]
    AB = [4, 5, 7, 6]
    for r in range(4 if FAR else 3):
        X, SX, X1, SX1 = "qx%d" % r, "sx%d" % r, "qx%d" % (r + 1), "sx%d" % (r + 1)
        qz, sz, LO = "qz%d" % r, "sz%d" % r, "lout%d" % r
        if FAR:
            qv, sv = "qv%d" % (r - 1), "sv%d" % (r - 1)
            U, SU = ("qu", "squ") if r == 0 else (qv, sv)
            LX, LS, LI, DY = "land%d" % r, "lsc%d" % r, "lin%d" % r, "dy"
        else:
            qv, sv = "qv%d" % r, "sv%d" % r
            U, SU = ("qu", "squ") if r == 0 else ("land%d" % r, "lsc%d" % r)
            LX, LS, LI, DY = X1, SX1, LO, "dx"

        def turn_scores(k):
            vec([R("bank%d" % SB[0])], [R("st")], lambda: g.vector.transpose(T.st[:], bank(SB[0], C)))

        def highest(k):
            vec([R("st"), R("rst")], [R("pa", 1, C + 1)], lambda: g.vector.tensor_tensor_scan(T.pa[:, 1:C + 1], T.rst[:], T.st[:], -BIG, ALU.min, ALU.max))

        def records(k):
            vec([R("st"), R("pa", 0, C)], [R("nr")], lambda: g.vector.tensor_tensor(T.nr[:], T.st[:], T.pa[:, 0:C], ALU.is_le))

        def rows(k):
            vec([R("nr"), R("down")], [R("ag", 0, C)], lambda: g.vector.tensor_tensor_scan(T.ag[:, 0:C], T.nr[:], T.down[:], 0.0, ALU.mult, ALU.max))

        def ends(k):
            vec([R("ag")], [R("kt", 32 * k, 32 * k + 32)], lambda: g.vector.transpose(T.kt[:, 32 * k:32 * k + 32], T.ag[:, 15:512:16]))

        def exchange_down(k):
            vec([R("kt")], [R("ag", C, 256)], lambda: g.vector.transpose(T.ag[:, C:256], T.kt[:, 16:48]))

        def lists_down(k):
            vec([R("ag", 0, 256), R("off", 0, 1), R("col", 0, 2)], [R("lst")],
                lambda: g.vector.tensor_scalar(T.lst[:], T.ag[:, 0:256].indirect(T.off[:, 0:1]), -1.0, T.col[:, 0:1], ALU.mult, ALU.add))

        def zed(b):
            vec([R("du%d" % b), R("dx%d" % b), R("lst")], [R("zt%d" % b)],
                lambda: g.vector.tensor_tensor(T.zt[:, b:4 * C:4], T.du[:, 128 * b:128 * b + 128].indirect(T.lst[:, 0:14]), T.dx[:, C * b:C * b + C], ALU.add))

        def picked(b):
            o = C * (b - 2)
            scaled("a", [R("du%d" % b), R("lst")], [R("ga", o, o + C)], T.ga[:, o:o + C], T.du[:, 128 * b:128 * b + 128].indirect(T.lst[:, 0:14]), 1.0)

        def added(b):
            o = C * (b - 2)
            vec([R("ga", o, o + C), R("bank%d" % b)], [R("zt%d" % b)], lambda: g.vector.tensor_tensor(T.zt[:, b:4 * C:4], T.ga[:, o:o + C], bank(b, C), ALU.add))

        def scan(k):
            lo, hi = ((0, C), (0, H), (H, C))[k // 10]
            k %= 10
            o = PS * k + lo
            n = hi - lo
            d1 = [R("bigc")] if k == 0 else [R("pb", o - PS, o - PS + n)]
            vec([R("bank%d" % SB[0])] + d1 + ([R("pb", o, o + 1)] if lo else []), [R("pb", o + 1, o + n + 1)],
                lambda: g.vector.tensor_tensor_scan(T.pb[:, o + 1:o + n + 1], T.ps[:, 512 * SB[0] + lo:512 * SB[0] + hi], T.bigc[:, 0:n] if k == 0 else T.pb[:, o - PS:o - PS + n],
                                                    T.pb[:, o:o + 1] if lo else -BIG, ALU.max, ALU.min))

        def sign(k):
            o = PS * k + C
            j = k // 2 + 1
            act([R("bank%d" % SB[1]), R("pb", o, o + 1)], [R("sg%d" % j)],
                lambda: g.scalar.activation(T.sg[:, j:5 * C:5], bank(SB[1], C), ACT.Sign, bias=T.pb[:, o:o + 1], scale=-1.0))

        def keys(k):
            lo = 5 * H * (k - 1)
            vec([R("keep%d" % j) for j in range(5)] + [R("sg%d" % j) for j in range(5)], [R("key%d" % k)],
                lambda: g.vector.tensor_tensor_scan(T.key[:, lo:lo + 5 * H], T.keep[:, lo:lo + 5 * H], T.sg[:, lo:lo + 5 * H], 0.0, ALU.mult, ALU.add))

        def least(k):
            o = PS * (k % 10)
            if k < 20:
                vec([R("key1"), R("low") if o == 0 else R("qb", o - PS, o - PS + H)], [R("qb", o + 1, o + H + 1)],
                    lambda: g.vector.tensor_tensor_scan(T.qb[:, o + 1:o + H + 1], T.key[:, 4:5 * H:5], T.low[:, 0:H] if o == 0 else T.qb[:, o - PS:o - PS + H], KEY, ALU.min, ALU.max))
            else:
                vec([R("key1"), R("key2"), R("qb", o + H, o + C + 1)], [R("qb", o + PS + H + 1, o + PS + C + 2)],
                    lambda: g.vector.tensor_tensor_scan(T.qb[:, o + PS + H + 1:o + PS + C + 2], T.key[:, 5 * H - 1:5 * C:5], T.qb[:, o + H:o + C + 1], -KEY, ALU.min, ALU.max))

        def marks(j):
            o = PS * (2 * j + 1) + C
            act([R("pb")], [R("lv%d" % j)], lambda: g.scalar.activation(T.lv[:, j + 1:40:5], T.pb[:, C:8 * PS:PS], ACT.Sign, bias=T.pb[:, o:o + 1], scale=-1.0))

        def levels(k):
            vec([R("lv%d" % j) for j in range(5)] + [R("keep%d" % j) for j in range(5)], [R("lev")],
                lambda: g.vector.tensor_tensor_scan(T.lev[:], T.keep[:, 0:40], T.lv[:], 0.0, ALU.mult, ALU.add))

        def fractions(k):
            a, q = k // 4, k % 4
            o = PS * (2 * a + 1) + C + 1
            vec([R("qb", o, o + 1), R("qb", o + PS, o + PS + 1), R("lev")], [R("nb%d" % k)],
                lambda: g.vector.tensor_tensor(T.nb[32 * a:32 * a + 32, q:8:4], T.qb[32 * q:32 * q + 32, o:o + PS + 1:PS], T.lev[32 * q:32 * q + 32, 10 * a + 4:10 * a + 10:5], ALU.subtract))

        def early(a):
            o = PS * (2 * a + 1) + C + 1
            vec([R("qb", o, o + 1), R("qb", o + PS, o + PS + 1), R("lev")], [R("nd", 2 * a, 2 * a + 2)],
                lambda: g.vector.tensor_tensor(T.nd[:, 2 * a:2 * a + 2], T.qb[:, o:o + PS + 1:PS], T.lev[:, 10 * a + 4:10 * a + 10:5], ALU.subtract))

        def spread(e, k):
            a, q = k // 4, k % 4
            scaled(e, [R("nd", 2 * a, 2 * a + 2)], [R("nb%d" % k)], T.nb[32 * a:32 * a + 32, q:8:4], T.nd[32 * q:32 * q + 32, 2 * a:2 * a + 2], 1.0)

        spreads = [R("nb%d" % k) for k in range(16)] + [R("nbz")]

        def turn_along(k):
            vec(spreads, [R("nt", 32 * k, 32 * k + 32)], lambda: g.vector.transpose(T.nt[:, 32 * k:32 * k + 32], T.nb[:, 0:32]))

        def exchange_along(k):
            vec([R("nt")], [R("nbd")], lambda: g.vector.transpose(T.nb[:, 32:64], T.nt[:, 16:48]))

        def lists_along(k):
            vec(spreads + [R("nbd"), R("off", 2, 3)], [R(LO)],
                lambda: g.vector.tensor_scalar(T[LO][:], T.nb[:, 0:64].indirect(T.off[:, 2:3]), 256.0, float(H), ALU.mult, ALU.add))

        def state(q, b):
            lo, hi = ((0, C), (0, H), (H, C))[b // 10]
            b %= 10
            scaled(q, [R("bank%d" % b)], [R("xt%d" % b, lo, hi)], T.xt[:, 4 * lo + b:4 * hi:4], T.ps[:, 512 * b + lo:512 * b + hi], 2.0 ** -5)

        def plane(q, nm, n, b, j):
            scaled(q, [R("bank%d" % j)], [R(nm + str(b))], T[nm][:, n * b:n * b + n], bank(j, n), 2.0 ** -6)

        def gather(q, b):
            scaled(q, [R(DY + str(b)), R(LI)], [R("vt%d" % b)], T.vt[:, b:512:4], T[DY][:, C * b:C * b + C].indirect(T[LI][:, 0:8]), 2.0)

        def hand_on(k):
            nm, mine, sem = (("land", X1 if FAR else qv, "arr"), ("lsc", SX1 if FAR else sv, "ars"), ("lin", LO, "arl"))[k]
            dst = T.cores[(rank + STEP[r]) % 8]
            src = T.cores[(rank - STEP[r]) % 8]
            rid, pid = topo.addr(dst, core)
            need("g", deps("g", [R(mine)], []))
            nm, arr = nm + str(r + 1), sem + str(r + 1)
            o, i = T[nm][:], T[mine][:, 0:8] if k == 2 else T[mine][:]
            g.remote_dma(o if k else o.bitcast(dt.uint8), i if k else i.bitcast(dt.uint8), T.sem[arr], T.sem["loc"], pid, rid, topo.mask(core, dst))
            count["loc"] += len(topo.engines(core, dst))
            count[arr] = len(topo.engines(src, core))
            note("g", (arr, count[arr], {arr: count[arr]}), [], [R(nm)])

        def stationary(k):
            quant(qv, sv, 0, 128, "vt", 0, [R("vt%d" % b) for b in range(4)])
            if not FAR:
                hand_on(0)
                hand_on(1)

        steps = {
            "k": lambda k: first[k](),
            "B": lambda j: mm(SB[j], C, U, SU, 0, X, SX, 0, True, True),
            "U": lambda b: mm(b, C, "cf", "scf", 128 * b, X, SX, 0, True, False),
            "W": lambda b: mm(b, C, "wq", "wsc", 128 * b, qz, sz, 0, False, True),
            "G": lambda b: mm(4 + b % 2, 128, "cf", "scf", 128 * b, U, SU, 0, True, True),
            "H": lambda b: plane("a", "du", 128, b, 4 + b % 2), "q": lambda b: plane("v", "du", 128, b, 4 + b % 2),
            "P": lambda b: mm(b, C, "cf", "scf", 128 * b, X, SX, 0, True, True),
            "C": lambda b: plane("a", "dx", C, b, b), "v": lambda b: plane("v", "dx", C, b, b),
            "A": lambda b: mm(AB[b], C, "cf", "scf", 128 * b, LX, LS, 0, True, True),
            "J": lambda b: plane("a", DY, C, b, AB[b]), "w": lambda b: plane("v", DY, C, b, AB[b]),
            "c": turn_scores, "a": highest, "b": records, "g": rows, "t": ends, "X": exchange_down, "L": lists_down, "p": zed,
            "T": lambda b: mm(b, C, "ch", "sch", 128 * (b - 2), X, SX, 0, True, True), "K": picked, "M": added,
            "s": scan, "n": sign, "j": keys, "u": least, "m": marks, "f": levels, "h": fractions,
            "e": early, "i": lambda k: spread("v", k), "I": lambda k: spread("a", k), "N": turn_along, "x": exchange_along, "l": lists_along,
            "R": lambda b: state("a", b), "r": lambda b: state("v", b),
            "F": lambda b: gather("a", b), "y": lambda b: gather("v", b),
            "Q": lambda k: quant(qz, sz, 0, C, "zt", 0, [R("zt%d" % b) for b in range(4)]),
            "Y": lambda k: quant(X1, SX1, 0, C, "xt", 0, [R("xt%d" % b) for b in range(4)]),
            "S": hand_on, "V": stationary,
        }
        for word in [w for w in (SEQ if r else SEQ0).split() if r < 3 or w[0] in "AJwFyV"]:
            steps[word[0]](int(word[1:] or "0"))
        if r == 0:
            quant("qvv", "sqvv", 0, 128, "vin", 0, [R("vin")])
        if r == 2:
            outputs()
    UL, SL = ("qv2", "sv2") if FAR else ("land3", "lsc3")
    jobs = [("a", [R(UL)], [], T.uc[:], T[UL][:].bitcast(dt.uint8))]
    jobs += [("sa"[k // 3], [R(SL)], [], T.usc[4 * k:4 * k + 4, :], T[SL][32 * k:32 * k + 4, :]) for k in range(4)]
    dmas("st", jobs)
    g.wait_ge(T.sem["loc"], count["loc"])
    for s in ("vs", "ts", "sa", "gc0", "ldx", "ldu", "ldv", "ldw", "ldp", "st"):
        g.sync.wait_ge(T.sem[s], count[s])
